import numpy as np, ml_dtypes
CORES = [66,74,82,90,194,202,210,218]
N = 8
import mx_ref
BF = ml_dtypes.bfloat16
def gentries(a):
    return np.ascontiguousarray(a.reshape(8, 16, -1).transpose(0, 2, 1)).reshape(8, -1)
def gtable(e):
    e = np.asarray(e); return np.ascontiguousarray(e.reshape(8, -1, 16).transpose(0, 2, 1)).reshape(128, -1).astype(np.int32)
def gcols(t, e):
    v = np.concatenate([t.reshape(8, 16, -1, 4), np.zeros((8, 16, 1, 4), BF)], axis=2)
    return np.ascontiguousarray(np.stack([v[g][:, e[g]] for g in range(8)])).reshape(128, -1)
def tile(rs):
    return np.stack(rs, axis=2).reshape(128, -1).astype(BF)
def pick(q, e):
    c = np.concatenate([q[0].reshape(128, -1, 4), np.zeros((128, 1, 4), np.uint8)], axis=1); s = np.concatenate([q[1], np.ones((16, 1), np.uint8)], axis=1)
    return (np.ascontiguousarray(c[:, e].reshape(128, -1)), np.ascontiguousarray(s[:, e]))
def join(*qs):
    return (np.concatenate([q[0] for q in qs], axis=1), np.concatenate([q[1] for q in qs], axis=1))
def put(q, e, v):
    c, s = q[0].reshape(128, -1, 4).copy(), q[1].copy(); c[:, e] = v[0].reshape(128, -1, 4); s[:, e] = v[1]
    return (c.reshape(128, -1), s)
def pk(c, s):
    return (np.ascontiguousarray(c), mx_ref.live(s))
def emit(q):
    return q[0], q[1]
def packed(v, rng):
    q = [mx_ref.quantize(np.ascontiguousarray(v[r])) for r in range(N)]
    return np.stack([a for a, b in q]), np.stack([mx_ref.plane(b, rng) for a, b in q])
def values_of_codes():
    e, c = np.zeros((128, 128, 4), np.float32), np.zeros((128, 2, 4), np.uint8)
    e[np.arange(128), np.arange(128), 0] = 1
    c[:127, :, 0] = np.arange(256).reshape(2, 128).T[:127]
    return mx_ref.matmul(mx_ref.quantize(e.reshape(128, 512).astype(BF)), (c.reshape(128, 8), np.full((16, 2), 127, np.uint8))).T.reshape(-1).astype(np.float64)
CODE_VALUE, SCALE_VALUE = values_of_codes(), 2.0 ** (np.arange(256) - 127.0)
def decode(q):
    return (CODE_VALUE[q[0]].reshape(16, 8, -1, 4) * SCALE_VALUE[q[1]][:, None, :, None] + 0.0).reshape(128, -1).astype(np.float32)
def f(rng, *shape):
    return mx_ref.flush((rng.standard_normal(shape, dtype=np.float32) * np.exp2(rng.integers(-2, 3, shape[:-1] + (1,)))).astype(BF))
def wide(rng, *shape, cols=0):
    v = rng.standard_normal(shape, dtype=np.float32) * np.exp2(rng.integers(-12, 13, shape)).astype(np.float32)
    if cols: v *= np.repeat(np.exp2(rng.integers(-cols, cols + 1, shape[:-2] + (1, shape[-1] // 4))) * (rng.random(shape[:-2] + (1, shape[-1] // 4)) > 0.0625), 4, axis=-1).astype(np.float32)
    return mx_ref.flush(v.astype(BF))
L, R = 128, 3
STEP = [1, 2, 4]
def contract(a, b, turn):
    turn = turn & (b >= 0)
    a, b = np.where(turn, b, a), np.where(turn, a, b)
    go, o = [int(a[L - 1])], []
    while go:
        n = go.pop()
        if n < L: o.append(n)
        else: go += [int(b[n - L]), int(a[n - L])]
    leaf = np.array(o)[1::2]
    up = np.zeros(2 * L, np.int64)
    up[b] = L + np.arange(L)
    up[a] = L + np.arange(L)
    parent = up[leaf]
    left = a[parent - L] == leaf
    add = np.full((2, 2 * L), -1)
    for i, now in enumerate((left, ~left)):
        l, p = leaf[now], parent[now]
        s = a[p - L] + b[p - L] - l
        add[i, s] = np.flatnonzero(now)
        top = up[p]
        w = a[top - L] == p
        a[top[w] - L] = s[w]
        b[top[~w] - L] = s[~w]
        up[s] = top
        a[p - L] = -1
        b[p - L] = -1
    return a, b, leaf, parent, add
def numbers_of(rng):
    return {"x": np.array(f(rng, N, 128, 8 * L)), "u": np.array(f(rng, N, 128, 512)), "v": np.array(f(rng, N, 128, 512))}
def weights(rng, w):
    c, p = packed(w, rng)
    return {"wc": c, "ws": p}
def trees(rng, kind, q=None):
    e = np.full((2, N, 8, L), -1)
    for r in range(N):
        for g in range(8):
            pool, k = rng.permutation(L).tolist(), int(kind[r, g])
            w, c = rng.random(L), rng.integers(0, 2, L)
            for i, n in enumerate(rng.permutation(L - 1).tolist()):
                j = int(w[i] * (len(pool) - 1)) if k == 0 or k == 5 and i >= L // 2 else i // 2 * 2 + 1 if k == 5 else 0
                two = pool[j:j + 2]
                if k == 4 or k == 1 and c[i] or k == 5 and q[r, g, L + n] > 0: two = two[::-1]
                pool[j:j + 2] = []
                pool.insert(len(pool) if k == 2 else j, L + n)
                e[:, r, g, n] = two
            e[0, r, g, L - 1] = pool[0]
    return {"ka": np.stack([gtable(a) for a in e[0]]), "kb": np.stack([gtable(a) for a in e[1]])}
def planted(rng, kind, q, size, unit):
    d = numbers_of(rng)
    x = d["x"].astype(np.float32).reshape(N, 8, 16, 2 * L, 4)
    x[:, :, :8] = 0
    x[:, :, 0, :, 0] = (10 - q) * 0.125 * size
    x[:, :, 1, :, 0] = (9 - q) * 0.125 * size
    u = d["u"].reshape(N, 128, 128, 4)
    u[:, :, ::16] = 0
    for h in range(0, 128, 16):
        u[:, h, h, 0] = (1.125 * unit).astype(np.float32).astype(BF)
        u[:, h + 1, h, 0] = (-1.25 * unit).astype(np.float32).astype(BF)
    w = np.array(f(rng, N, 128, 2048)).reshape(N, 128, 4, 8, 16, 4)
    w[:, :, :, :, :8] = 0
    return {"x": x.reshape(N, 128, 8 * L).astype(BF), "u": u.reshape(N, 128, 512), "v": d["v"], **trees(rng, kind, q), **weights(rng, w.reshape(N, 128, 2048))}
def setup_inputs(rng):
    return {**numbers_of(rng), **trees(rng, rng.integers(0, 3, (N, 8))), **weights(rng, f(rng, N, 128, 2048))}
def setup_inputs_near(rng):
    q = rng.integers(-1, 2, (N, 8, 2 * L))
    size = np.exp2(-1.0 * rng.integers(0, 21, (N, 8, 2 * L)))
    small = rng.permutation(N) % 2 == 0
    size[small] = 2.0 ** -30
    kind = rng.integers(0, 3, (N, 8))
    g = np.stack([rng.permutation(8) for r in range(N)])
    kind[np.arange(N), g[:, 0]] = 5
    d = planted(rng, kind, q, size, np.where(small, 2.0 ** -30, 1.0))
    x = d["x"].reshape(N, 8, 16, 2 * L, 4)
    for r in range(N):
        e = int(g[r, 1])
        x[r, e, :8] = 0
        x[r, e, 0, :, 0] = np.exp2(-12.0 - np.arange(2 * L) % 8).astype(np.float32).astype(BF)
        x[r, e, 2, :, 0] = 1.9921875
    return {**d, "x": x.reshape(N, 128, 8 * L)}
def setup_inputs_deep(rng):
    k = np.stack([rng.permutation(8) for r in range(N)])
    m = (k // 2)[:, :, None]
    q = np.where(m < 3, m - 1, rng.integers(0, 2, (N, 8, 2 * L)) * 2 - 1)
    return planted(rng, 3 + k % 2, q, np.ones((N, 8, 2 * L)), np.ones(N))
def setup_inputs_huge(rng):
    d = numbers_of(rng)
    o = rng.permutation(N)
    c = np.stack([rng.permutation(2 * L) % 2 * 2.0 - 1.0 for r in range(N)])
    c[o == 0] = 1
    c[o == 1] = -1
    x = 2.0 ** 28 * (1 + rng.random((N, 128, 2 * L, 4))) * c[:, None, :, None]
    g = np.stack([rng.permutation(8) % 2 * 2.0 - 1.0 for r in range(N)])
    u = d["u"].reshape(N, 128, 128, 4)
    u[:, :, ::16] = (2.0 ** 30 * (0.75 + 0.25 * rng.random((N, 128, 8, 4))) * g[:, None, :, None]).astype(np.float32).astype(BF)
    w = np.zeros((N, 128, 4, 128, 4), np.float32)
    i = np.arange(128)
    for b in range(4): w[:, i, b, i, b] = 2
    return {"x": x.astype(np.float32).reshape(N, 128, 8 * L).astype(BF), "u": u.reshape(N, 128, 512), "v": d["v"], **trees(rng, rng.integers(0, 3, (N, 8))), **weights(rng, w.reshape(N, 128, 2048).astype(BF))}
def setup_inputs_spread(rng):
    d = setup_inputs(rng)
    d["x"] = wide(rng, N, 128, 8 * L, cols=6)
    return d
def check_inputs(d):
    bad = []
    for k in ("x", "u", "v"):
        a = np.abs(d[k].astype(np.float32))
        if not (np.isfinite(a).all() and ((a == 0) | (a >= 2.0 ** -30) & (a <= 2.0 ** 30)).all()): bad.append("a value of " + k)
    top = 2 * L - 1
    for r in range(N):
        a, b = gentries(d["ka"][r]).astype(np.int64), gentries(d["kb"][r]).astype(np.int64)
        if (b[:, L - 1] != -1).any(): bad.append("kb: the last entry of a group isn't -1")
        k = np.concatenate([a, b[:, :L - 1]], axis=1)
        if (np.sort(k, axis=1) != np.arange(top)).any():
            bad.append("ka, kb: a node isn't a child exactly once")
            continue
        up = np.full((8, 2 * L), top)
        np.put_along_axis(up, k, np.tile(np.concatenate([L + np.arange(L), L + np.arange(L - 1)]), (8, 1)), axis=1)
        for i in range(10): up = np.take_along_axis(up, up, axis=1)
        if (up != top).any(): bad.append("ka, kb: a node isn't under the head")
    return bad
def reference(x, u, v, ka, kb, wc, ws):
    qu = [mx_ref.quantize(u[r]) for r in range(N)]
    lay = [pk(wc[r], ws[r]) for r in range(N)]
    state = [x[r] for r in range(N)]
    own = [[(gentries(ka[r])[g], gentries(kb[r])[g]) for g in range(8)] for r in range(N)]
    for t in range(R):
        sent, add = [], []
        for r in range(N):
            q = mx_ref.quantize(state[r])
            state[r] = decode(q).astype(BF)
            p = mx_ref.matmul(qu[r], q)[::16, L:]
            done = [contract(own[r][g][0], own[r][g][1], p[g] > 0) for g in range(8)]
            own[r] = [e[:2] for e in done]
            one = gcols(state[r], np.stack([e[2] for e in done])).astype(np.float32)
            two = gcols(state[r], np.stack([e[3] for e in done])).astype(np.float32)
            sent.append(mx_ref.quantize(((one + two) * np.float32(0.5)).astype(BF)))
            add.append(np.stack([e[4] for e in done]))
        for r in range(N):
            q = sent[r ^ STEP[t]]
            h = tile([np.maximum(mx_ref.matmul(pick(lay[r], np.arange(128 * b, 128 * b + 128)), q), np.float32(0.0)) * np.float32(0.03125) for b in range(4)])
            for i in range(2):
                state[r] = (state[r].astype(np.float32) + gcols(h, add[r][:, i]).astype(np.float32)).astype(BF)
    y, kid = np.zeros((N, 128, 2 * L), np.float32), np.zeros((N, 8, 2 * L), np.float32)
    oc, osc = np.zeros((N, 128, 8 * L), np.uint8), np.zeros((N, 16, 2 * L), np.uint8)
    for r in range(N):
        q = mx_ref.quantize(state[r])
        y[r] = mx_ref.matmul(mx_ref.quantize(v[r]), q)
        for g in range(8): kid[r, g] = np.concatenate(own[r][g])
        oc[r], osc[r] = emit(q)
    return {"y": y, "kid": kid, "oc": oc, "osc": osc}

@@ -1,0 +1,674 @@
+from concourse.mybir import dt, AluOpType, ActivationFunctionType
+
+C4 = "float8_e4m3fn_x4"
+SCRATCH = {
+    "lf": ("sbuf", [128, 16384], "float32"), "lb": ("sbuf", [128, 22528], "bfloat16"),
+    "li": ("sbuf", [128, 128], "int32"), "lu": ("sbuf", [128, 1280], "uint16"),
+    "kin": ("sbuf", [128, 16], "int32"),
+    "xin": ("sbuf", [128, 1024], "bfloat16"), "uin": ("sbuf", [128, 512], "bfloat16"), "vin": ("sbuf", [128, 512], "bfloat16"),
+    "xs": ("sbuf", [128, 1280], "bfloat16"), "th": ("sbuf", [128, 256], "bfloat16"),
+    "g1": ("sbuf", [128, 256], "bfloat16"), "ft": ("sbuf", [128, 512], "bfloat16"),
+    "hb": ("sbuf", [128, 528], "bfloat16"), "tsb": ("sbuf", [128, 256], "bfloat16"),
+    "ab": ("sbuf", [128, 256], "bfloat16"), "ub": ("sbuf", [128, 256], "bfloat16"),
+    "one": ("sbuf", [128, 528], "bfloat16"), "eb": ("sbuf", [128, 528], "bfloat16"), "zt": ("sbuf", [128, 512], "bfloat16"),
+    "yb": ("sbuf", [128, 256], "float32"),
+    "qe": ("sbuf", [128, 512], C4), "se": ("sbuf", [128, 512], "uint8"),
+    "qu": ("sbuf", [128, 128], C4), "su": ("sbuf", [128, 128], "uint8"),
+    "qp": ("sbuf", [128, 128], C4), "sp": ("sbuf", [128, 128], "uint8"),
+    "qv": ("sbuf", [128, 128], C4), "sv": ("sbuf", [128, 128], "uint8"),
+    "qw": ("sbuf", [128, 512], C4), "sw": ("sbuf", [128, 512], "uint8"),
+    "qx": ("sbuf", [128, 256], C4), "sx": ("sbuf", [128, 256], "uint8"),
+    "qf": ("sbuf", [128, 384], C4), "sf": ("sbuf", [128, 384], "uint8"),
+    "qz": ("sbuf", [128, 128], C4), "sz": ("sbuf", [128, 128], "uint8"),
+    "ql": ("sbuf", [128, 624], C4), "sl": ("sbuf", [128, 624], "uint8"),
+    "ps": ("psum", [128, 4096], "float32"),
+}
+SEMAPHORES = ["sV", "sS", "sP", "sG", "sent", "arr0", "arr1", "arr2", "dka", "dkb", "dxh", "dxl", "du", "dv", "dwc", "dws",
+              "dkid", "doc", "dos0", "dos1", "dos2", "dos3", "dy0", "dy1",
+              "dz0", "dz1", "dz2", "dz3", "dzs0", "dzs1", "dzs2", "dzs3"]
+A = AluOpType
+AF = ActivationFunctionType
+LAND = [128, 320, 480]
+CY, GA, SC, LAT, FAR = 1.0, 1.56, 3.8, 60.0, 2400.0
+TWO = ("lb", "lu", "xin", "uin", "vin", "xs", "th", "g1", "ft", "hb", "tsb", "ab", "ub", "one", "eb", "zt")
+PLAN = {}
+TRIES = 3500
+
+
+def place(ops, prio, links, pen, back):
+    busy = {e: [] for e in "VSPGY"}
+    got = [None] * len(ops)
+    last = 0.0
+    todo = sorted(range(len(ops)), key=lambda j: prio[j])
+    while todo:
+        k = len(todo) - 1
+        while any(got[d] is None for d, w in links[todo[k]]):
+            k -= 1
+        i = todo.pop(k)
+        o = ops[i]
+        ready = o["tail"] if back else 0.0
+        for d, w in links[i]:
+            if got[d][2] + w > ready:
+                ready = got[d][2] + w
+        best = None
+        for k, (e, c, f) in enumerate(o["alts"]):
+            s, b = ready, busy[e]
+            j = len(b)
+            while j > 0 and b[j - 1][1] > s:
+                j -= 1
+            while j < len(b) and s + c > b[j][0]:
+                s = max(s, b[j][1])
+                j += 1
+            key = s + c + (pen[i] if e == "V" else 0.0)
+            if best is None or key < best[0]:
+                best = (key, e, k, s, c, j)
+        key, e, k, s, c, j = best
+        busy[e].insert(j, (s, s + c))
+        got[i] = (k, s, s + c)
+        last = max(last, s + c + (0.0 if back else o["tail"]))
+    return last, got
+
+
+def plan(ops):
+    n = len(ops)
+    if n in PLAN:
+        return PLAN[n]
+    pre = [[(d, ops[d]["tail"] + LAT if hard else 0.5) for d, hard in o["deps"].items()] for o in ops]
+    post = [[] for o in ops]
+    level = [0.0] * n
+    for i in range(n - 1, -1, -1):
+        level[i] += min(x[1] for x in ops[i]["alts"]) + ops[i]["tail"] + LAT
+        for d, w in pre[i]:
+            post[d].append((i, w))
+            level[d] = max(level[d], level[i])
+    seed = [12345]
+
+    def rnd():
+        seed[0] = (seed[0] * 1103515245 + 12345) % 2147483648
+        return (seed[0] >> 8) / 8388608.0
+
+    def both(prio, pen):
+        end, got = place(ops, prio, pre, pen, False)
+        e2, g2 = place(ops, [got[i][2] + ops[i]["tail"] for i in range(n)], post, pen, True)
+        p2 = [b[2] for b in g2]
+        e2, g2 = place(ops, p2, pre, pen, False)
+        return (end, got, prio, pen) if end <= e2 else (e2, g2, p2, pen)
+
+    cur = both(level, [150.0] * n)
+    for k in range(6):
+        cur = min(cur, both(cur[2] if k else [-b[1] for b in cur[1]], cur[3]), key=lambda x: x[0])
+    best = cur
+    for k in range(TRIES):
+        mid, wide, amp = rnd() * cur[0], 500 + 4000 * rnd(), 1500 * rnd() ** 2
+        prio, pen = [-b[1] for b in cur[1]], list(cur[3])
+        for i in range(n):
+            if abs(cur[1][i][1] - mid) < wide:
+                prio[i] += amp * rnd()
+                if rnd() < 0.15:
+                    pen[i] = 1200 * rnd() ** 2 - 200
+        new = both(prio, pen)
+        if new[0] < cur[0] + 60 * (1 - k / TRIES):
+            cur = new
+            if new[0] < best[0]:
+                best = new
+    PLAN[n] = best[1]
+    return best[1]
+
+
+def rank_program(g, core, T, topo):
+    rank = T.rank_of(core)
+    if rank is None:
+        return
+    Q = {"V": g.vector, "S": g.scalar, "P": g.tensor, "G": g, "Y": g.sync}
+    ops = []
+    log = {}
+    top = {"lf": 0, "lb": 0, "li": 0, "lu": 0}
+
+    def new(pool, n):
+        a = top[pool]
+        top[pool] = a + (n + 15) // 16 * 16
+        return (pool, a, a + n, 1)
+
+    def F(n): return new("lf", n)
+    def B(n): return new("lb", n)
+    def I(n): return new("li", n)
+    def U(n): return new("lu", n)
+    def W(name, a, b, s=1): return (name, a, b, s)
+    def sub(v, a, b, s=1): return (v[0], v[1] + a, v[1] + b, s)
+    def ap(v): return T[v[0]][:, v[1]:v[2]:v[3]] if v[3] != 1 else T[v[0]][:, v[1]:v[2]]
+    def num(s): return ap(s) if isinstance(s, tuple) else s
+    def views(*xs): return [x for x in xs if isinstance(x, tuple)]
+    def col(v, j): return sub(v, j, j + 1)
+    def n_of(v): return (v[2] - v[1] + v[3] - 1) // v[3]
+    def src(v, ind): return ap(v).indirect(ap(ind)) if ind else ap(v)
+
+    def do(alts, wr, rd, sem=None, inc=1, tail=0.0, chain=False, after=()):
+        deps = {d: True for d in after}
+        spans = []
+        for v, w in [(v, True) for v in wr] + [(v, False) for v in rd]:
+            lo, hi = v[1], v[2]
+            ps = v[0] == "ps"
+            if ps:
+                lo, hi = lo // 512 * 512, (hi + 511) // 512 * 512
+            spans.append((v[0], lo, hi, w or ps))
+            for (l2, h2, w2, d) in log.get(v[0], []):
+                if l2 < hi and lo < h2 and (w or w2):
+                    deps[d] = deps.get(d, False) or not (chain and ps)
+        me = len(ops)
+        ops.append({"alts": alts, "deps": deps, "sem": sem, "inc": inc, "tail": tail})
+        for (name, lo, hi, w) in spans:
+            old = log.get(name, [])
+            if w:
+                old = [x for x in old if not (lo <= x[0] and x[1] <= hi)]
+            log[name] = old + [(lo, hi, w, me)]
+        return me
+
+    def vt(o, i, ind, k=1.0):
+        if ind:
+            return 50 + 16 * n_of(ind) * GA * CY
+        if k == 1.0 and o[0] in TWO and i[0] in TWO:
+            k = 0.5
+        return max(64, n_of(o) * k) * CY
+
+    def st(o, ind): return 65 + 16 * n_of(ind) * GA * CY if ind else 60 + max(64, n_of(o)) * CY
+
+    def ts_call(o, i, s1, op0, s2, op1, ind):
+        if op1 is None:
+            return lambda: g.vector.tensor_scalar(ap(o), src(i, ind), num(s1), None, op0)
+        return lambda: g.vector.tensor_scalar(ap(o), src(i, ind), num(s1), num(s2), op0, op1)
+
+    def ts(o, i, s1, op0, s2=None, op1=None, ind=None):
+        do([("V", vt(o, i, ind), ts_call(o, i, s1, op0, s2, op1, ind))], [o], views(i, s1, s2, ind))
+        return o
+
+    def lin(o, i, m=1.0, a=0.0, ind=None, only=None):
+        if m == 1.0 and a == 0.0:
+            v = lambda: g.vector.tensor_copy(ap(o), src(i, ind))
+            s = lambda: g.scalar.activation(ap(o), src(i, ind), AF.Copy)
+        else:
+            v = ts_call(o, i, m, A.mult, a, A.add, ind)
+            s = lambda: g.scalar.activation(ap(o), src(i, ind), AF.Identity, bias=num(a), scale=num(m))
+        alts = [("V", vt(o, i, ind), v)]
+        if o[0] not in ("li", "lu") and i[0] not in ("li", "lu", "kin"):
+            alts.append(("S", st(o, ind), s))
+        do([x for x in alts if only in (None, x[0])], [o], views(i, m, a, ind))
+        return o
+
+    def tt(o, a, b, op, ind=None):
+        do([("V", vt(o, a, ind, 2.0), lambda: g.vector.tensor_tensor(ap(o), src(a, ind), ap(b), op))], [o], views(a, b, ind))
+        return o
+
+    def put(win, off, i):
+        do([("V", 50 + n_of(i) * SC * CY, lambda: g.vector.tensor_copy(ap(win).indirect(ap(off)), ap(i)))], [win], [off, i])
+
+    def iota(o, pat, base, cm=0):
+        if o[0] == "li":
+            f = lambda: g.iota(ap(o), pat, base, cm)
+        else:
+            f = lambda: g.iota(ap(o), pat, base, cm, allow_small_or_imprecise_dtypes=True)
+        do([("G", 130 + 2 * CY * n_of(o), f)], [o], [])
+        return o
+
+    def fill(o, c, only=None):
+        alts = [("V", vt(o, o, None), lambda: g.vector.memset(ap(o), float(c))),
+                ("G", 130 + 2 * CY * n_of(o), lambda: g.iota(ap(o), [[0, n_of(o)]], c, 0, allow_small_or_imprecise_dtypes=True))]
+        do([x for x in alts if only in (None, x[0])], [o], [])
+        return o
+
+    def scan(o, d0, d1, op0, op1):
+        do([("V", vt(o, d1, None), lambda: g.vector.tensor_tensor_scan(ap(o), ap(d0), ap(d1), 0.0, op0, op1))], [o], [d0, d1])
+        return o
+
+    def act(o, i, func, ind=None, bias=0.0, scale=1.0):
+        if func == AF.Copy:
+            f = lambda: g.scalar.activation(ap(o), src(i, ind), func)
+        else:
+            f = lambda: g.scalar.activation(ap(o), src(i, ind), func, bias=num(bias), scale=num(scale))
+        do([("S", st(o, ind), f)], [o], views(i, ind, bias, scale))
+        return o
+
+    def relu(o, i):
+        do([("V", vt(o, i, None), ts_call(o, i, 0.0, A.max, 0.03125, A.mult, None)),
+            ("S", st(o, None), lambda: g.scalar.activation(ap(o), ap(i), AF.Relu, scale=0.03125))], [o], [i])
+
+    def quant(n, a, b, i):
+        c, s = W("q" + n, a, b), W("s" + n, a, b)
+        do([("V", 12 + 0.22 * n_of(i), lambda: g.vector.quantize_mx(ap(c), ap(s), ap(i)))], [c, s], [i])
+
+    def mm(o, l, la, r, ra, start=True, stop=True):
+        n = n_of(o)
+        lc, ls, rc, rs = W("q" + l, la, la + 128), W("s" + l, la, la + 128), W("q" + r, ra, ra + n), W("s" + r, ra, ra + n)
+        do([("P", (n + 16) * 0.7, lambda: g.tensor.matmul_mx(ap(o), ap(lc), ap(ls), ap(rc), ap(rs), start, stop))],
+           [o], [lc, ls, rc, rs], chain=not start)
+
+    def dma(e, sem, out, in_, wr, rd, tail, after=()):
+        return do([(e, 100.0, lambda: Q[e].dma_start(out, in_))], wr, rd, sem=sem, inc=16, tail=tail, after=after)
+
+    kin = W("kin", 0, 16)
+    dma("Y", "dka", T.kin[:, 0:8], T.ka[:], [sub(kin, 0, 8)], [], 1600.0)
+    dma("S", "dkb", T.kin[:, 8:16], T.kb[:], [sub(kin, 8, 16)], [], 1600.0)
+    dma("S", "du", T.uin[:], T.u[:], [W("uin", 0, 512)], [], 2300.0)
+    dma("Y", "dxh", T.xin[:, 512:1024], T.x[:, 512:1024], [W("xin", 512, 1024)], [], 2500.0)
+    dx = dma("Y", "dxl", T.xin[:, 0:512], T.x[:, 0:512], [W("xin", 0, 512)], [], 2800.0)
+    dma("Y", "dwc", T.qw[:].bitcast(dt.uint8), T.wc[:], [W("qw", 0, 512)], [], 3000.0, (dx,))
+    dma("Y", "dws", T.sw[:], T.ws[:], [W("sw", 0, 512)], [], 3000.0, (dx,))
+    dma("Y", "dv", T.vin[:], T.v[:], [W("vin", 0, 512)], [], 3000.0, (dx,))
+
+    pi = iota(I(1), [[0, 1]], 0, 1)
+    one = fill(W("one", 0, 528), 1, "V")
+    io1b = scan(B(256), sub(one, 0, 256), sub(one, 0, 256), A.mult, A.add)
+    io = lin(F(128), sub(io1b, 0, 128), 1.0, -1.0)
+    io1 = lin(F(256), io1b)
+    pay = B(256)
+    lin(sub(pay, 0, 255), sub(io1b, 0, 255))
+    fill(col(pay, 255), 128)
+    lut = B(256)
+    fill(sub(lut, 0, 128), 256)
+    lin(sub(lut, 128, 256), sub(io1b, 0, 128))
+    eb = W("eb", 0, 528)
+    do([("G", 170 + 2 * CY * 528, lambda: g.affine_select(ap(eb), ap(one), [[-1, 528]], A.is_equal, 0.0, 3, 4))], [eb], [one])
+    crf = F(20)
+    for c in range(4):
+        iota(sub(crf, 5 * c, 4 * c + 4), [[16, 4 - c]], 16 * c)
+        iota(sub(crf, 4 * c + 4, 5 * c + 5), [[16, c + 1]], 64)
+    quant("z", 0, 128, fill(W("zt", 0, 512), 0))
+    for k, z in enumerate((0, 192, 352, 496)):
+        dma("Y", "dz%d" % k, T.ql[:, z:z + 128].bitcast(dt.uint8), T.qz[:].bitcast(dt.uint8),
+            [W("ql", z, z + 128)], [W("qz", 0, 128)], 2200.0, (dx,))
+        dma("Y", "dzs%d" % k, T.sl[:, z:z + 128], T.sz[:], [W("sl", z, z + 128)], [W("sz", 0, 128)], 2200.0, (dx,))
+    for b in range(4):
+        quant("e", 128 * b, 128 * b + 128, W("eb", 3 - b, 515 - b))
+    ri = I(3)
+    ts(col(ri, 0), pi, 15, A.bitwise_and)
+    ts(col(ri, 1), pi, 2, A.arith_shift_right, 3, A.bitwise_and)
+    ts(col(ri, 2), pi, 3, A.bitwise_and)
+    rf = lin(F(3), ri)
+    r, r4, r3 = col(rf, 0), col(rf, 1), col(rf, 2)
+    TB = B(384)
+    fill(sub(TB, 127, 256, 128), 1)
+    inv16 = ts(F(1), r, 15.0, A.is_equal, 1.0 / 1024, A.max)
+    inv4 = ts(F(1), r4, 3.0, A.is_equal, 1.0 / 1024, A.max)
+    inv44 = lin(F(1), inv4, 4.0)
+    invm = lin(F(1), inv16, -128.0)
+    r3m = lin(F(1), r3, 1.0, -4.0)
+    r1, r41, r256 = lin(F(1), r, 1.0, 1.0), lin(F(1), r4, 1.0, 1.0), lin(F(1), r, 1.0, 256.0)
+    d0, d1 = F(32), F(32)
+    ts(sub(d0, 0, 16), sub(io, 0, 16), r, A.not_equal)
+    ts(sub(d1, 0, 16), sub(io, 0, 16), r1, A.is_equal, 1024.0, A.mult)
+    ts(sub(d0, 16, 32), sub(io, 0, 16), r4, A.not_equal)
+    ts(sub(d1, 16, 32), sub(io, 0, 16), r41, A.is_equal, 1024.0, A.mult)
+    pt = F(32)
+    tt(sub(pt, 0, 16), sub(d0, 0, 16), sub(d1, 0, 16), A.max)
+    tt(sub(pt, 16, 32), sub(d0, 16, 32), sub(d1, 16, 32), A.max)
+    c16 = lin(U(8), sub(io, 0, 8), 0.0, r)
+    c4 = lin(U(8), sub(io, 0, 8), 0.0, r3)
+    P16b = B(320)
+    lin(sub(P16b, 0, 128), sub(pt, 0, 16), ind=c16)
+    lin(sub(P16b, 128, 256), sub(P16b, 0, 128))
+    lin(sub(P16b, 256, 320), sub(P16b, 0, 64))
+    P16 = lin(F(128), sub(P16b, 0, 128))
+    P4 = lin(F(128), sub(pt, 16, 32), ind=c4)
+    self2 = F(16)
+    lin(sub(self2, 0, 8), sub(io, 0, 8), 16.0, r256)
+    lin(sub(self2, 8, 16), sub(io, 0, 8), 16.0, r256)
+    cU = lin(U(8), sub(io, 0, 8), 16.0)
+    nio = iota(F(8), [[-1, 8]], 0)
+
+    def wrapscan(v, per=16, half=False):
+        n = n_of(v)
+        o = B(n) if half else F(n)
+        scan(o, sub(P16b if half else P16 if per == 16 else P4, 0, n), v, A.mult, A.max)
+        return sub(o, per - 1, n, per)
+
+    def wrap(v, o=None, add=-1.0, half=False):
+        s = wrapscan(v, 16, half)
+        return lin(o or U(n_of(s)), s, inv16, add)
+
+    k8 = ts(I(16), kin, 255, A.bitwise_and)
+    ksc = lin(U(16), k8)
+    X = F(24)
+    lin(sub(X, 0, 16), k8)
+    lin(sub(X, 16, 24), sub(X, 0, 8))
+    PS1 = B(256)
+    put(PS1, ksc, pay)
+    WPS, wps = U(16), F(16)
+    for h in (8, 0):
+        s = wrapscan(sub(PS1, 16 * h, 16 * h + 128), 16, True)
+        lin(sub(WPS, h, h + 8), s, inv16, -1.0)
+        lin(sub(wps, h, h + 8), s, inv16, 255.0)
+    BA = B(256)
+    lin(sub(BA, 0, 128), lut, ind=sub(ksc, 8, 16))
+    lin(sub(BA, 128, 256), lut, ind=sub(ksc, 0, 8))
+    sib = lin(B(128), BA, ind=sub(WPS, 8, 16))
+    quant("u", 0, 128, W("uin", 0, 512))
+    do([("V", 250.0, lambda: g.vector.tensor_copy(T.qp[:, 0:128].bitcast(dt.uint32),
+                                                  T.qu[:, 0:128].bitcast(dt.uint32).indirect(ap(cU))))],
+       [W("qp", 0, 128)], [W("qu", 0, 128), cU])
+    act(W("sp", 0, 128), W("su", 0, 128), AF.Copy, ind=cU)
+    PP = W("ps", 2048, 2176)
+
+    def scores(x):
+        quant("x", 128, 256, W(x, 512, 1024))
+        mm(PP, "p", 0, "x", 128)
+        quant("x", 0, 128, W(x, 0, 512))
+        for b in range(4):
+            mm(W("ps", 512 * b, 512 * b + 256), "e", 128 * b, "x", 0)
+        for b in range(4):
+            lin(W("xs", b, 1024, 4), W("ps", 512 * b, 512 * b + 256))
+
+    scores("xin")
+    base, delta = F(32), F(32)
+    slot = ts(F(16), wps, 384.0, A.is_ge, -128.0, A.mult)
+    par = F(8)
+    tt(sub(base, 8, 16), sub(wps, 8, 16), sub(slot, 8, 16), A.add)
+    tt(par, sub(wps, 0, 8), sub(slot, 0, 8), A.add)
+    fill(sub(base, 24, 32), 128)
+    sibw = wrap(sib, o=F(8), add=127.0, half=True)
+    u1 = tt(F(8), sibw, sub(base, 8, 16), A.min)
+    tt(sub(delta, 8, 16), u1, sub(base, 8, 16), A.subtract)
+    ts(sub(delta, 24, 32), sibw, 383.0, A.is_equal)
+    pen = ts(F(24), X, 128.0, A.is_lt, 512.0, A.mult)
+    X2 = tt(F(24), X, pen, A.add)
+    inner = tt(F(16), sub(X2, 8, 24), self2, A.min)
+    bump = lin(F(16), sub(pen, 0, 16), -2.0, 1024.0)
+    in2 = tt(F(16), inner, bump, A.add)
+    s01 = tt(F(16), sub(X2, 0, 16), in2, A.min)
+    nY = lin(F(16), sub(pen, 8, 24), 2.0 ** -18, 2.0 ** -9)
+    w01 = tt(F(16), sub(pen, 0, 16), nY, A.mult)
+    lin(sub(base, 0, 8), sub(s01, 0, 8))
+    tt(sub(delta, 0, 8), sub(s01, 8, 16), sub(s01, 0, 8), A.subtract)
+    lin(sub(base, 16, 24), sub(w01, 0, 8), 1.0, 128.0)
+    tt(sub(delta, 16, 24), sub(w01, 8, 16), sub(w01, 0, 8), A.subtract)
+    ts(sub(TB, 128, 255), sub(PP, 0, 127), 0.0, A.is_gt, 1.0, A.add)
+    lin(sub(TB, 0, 127), sub(TB, 128, 255), -1.0, 3.0)
+    lin(sub(TB, 256, 384), sub(TB, 0, 256), ind=sub(WPS, 8, 16))
+    ilb = lin(B(128), sub(TB, 0, 256), 1.0, 127.0, ind=sub(WPS, 0, 8))
+    s = wrapscan(sub(TB, 128, 384), 16, True)
+    sel = F(32)
+    lin(sub(sel, 0, 16), s, inv16, -1.0)
+    lin(sub(sel, 16, 32), s, inv16, -1.0)
+    m1 = tt(F(32), sel, delta, A.mult)
+    m2 = tt(F(32), m1, base, A.add)
+    WS = lin(U(32), m2, 1.0, -128.0)
+    Wc = sub(WS, 0, 16)
+    R = B(256)
+    for h in range(2):
+        lin(sub(R, 128 * h, 128 * h + 128), io1b, ind=sub(Wc, 8 * h, 8 * h + 8))
+    val = lin(B(256), nio, ind=sub(WS, 16, 32))
+    for i in range(8):
+        own = B(256)
+        for h in range(2):
+            lin(sub(own, 128 * h, 128 * h + 128), sub(val, 128 * h, 128 * h + 128), only="VS"[h])
+        val = tt(B(256), val, own, A.add, ind=Wc)
+        if i < 7:
+            R2, W2 = B(256), U(16)
+            for h in range(2):
+                lin(sub(R2, 128 * h, 128 * h + 128), R, ind=sub(Wc, 8 * h, 8 * h + 8), only="S")
+                wrap(sub(R2, 128 * h, 128 * h + 128), o=sub(W2, 8 * h, 8 * h + 8), half=True)
+            R, Wc = R2, W2
+    sil = wrapscan(ilb, 16, True)
+    wpar = lin(U(8), par, 1.0, -128.0)
+    UP = lin(F(128), io1, ind=wpar)
+    ev0 = lin(F(8), sil, invm, 16256.0)
+    ev1 = tt(F(8), ev0, par, A.add)
+    Wev = lin(U(8), ev1)
+    num1 = tt(B(128), val, ilb, A.add, ind=Wev)
+    Wn = wrap(num1, half=True)
+    fill(W("ft", 0, 512), 0)
+    LID = sub(io1, 0, 128)
+    WAB = X
+    tw = F(16)
+    lin(sub(tw, 0, 8), sub(sel, 0, 8))
+    lin(sub(tw, 8, 16), sub(sel, 0, 8))
+    S1 = fill(F(320), 1)
+    RZ, PRV, MK = F(392), fill(F(256), 0), B(768)
+    fill(sub(RZ, 0, 8), 0)
+    REP = sub(RZ, 8, 392)
+    for t in range(3):
+        fill(sub(MK, 256 * t, 256 * t + 256), 0)
+    T01 = fill(B(256), 1)
+    t01 = sub(T01, 128, 256)
+    BI = B(256)
+    lin(sub(BI, 0, 128), io1b, ind=sub(ksc, 8, 16))
+    lin(sub(BI, 128, 256), io1b, ind=sub(ksc, 0, 8))
+    SIB = lin(B(128), BI, ind=sub(WPS, 0, 8))
+    iota(sub(REP, 0, 256), [[1, 256]], 1)
+    fill(sub(REP, 256, 384), 256)
+    fill(W("xs", 1024, 1280), 0)
+    fill(W("hb", 0, 272), 0)
+    kc = iota(F(64), [[1, 64]], 257)
+    r416 = lin(F(1), r4, 1.0, 272.0)
+
+    for t in range(3):
+        K = 64 >> t
+        OL = F(128 if t == 0 else 64)
+        put(OL, Wn, LID)
+        lk = sub(OL, 1, 2 * K, 2)
+        if t == 1:
+            OP = F(64)
+            put(OP, Wn, PID)
+            pk = sub(OP, 1, 2 * K, 2)
+        else:
+            Wk = wrap(lk)
+            pk = lin(F(K), UP, ind=Wk)
+        Wl = lin(U(K // 4), wrapscan(lk, 4), inv44, r3m)
+        g1 = lin(W("g1", 0, 4 * K), W("xs", 0, 1024), ind=Wl)
+        Wp4 = lin(U(K // 4), wrapscan(pk, 4), inv44, r3m)
+        lin(W("ft", 0, 4 * K), tt(W("th", 0, 4 * K), W("xs", 0, 1024), g1, A.add, ind=Wp4), 0.5)
+        quant("f", 128 * t, 128 * t + 128, W("ft", 0, 512))
+        d = T.cores[rank ^ (1 << t)]
+        a = LAND[t]
+
+        def send(d=d, a=a, t=t, K=K):
+            rid, pid = topo.addr(d, core)
+            arr, mask = T.sem["arr%d" % t], topo.mask(core, d)
+            g.remote_dma(T.ql[:, a:a + K].bitcast(dt.uint8), T.qf[:, 128 * t:128 * t + K].bitcast(dt.uint8), arr, T.sem.sent,
+                         pid, rid, mask)
+            g.remote_dma(T.sl[:, a:a + K], T.sf[:, 128 * t:128 * t + K], arr, T.sem.sent, pid, rid, mask)
+            return 2 * len(topo.engines(core, d))
+
+        do([("G", 200.0, send)], [W("ql", a, a + K), W("sl", a, a + K)],
+           [W("qf", 128 * t, 128 * t + 128), W("sf", 128 * t, 128 * t + 128)],
+           sem="arr%d" % t, inc=2 * len(topo.engines(d, core)), tail=FAR)
+
+        if t > 0:
+            lin(sub(t1, 0, 127), sub(t01, 0, 127), 1.0, 1.0)
+            s = wrapscan(t1, 16, True)
+            tw = F(16)
+            lin(sub(tw, 0, 8), s, inv16, -1.0)
+            lin(sub(tw, 8, 16), s, inv16, -1.0)
+        dd = tt(F(16), sub(WAB, 8, 24), sub(WAB, 0, 16), A.subtract)
+        LRw = tt(F(16), tt(F(16), dd, tw, A.mult), sub(WAB, 0, 16), A.add)
+        WLR = lin(U(16), LRw)
+        Wp = wrap(pk)
+        hk = lin(F(1), r3, float(K), r416)
+        hk2 = lin(F(1), r3, float(K), 15.0)
+        HC = lin(U(K // 4), sub(io, 0, K // 4), 4.0, hk)
+        if t == 0:
+            left = lin(F(K), ilb, 1.0, -128.0, ind=Wk)
+            s1 = lin(sub(S1, 0, K), SIB, ind=Wk)
+        else:
+            gl = lin(F(K), sub(ABb, 0, 256), ind=Wp)
+            gs = tt(F(K), sub(ABb, 128, 384), gl, A.add, ind=Wp)
+            left = tt(F(K), T01, tt(F(K), gl, lk, A.is_equal), A.not_equal, ind=Wp)
+            s1 = tt(sub(S1, 0, K), gs, lk, A.subtract)
+        lin(sub(S1, 256, 256 + K), s1)
+        prv = tt(F(K), left, sub(kc, 0, K), A.mult)
+        Ws1 = wrap(s1)
+        right = lin(B(K), left, -1.0, 1.0)
+        mk = sub(MK, 256 * t, 256 * t + 256)
+        put(PRV, Wp, prv)
+        put(mk, Ws1, right)
+        SP = F(2 * K)
+        ix = tt(sub(SP, K, 2 * K), PRV, sub(io1, 0, K), A.max, ind=Ws1)
+        dup = tt(F(K), mk, prv, A.mult, ind=Wp)
+        so = tt(sub(SP, 0, K), S1, dup, A.max, ind=wrap(ix))
+        s = wrapscan(SP, 4)
+        XO = lin(U(K // 4), (s[0], s[1], s[1] + K - 3, 4), inv44, r3m)
+        HO = lin(U(K // 4), (s[0], s[1] + K, s[2], 4), inv4, hk2)
+        Ts = lin(W("tsb", 0, 4 * K), W("xs", 0, 1280), ind=XO)
+        put(REP, Wp, so)
+        a1 = lin(B(256), REP, ind=WLR)
+        if t < 2:
+            ABb = B(384)
+            fill(sub(ABb, 0, 128), 1)
+            AB1 = lin(sub(ABb, 128, 384), REP, ind=wrap(a1, half=True))
+        if t == 1:
+            put(sub(ABb, 0, 256), Wp, iota(F(32), [[2, 32]], 258))
+            put(sub(ABb, 128, 384), Wp, iota(F(32), [[2, 32]], 322))
+        n = 2 if t == 0 else 4
+        for b in range(4):
+            j = b % n
+            bank = 2560 + 512 * (b // n)
+            mm(W("ps", bank, bank + 128), "w", 128 * b, "l", a - K * j, j == 0, j == n - 1)
+        hb = W("hb", 0, 272 + 4 * K)
+        if t == 0:
+            relu(W("hb", 272, 400), W("ps", 2560, 2688))
+            relu(W("hb", 400, 528), W("ps", 3072, 3200))
+        else:
+            relu(W("hb", 272, 272 + 4 * K), W("ps", 2560, 2560 + 4 * K))
+        ab = tt(W("ab", 0, 4 * K), hb, Ts, A.add, ind=HO)
+        ub = tt(W("ub", 0, 4 * K), hb, ab, A.add, ind=HC)
+        put(W("xs", 0, 1280), XO, ub)
+        if t == 2:
+            break
+        WAB = F(24)
+        wrap(AB1, o=sub(WAB, 0, 16), half=True)
+        lin(sub(WAB, 16, 24), sub(WAB, 0, 8))
+        if t == 0:
+            ll = ts(F(8), sub(LRw, 0, 8), 128.0, A.is_lt)
+            i1 = lin(F(8), ll, -1024.0, 256.0)
+            i2 = tt(F(8), i1, sub(LRw, 0, 8), A.add)
+            i3 = tt(F(8), i2, sub(self2, 0, 8), A.max)
+            Wm = lin(U(8), i3, 1.0, -256.0)
+            mid1 = lin(B(128), val, 1.0, 129.0, ind=Wm)
+            Wmid = lin(U(8), tt(F(8), wrap(mid1, o=F(8), half=True), ll, A.add))
+            INV = F(144)
+            put(INV, Wmid, sub(io1, 0, 128))
+            f1 = tt(F(63), sub(INV, 1, 127, 2), sub(INV, 2, 128, 2), A.add)
+            WR = lin(U(20), crf, 1.0, r)
+            GID = F(128)
+            fill(col(GID, 0), 256)
+            tt(sub(GID, 1, 64), f1, lin(F(63), sub(pk, 0, 63), 1.0, -256.0), A.subtract)
+            lin(sub(GID, 64, 128), sub(GID, 0, 64))
+            WG = wrap(lin(B(320), GID, ind=WR), add=-129.0, half=True)
+            W1 = wrap(sub(GID, 0, 64), add=-129.0)
+            lh = B(128)
+            lin(sub(lh, 0, 64), sub(val, 0, 128), 0.5, 192.25, ind=W1)
+            lin(sub(lh, 64, 128), sub(val, 128, 256), 0.5, 192.25, ind=W1)
+            LH1 = lin(F(128), lh, 1.0, -127.0)
+            lo1, hi1 = sub(LH1, 0, 64), sub(LH1, 64, 128)
+            icol = lin(F(4), sub(io, 0, 4), 16.0, r)
+            nb, ia, ib = lin(F(4), icol, -1.0, -0.5), lin(F(4), icol, 1.0, 2.0), lin(F(4), icol, 1.0, -64.0)
+            KK = F(320)
+            for c in range(4):
+                sg = act(F(64), sub(io, 0, 64), AF.Sign, bias=col(nb, c))
+                act(sub(KK, 80 * c, 64 * c + 64), sub(sg, 16 * c, 64), AF.Relu, scale=col(ia, c))
+                act(sub(KK, 64 * c + 64, 80 * c + 80), sub(sg, 0, 16 * c + 16), AF.Relu, scale=col(ib, c))
+            bd = F(128)
+            lin(sub(bd, 0, 64), sub(lh, 0, 64), 1.0, -127.0)
+            lin(sub(bd, 64, 128), sub(lh, 64, 128), -1.0, 192.0)
+            Mk = tt(F(320), bd, KK, A.is_lt, ind=WR)
+            uv = F(128)
+            tt(sub(uv, 0, 64), hi1, sub(io1, 0, 64), A.subtract)
+            tt(sub(uv, 64, 128), lo1, sub(io1, 0, 64), A.subtract)
+        else:
+            CUM = F(80)
+            al = lin(F(64), EV, ind=Wn)
+            fill(sub(CUM, 0, 1), 0)
+            scan(sub(CUM, 1, 65), ones, al, A.mult, A.add)
+            cum = lin(F(64), sub(CUM, 0, 64))
+            tsl = lin(F(64), t01, -2.0, 1.0, ind=W1)
+            n1 = tt(F(64), sub(CUM, 0, 65), cum, A.subtract, ind=sub(WLH, 0, 4))
+            n2 = tt(F(64), sub(CUM, 0, 65), cum, A.subtract, ind=sub(WLH, 4, 8))
+            uv = F(128)
+            tt(sub(uv, 0, 64), n2, tsl, A.mult)
+            tt(sub(uv, 64, 128), n1, tsl, A.mult)
+        C = tt(F(320), uv, Mk, A.mult, ind=WR)
+        if t == 0:
+            lin(sub(C, 64, 320, 64), icol)
+            t1 = B(128)
+            fill(col(t1, 127), 1)
+            RS = fill(B(320), 1)
+            fill(sub(RS, 0, 320, 80), 0)
+            LID = lin(F(64), sub(OL, 0, 128, 2))
+            PID = F(64)
+            j1 = tt(F(63), sub(LH1, 1, 64), sub(io1, 0, 63), A.is_equal)
+            j2 = tt(F(63), sub(GID, 1, 64), sub(GID, 0, 63), A.subtract)
+            lin(col(PID, 63), col(GID, 63))
+            j3 = tt(F(63), j1, j2, A.mult)
+            tt(sub(PID, 0, 63), j3, sub(GID, 0, 63), A.add)
+            ones = fill(F(64), 1)
+            EV = iota(F(64), [[0, 32], [-1, 2]], 1)
+            UP = fill(F(384), 1)
+            WLH = wrap(lh, add=-128.0, half=True)
+        else:
+            hh = lin(B(4), posw, 0.5, 129.75)
+            alw = tt(F(4), lin(F(4), hh, 2.0, -259.0), posw, A.subtract)
+            bs = tt(F(4), lin(F(4), hh, -63.0, 8190.0), lin(F(4), posw, 32.0), A.add)
+            Cr, C = C, F(320)
+            for c in range(4):
+                lin(sub(C, 80 * c, 80 * c + 80), sub(Cr, 80 * c, 80 * c + 80), col(alw, c))
+            lin(sub(C, 64, 320, 64), bs)
+            k3 = F(128)
+            for h in range(2):
+                lin(sub(k3, 64 * h, 64 * h + 64), sub(AB1, 128 * h, 128 * h + 128), ind=W1)
+            put(UP, wrap(k3), GID)
+        scores("xs")
+        ts(sub(t01, 0, 127), sub(PP, 0, 127), 0.0, A.is_gt)
+        pr = tt(B(320), t01, C, A.mult, ind=WG)
+        posw = sub(scan(B(320), RS, pr, A.mult, A.add), 79, 320, 80)
+        Wn = lin(U(4), posw)
+
+    quant("v", 0, 128, W("vin", 0, 512))
+    quant("x", 0, 128, W("xs", 0, 512))
+    quant("x", 128, 256, W("xs", 512, 1024))
+    dma("Y", "doc", T.oc[:], T.qx[:].bitcast(dt.uint8), [], [W("qx", 0, 256)], 2300.0)
+    for k in range(4):
+        dma("Y", "dos%d" % k, T.osc[4 * k:4 * k + 4, :], T.sx[32 * k:32 * k + 4, :], [], [W("sx", 0, 256)], 1600.0)
+    for h in range(2):
+        mm(W("ps", 512 * h, 512 * h + 128), "v", 0, "x", 128 * h)
+    lin(W("yb", 0, 128), W("ps", 0, 128), only="V")
+    lin(W("yb", 128, 256), W("ps", 512, 640), only="S")
+    dma("Y", "dy0", T.y[:, 0:128], T.yb[:, 0:128], [], [W("yb", 0, 128)], 2000.0)
+    dma("S", "dy1", T.y[:, 128:256], T.yb[:, 128:256], [], [W("yb", 128, 256)], 2000.0)
+    s, rw = wrapscan(sub(REP, 128, 256)), F(16)
+    lin(sub(rw, 0, 8), s, inv16, 127.0)
+    lin(sub(rw, 8, 16), s, inv16, 127.0)
+    off = tt(F(16), wrap(a1, o=F(16), add=7.0, half=True), tt(F(16), rw, self2, A.is_equal), A.mult)
+    ko = lin(F(256), RZ, 1.0, -1.0, ind=lin(U(16), off))
+    fill(col(ko, 255), -1)
+    dma("Y", "dkid", T.kid[:], T.lf[0:128:16, ko[1]:ko[2]], [], [ko], 1600.0)
+
+    got = plan(ops)
+    total, known, clocks = {}, {e: {} for e in Q}, {}
+
+    def wait(e, sem, v):
+        if known[e].get(sem, 0) >= v:
+            return
+        Q[e].wait_ge(T.sem[sem], v)
+        for k, x in clocks.get((sem, v), {}).items():
+            if known[e].get(k, 0) < x:
+                known[e][k] = x
+        known[e][sem] = v
+
+    for i in sorted(range(len(ops)), key=lambda i: (got[i][1], i)):
+        o = ops[i]
+        e, c, f = o["alts"][got[i][0]]
+        need = {}
+        for d, hard in o["deps"].items():
+            if hard:
+                s, v = ops[d]["mark"]
+                need[s] = max(need.get(s, 0), v)
+        for s, v in sorted(need.items(), key=lambda x: -len(clocks.get(x, {}))):
+            wait(e, s, v)
+        sem = o["sem"] or "s" + e
+        total[sem] = total.get(sem, 0) + o["inc"]
+        o["mark"] = (sem, total[sem])
+        if sem.startswith("arr"):
+            total["sent"] = total.get("sent", 0) + f()
+        else:
+            f().then_inc(T.sem[sem], o["inc"])
+            clocks[o["mark"]] = dict(known[e])
+    for s, v in sorted(total.items()):
+        wait("Y", s, v)

@@ -1,38 +1,26 @@
 from concourse.mybir import dt, AluOpType, ActivationFunctionType
 
 C4 = "float8_e4m3fn_x4"
+TILES = {"lb": 22528, "xin": 1024, "uin": 512, "vin": 512, "xs": 1280, "th": 1024, "th2": 512, "sm": 512, "g1": 256, "ft": 512,
+         "hb": 528, "tsb": 256, "ab": 256, "ub": 256, "one": 528, "eb": 528, "zt": 512}
+PACKS = {"e": 512, "u": 128, "p": 128, "v": 128, "w": 512, "x": 256, "f": 384, "z": 128, "l": 624}
 SCRATCH = {
-    "lf": ("sbuf", [128, 16384], "float32"), "lb": ("sbuf", [128, 22528], "bfloat16"),
-    "li": ("sbuf", [128, 128], "int32"), "lu": ("sbuf", [128, 1280], "uint16"),
-    "kin": ("sbuf", [128, 16], "int32"),
-    "xin": ("sbuf", [128, 1024], "bfloat16"), "uin": ("sbuf", [128, 512], "bfloat16"), "vin": ("sbuf", [128, 512], "bfloat16"),
-    "xs": ("sbuf", [128, 1280], "bfloat16"), "th": ("sbuf", [128, 256], "bfloat16"),
-    "g1": ("sbuf", [128, 256], "bfloat16"), "ft": ("sbuf", [128, 512], "bfloat16"),
-    "hb": ("sbuf", [128, 528], "bfloat16"), "tsb": ("sbuf", [128, 256], "bfloat16"),
-    "ab": ("sbuf", [128, 256], "bfloat16"), "ub": ("sbuf", [128, 256], "bfloat16"),
-    "one": ("sbuf", [128, 528], "bfloat16"), "eb": ("sbuf", [128, 528], "bfloat16"), "zt": ("sbuf", [128, 512], "bfloat16"),
-    "yb": ("sbuf", [128, 256], "float32"),
-    "qe": ("sbuf", [128, 512], C4), "se": ("sbuf", [128, 512], "uint8"),
-    "qu": ("sbuf", [128, 128], C4), "su": ("sbuf", [128, 128], "uint8"),
-    "qp": ("sbuf", [128, 128], C4), "sp": ("sbuf", [128, 128], "uint8"),
-    "qv": ("sbuf", [128, 128], C4), "sv": ("sbuf", [128, 128], "uint8"),
-    "qw": ("sbuf", [128, 512], C4), "sw": ("sbuf", [128, 512], "uint8"),
-    "qx": ("sbuf", [128, 256], C4), "sx": ("sbuf", [128, 256], "uint8"),
-    "qf": ("sbuf", [128, 384], C4), "sf": ("sbuf", [128, 384], "uint8"),
-    "qz": ("sbuf", [128, 128], C4), "sz": ("sbuf", [128, 128], "uint8"),
-    "ql": ("sbuf", [128, 624], C4), "sl": ("sbuf", [128, 624], "uint8"),
-    "ps": ("psum", [128, 4096], "float32"),
+    "lf": ("sbuf", [128, 16384], "float32"), "li": ("sbuf", [128, 128], "int32"), "lu": ("sbuf", [128, 1280], "uint16"),
+    "kin": ("sbuf", [128, 16], "int32"), "yb": ("sbuf", [128, 256], "float32"), "ps": ("psum", [128, 4096], "float32"),
 }
+SCRATCH.update({k: ("sbuf", [128, n], "bfloat16") for k, n in TILES.items()})
+SCRATCH.update({"q" + k: ("sbuf", [128, n], C4) for k, n in PACKS.items()})
+SCRATCH.update({"s" + k: ("sbuf", [128, n], "uint8") for k, n in PACKS.items()})
 SEMAPHORES = ["sV", "sS", "sP", "sG", "sent", "arr0", "arr1", "arr2", "dka", "dkb", "dxh", "dxl", "du", "dv", "dwc", "dws",
               "dkid", "doc", "dos0", "dos1", "dos2", "dos3", "dy0", "dy1",
               "dz0", "dz1", "dz2", "dz3", "dzs0", "dzs1", "dzs2", "dzs3"]
 A = AluOpType
 AF = ActivationFunctionType
 LAND = [128, 320, 480]
-CY, GA, SC, LAT, FAR = 1.0, 1.56, 3.8, 60.0, 2400.0
-TWO = ("lb", "lu", "xin", "uin", "vin", "xs", "th", "g1", "ft", "hb", "tsb", "ab", "ub", "one", "eb", "zt")
+CY, GA, SC, LAT, FAR = 0.9, 1.56, 3.8, 180.0, 3500.0
+TWO = tuple(TILES) + ("lu",)
 PLAN = {}
-TRIES = 3500
+TRIES = 4500
 
 
 def place(ops, prio, links, pen, back):
@@ -135,6 +123,7 @@ def rank_program(g, core, T, topo):
     def U(n): return new("lu", n)
     def W(name, a, b, s=1): return (name, a, b, s)
     def sub(v, a, b, s=1): return (v[0], v[1] + a, v[1] + b, s)
+    def part(v, h, n): return sub(v, n * h, n * h + n)
     def ap(v): return T[v[0]][:, v[1]:v[2]:v[3]] if v[3] != 1 else T[v[0]][:, v[1]:v[2]]
     def num(s): return ap(s) if isinstance(s, tuple) else s
     def views(*xs): return [x for x in xs if isinstance(x, tuple)]
@@ -152,7 +141,7 @@ def rank_program(g, core, T, topo):
                 lo, hi = lo // 512 * 512, (hi + 511) // 512 * 512
             spans.append((v[0], lo, hi, w or ps))
             for (l2, h2, w2, d) in log.get(v[0], []):
-                if l2 < hi and lo < h2 and (w or w2):
+                if l2 < hi and lo < h2 and (w or ps or w2):
                     deps[d] = deps.get(d, False) or not (chain and ps)
         me = len(ops)
         ops.append({"alts": alts, "deps": deps, "sem": sem, "inc": inc, "tail": tail})
@@ -242,7 +231,7 @@ def rank_program(g, core, T, topo):
            [o], [lc, ls, rc, rs], chain=not start)
 
     def dma(e, sem, out, in_, wr, rd, tail, after=()):
-        return do([(e, 100.0, lambda: Q[e].dma_start(out, in_))], wr, rd, sem=sem, inc=16, tail=tail, after=after)
+        return do([(x, 200.0, lambda x=x: Q[x].dma_start(out, in_)) for x in e], wr, rd, sem=sem, inc=16, tail=tail, after=after)
 
     kin = W("kin", 0, 16)
     dma("Y", "dka", T.kin[:, 0:8], T.ka[:], [sub(kin, 0, 8)], [], 1600.0)
@@ -324,18 +313,22 @@ def rank_program(g, core, T, topo):
         s = wrapscan(v, 16, half)
         return lin(o or U(n_of(s)), s, inv16, add)
 
+    def wrap4(v):
+        return lin(U(n_of(v) // 4), wrapscan(v, 4), inv44, r3m)
+
     k8 = ts(I(16), kin, 255, A.bitwise_and)
     ksc = lin(U(16), k8)
     X = F(24)
     lin(sub(X, 0, 16), k8)
     lin(sub(X, 16, 24), sub(X, 0, 8))
     PS1 = B(256)
-    put(PS1, ksc, pay)
+    for h in range(2):
+        put(PS1, part(ksc, h, 8), part(pay, h, 128))
     WPS, wps = U(16), F(16)
-    for h in (8, 0):
-        s = wrapscan(sub(PS1, 16 * h, 16 * h + 128), 16, True)
-        lin(sub(WPS, h, h + 8), s, inv16, -1.0)
-        lin(sub(wps, h, h + 8), s, inv16, 255.0)
+    for h in (1, 0):
+        s = wrapscan(part(PS1, h, 128), 16, True)
+        lin(part(WPS, h, 8), s, inv16, -1.0)
+        lin(part(wps, h, 8), s, inv16, 255.0)
     BA = B(256)
     lin(sub(BA, 0, 128), lut, ind=sub(ksc, 8, 16))
     lin(sub(BA, 128, 256), lut, ind=sub(ksc, 0, 8))
@@ -346,6 +339,7 @@ def rank_program(g, core, T, topo):
        [W("qp", 0, 128)], [W("qu", 0, 128), cU])
     act(W("sp", 0, 128), W("su", 0, 128), AF.Copy, ind=cU)
     PP = W("ps", 2048, 2176)
+    th = W("th", 0, 1024)
 
     def scores(x):
         quant("x", 128, 256, W(x, 512, 1024))
@@ -354,9 +348,11 @@ def rank_program(g, core, T, topo):
         for b in range(4):
             mm(W("ps", 512 * b, 512 * b + 256), "e", 128 * b, "x", 0)
         for b in range(4):
-            lin(W("xs", b, 1024, 4), W("ps", 512 * b, 512 * b + 256))
+            lin(W("th", b, 1024, 4), W("ps", 512 * b, 512 * b + 256), 0.5)
+        lin(W("xs", 0, 1024), th, 2.0)
 
     scores("xin")
+    th2 = lin(W("th2", 0, 512), W("th", 0, 512))
     base, delta = F(32), F(32)
     slot = ts(F(16), wps, 384.0, A.is_ge, -128.0, A.mult)
     par = F(8)
@@ -380,42 +376,42 @@ def rank_program(g, core, T, topo):
     lin(sub(base, 16, 24), sub(w01, 0, 8), 1.0, 128.0)
     tt(sub(delta, 16, 24), sub(w01, 8, 16), sub(w01, 0, 8), A.subtract)
     ts(sub(TB, 128, 255), sub(PP, 0, 127), 0.0, A.is_gt, 1.0, A.add)
-    lin(sub(TB, 0, 127), sub(TB, 128, 255), -1.0, 3.0)
+    ts(sub(TB, 0, 127), sub(PP, 0, 127), 0.0, A.is_le, 1.0, A.add)
     lin(sub(TB, 256, 384), sub(TB, 0, 256), ind=sub(WPS, 8, 16))
     ilb = lin(B(128), sub(TB, 0, 256), 1.0, 127.0, ind=sub(WPS, 0, 8))
     s = wrapscan(sub(TB, 128, 384), 16, True)
-    sel = F(32)
-    lin(sub(sel, 0, 16), s, inv16, -1.0)
-    lin(sub(sel, 16, 32), s, inv16, -1.0)
-    m1 = tt(F(32), sel, delta, A.mult)
-    m2 = tt(F(32), m1, base, A.add)
+    sel, m1, di = lin(F(16), s, inv16, -1.0), F(32), lin(F(32), delta, inv16)
+    tt(sub(m1, 0, 16), s, sub(di, 0, 16), A.mult)
+    tt(sub(m1, 16, 32), s, sub(di, 16, 32), A.mult)
+    m2 = tt(F(32), m1, tt(F(32), base, delta, A.subtract), A.add)
     WS = lin(U(32), m2, 1.0, -128.0)
     Wc = sub(WS, 0, 16)
     R = B(256)
     for h in range(2):
-        lin(sub(R, 128 * h, 128 * h + 128), io1b, ind=sub(Wc, 8 * h, 8 * h + 8))
+        lin(part(R, h, 128), io1b, ind=part(Wc, h, 8))
     val = lin(B(256), nio, ind=sub(WS, 16, 32))
     for i in range(8):
-        own = B(256)
+        own, v2 = B(256), B(256)
         for h in range(2):
-            lin(sub(own, 128 * h, 128 * h + 128), sub(val, 128 * h, 128 * h + 128), only="VS"[h])
-        val = tt(B(256), val, own, A.add, ind=Wc)
+            lin(part(own, h, 128), part(val, h, 128))
+        for h in range(2):
+            tt(part(v2, h, 128), val, part(own, h, 128), A.add, ind=part(Wc, h, 8))
+        val = v2
         if i < 7:
             R2, W2 = B(256), U(16)
             for h in range(2):
-                lin(sub(R2, 128 * h, 128 * h + 128), R, ind=sub(Wc, 8 * h, 8 * h + 8), only="S")
-                wrap(sub(R2, 128 * h, 128 * h + 128), o=sub(W2, 8 * h, 8 * h + 8), half=True)
+                lin(part(R2, h, 128), R, ind=part(Wc, h, 8), only="S")
+                wrap(part(R2, h, 128), o=part(W2, h, 8), half=True)
             R, Wc = R2, W2
     sil = wrapscan(ilb, 16, True)
-    wpar = lin(U(8), par, 1.0, -128.0)
-    UP = lin(F(128), io1, ind=wpar)
-    ev0 = lin(F(8), sil, invm, 16256.0)
-    ev1 = tt(F(8), ev0, par, A.add)
-    Wev = lin(U(8), ev1)
-    num1 = tt(B(128), val, ilb, A.add, ind=Wev)
+    PID = lin(F(128), io1, ind=lin(U(8), par, 1.0, -128.0))
+    ev1 = tt(F(8), lin(F(8), sil, invm, 16256.0), par, A.add)
+    num1 = tt(B(128), val, ilb, A.add, ind=lin(U(8), ev1))
     Wn = wrap(num1, half=True)
     fill(W("ft", 0, 512), 0)
-    LID = sub(io1, 0, 128)
+    W4 = wrap4(PID)
+    for h in range(4):
+        tt(W("sm", 128 * h, 128 * h + 128), th, part(th2, h, 128), A.add, ind=part(W4, h, 8))
     WAB = X
     tw = F(16)
     lin(sub(tw, 0, 8), sub(sel, 0, 8))
@@ -425,7 +421,7 @@ def rank_program(g, core, T, topo):
     fill(sub(RZ, 0, 8), 0)
     REP = sub(RZ, 8, 392)
     for t in range(3):
-        fill(sub(MK, 256 * t, 256 * t + 256), 0)
+        fill(part(MK, t, 256), 0)
     T01 = fill(B(256), 1)
     t01 = sub(T01, 128, 256)
     BI = B(256)
@@ -441,20 +437,16 @@ def rank_program(g, core, T, topo):
 
     for t in range(3):
         K = 64 >> t
-        OL = F(128 if t == 0 else 64)
-        put(OL, Wn, LID)
-        lk = sub(OL, 1, 2 * K, 2)
-        if t == 1:
-            OP = F(64)
-            put(OP, Wn, PID)
-            pk = sub(OP, 1, 2 * K, 2)
-        else:
-            Wk = wrap(lk)
-            pk = lin(F(K), UP, ind=Wk)
-        Wl = lin(U(K // 4), wrapscan(lk, 4), inv44, r3m)
-        g1 = lin(W("g1", 0, 4 * K), W("xs", 0, 1024), ind=Wl)
-        Wp4 = lin(U(K // 4), wrapscan(pk, 4), inv44, r3m)
-        lin(W("ft", 0, 4 * K), tt(W("th", 0, 4 * K), W("xs", 0, 1024), g1, A.add, ind=Wp4), 0.5)
+        m = 128 if t == 0 else 64
+        OL = F(m)
+        put(OL, Wn, sub(io1, 0, m))
+        ok = sub(OL, 1, 2 * K, 2)
+        Wl = wrap4(ok)
+        for h in range(2):
+            lin(W("ft", 2 * K * h, 2 * K * h + 2 * K), W("sm", 0, 4 * m), ind=part(Wl, h, K // 8))
+        Wk = wrap(ok)
+        lk = ok if t == 0 else lin(F(K), LID, ind=Wk)
+        pk = lin(F(K), PID, ind=Wk)
         quant("f", 128 * t, 128 * t + 128, W("ft", 0, 512))
         d = T.cores[rank ^ (1 << t)]
         a = LAND[t]
@@ -496,7 +488,7 @@ def rank_program(g, core, T, topo):
         prv = tt(F(K), left, sub(kc, 0, K), A.mult)
         Ws1 = wrap(s1)
         right = lin(B(K), left, -1.0, 1.0)
-        mk = sub(MK, 256 * t, 256 * t + 256)
+        mk = part(MK, t, 256)
         put(PRV, Wp, prv)
         put(mk, Ws1, right)
         SP = F(2 * K)
@@ -537,10 +529,8 @@ def rank_program(g, core, T, topo):
         lin(sub(WAB, 16, 24), sub(WAB, 0, 8))
         if t == 0:
             ll = ts(F(8), sub(LRw, 0, 8), 128.0, A.is_lt)
-            i1 = lin(F(8), ll, -1024.0, 256.0)
-            i2 = tt(F(8), i1, sub(LRw, 0, 8), A.add)
-            i3 = tt(F(8), i2, sub(self2, 0, 8), A.max)
-            Wm = lin(U(8), i3, 1.0, -256.0)
+            i2 = tt(F(8), lin(F(8), ll, -1024.0, 256.0), sub(LRw, 0, 8), A.add)
+            Wm = lin(U(8), tt(F(8), i2, sub(self2, 0, 8), A.max), 1.0, -256.0)
             mid1 = lin(B(128), val, 1.0, 129.0, ind=Wm)
             Wmid = lin(U(8), tt(F(8), wrap(mid1, o=F(8), half=True), ll, A.add))
             INV = F(144)
@@ -596,11 +586,12 @@ def rank_program(g, core, T, topo):
             j1 = tt(F(63), sub(LH1, 1, 64), sub(io1, 0, 63), A.is_equal)
             j2 = tt(F(63), sub(GID, 1, 64), sub(GID, 0, 63), A.subtract)
             lin(col(PID, 63), col(GID, 63))
-            j3 = tt(F(63), j1, j2, A.mult)
-            tt(sub(PID, 0, 63), j3, sub(GID, 0, 63), A.add)
+            tt(sub(PID, 0, 63), tt(F(63), j1, j2, A.mult), sub(GID, 0, 63), A.add)
             ones = fill(F(64), 1)
             EV = iota(F(64), [[0, 32], [-1, 2]], 1)
             UP = fill(F(384), 1)
+            W4L = wrap4(LID)
+            WLID = wrap(LID)
             WLH = wrap(lh, add=-128.0, half=True)
         else:
             hh = lin(B(4), posw, 0.5, 129.75)
@@ -608,13 +599,18 @@ def rank_program(g, core, T, topo):
             bs = tt(F(4), lin(F(4), hh, -63.0, 8190.0), lin(F(4), posw, 32.0), A.add)
             Cr, C = C, F(320)
             for c in range(4):
-                lin(sub(C, 80 * c, 80 * c + 80), sub(Cr, 80 * c, 80 * c + 80), col(alw, c))
+                lin(part(C, c, 80), part(Cr, c, 80), col(alw, c))
             lin(sub(C, 64, 320, 64), bs)
             k3 = F(128)
             for h in range(2):
-                lin(sub(k3, 64 * h, 64 * h + 64), sub(AB1, 128 * h, 128 * h + 128), ind=W1)
+                lin(part(k3, h, 64), part(AB1, h, 128), ind=W1)
             put(UP, wrap(k3), GID)
+            PID = lin(F(64), UP, ind=WLID)
         scores("xs")
+        W4 = wrap4(PID)
+        for h in range(2):
+            g1 = lin(W("g1", 128 * h, 128 * h + 128), th, ind=part(W4L, h, 8))
+            tt(W("sm", 128 * h, 128 * h + 128), th, g1, A.add, ind=part(W4, h, 8))
         ts(sub(t01, 0, 127), sub(PP, 0, 127), 0.0, A.is_gt)
         pr = tt(B(320), t01, C, A.mult, ind=WG)
         posw = sub(scan(B(320), RS, pr, A.mult, A.add), 79, 320, 80)
@@ -625,7 +621,7 @@ def rank_program(g, core, T, topo):
     quant("x", 128, 256, W("xs", 512, 1024))
     dma("Y", "doc", T.oc[:], T.qx[:].bitcast(dt.uint8), [], [W("qx", 0, 256)], 2300.0)
     for k in range(4):
-        dma("Y", "dos%d" % k, T.osc[4 * k:4 * k + 4, :], T.sx[32 * k:32 * k + 4, :], [], [W("sx", 0, 256)], 1600.0)
+        dma("YS", "dos%d" % k, T.osc[4 * k:4 * k + 4, :], T.sx[32 * k:32 * k + 4, :], [], [W("sx", 0, 256)], 1600.0)
     for h in range(2):
         mm(W("ps", 512 * h, 512 * h + 128), "v", 0, "x", 128 * h)
     lin(W("yb", 0, 128), W("ps", 0, 128), only="V")
@@ -638,7 +634,7 @@ def rank_program(g, core, T, topo):
     off = tt(F(16), wrap(a1, o=F(16), add=7.0, half=True), tt(F(16), rw, self2, A.is_equal), A.mult)
     ko = lin(F(256), RZ, 1.0, -1.0, ind=lin(U(16), off))
     fill(col(ko, 255), -1)
-    dma("Y", "dkid", T.kid[:], T.lf[0:128:16, ko[1]:ko[2]], [], [ko], 1600.0)
+    dma("YS", "dkid", T.kid[:], T.lf[0:128:16, ko[1]:ko[2]], [], [ko], 1600.0)
 
     got = plan(ops)
     total, known, clocks = {}, {e: {} for e in Q}, {}

@@ -1,12 +1,14 @@
+import math
 from concourse.mybir import dt, AluOpType, ActivationFunctionType
 
 C4 = "float8_e4m3fn_x4"
-TILES = {"lb": 22528, "xin": 1024, "uin": 512, "vin": 512, "xs": 1280, "th": 1024, "th2": 512, "sm": 512, "g1": 256, "ft": 512,
+TILES = {"lb": 28672, "xin": 1024, "uin": 512, "vin": 512, "xs": 1280, "g1": 256, "ft": 512,
          "hb": 528, "tsb": 256, "ab": 256, "ub": 256, "one": 528, "eb": 528, "zt": 512}
 PACKS = {"e": 512, "u": 128, "p": 128, "v": 128, "w": 512, "x": 256, "f": 384, "z": 128, "l": 624}
 SCRATCH = {
-    "lf": ("sbuf", [128, 16384], "float32"), "li": ("sbuf", [128, 128], "int32"), "lu": ("sbuf", [128, 1280], "uint16"),
+    "lf": ("sbuf", [128, 12288], "float32"), "li": ("sbuf", [128, 128], "int32"), "lu": ("sbuf", [128, 1280], "uint16"),
     "kin": ("sbuf", [128, 16], "int32"), "yb": ("sbuf", [128, 256], "float32"), "ps": ("psum", [128, 4096], "float32"),
+    "sm": ("sbuf", [128, 512], "float32"),
 }
 SCRATCH.update({k: ("sbuf", [128, n], "bfloat16") for k, n in TILES.items()})
 SCRATCH.update({"q" + k: ("sbuf", [128, n], C4) for k, n in PACKS.items()})
@@ -122,34 +124,36 @@ def rank_program(g, core, T, topo):
     def I(n): return new("li", n)
     def U(n): return new("lu", n)
     def W(name, a, b, s=1): return (name, a, b, s)
-    def sub(v, a, b, s=1): return (v[0], v[1] + a, v[1] + b, s)
+    def sub(v, a, b, s=1): return (v[0], v[1] + a * v[3], min(v[2], v[1] + b * v[3]), s * v[3])
     def part(v, h, n): return sub(v, n * h, n * h + n)
+    def n_of(v): return (v[2] - v[1] + v[3] - 1) // v[3]
+    def even(v): return sub(v, 0, n_of(v), 2)
+    def odd(v): return sub(v, 1, n_of(v), 2)
     def ap(v): return T[v[0]][:, v[1]:v[2]:v[3]] if v[3] != 1 else T[v[0]][:, v[1]:v[2]]
     def num(s): return ap(s) if isinstance(s, tuple) else s
     def views(*xs): return [x for x in xs if isinstance(x, tuple)]
     def col(v, j): return sub(v, j, j + 1)
-    def n_of(v): return (v[2] - v[1] + v[3] - 1) // v[3]
     def src(v, ind): return ap(v).indirect(ap(ind)) if ind else ap(v)
 
     def do(alts, wr, rd, sem=None, inc=1, tail=0.0, chain=False, after=()):
         deps = {d: True for d in after}
         spans = []
         for v, w in [(v, True) for v in wr] + [(v, False) for v in rd]:
-            lo, hi = v[1], v[2]
+            lo, hi, step = v[1], v[1] + (n_of(v) - 1) * v[3] + 1, v[3]
             ps = v[0] == "ps"
             if ps:
-                lo, hi = lo // 512 * 512, (hi + 511) // 512 * 512
-            spans.append((v[0], lo, hi, w or ps))
-            for (l2, h2, w2, d) in log.get(v[0], []):
-                if l2 < hi and lo < h2 and (w or ps or w2):
+                lo, hi, step = lo // 512 * 512, (hi + 511) // 512 * 512, 1
+            spans.append((v[0], lo, hi, step, w or ps))
+            for (l2, h2, s2, w2, d) in log.get(v[0], []):
+                if l2 < hi and lo < h2 and (w or ps or w2) and (lo - l2) % math.gcd(step, s2) == 0:
                     deps[d] = deps.get(d, False) or not (chain and ps)
         me = len(ops)
         ops.append({"alts": alts, "deps": deps, "sem": sem, "inc": inc, "tail": tail})
-        for (name, lo, hi, w) in spans:
+        for (name, lo, hi, step, w) in spans:
             old = log.get(name, [])
             if w:
-                old = [x for x in old if not (lo <= x[0] and x[1] <= hi)]
-            log[name] = old + [(lo, hi, w, me)]
+                old = [x for x in old if not (lo <= x[0] and x[1] <= hi and x[2] % step == 0 and (x[0] - lo) % step == 0)]
+            log[name] = old + [(lo, hi, step, w, me)]
         return me
 
     def vt(o, i, ind, k=1.0):
@@ -204,8 +208,9 @@ def rank_program(g, core, T, topo):
         do([x for x in alts if only in (None, x[0])], [o], [])
         return o
 
-    def scan(o, d0, d1, op0, op1):
-        do([("V", vt(o, d1, None), lambda: g.vector.tensor_tensor_scan(ap(o), ap(d0), ap(d1), 0.0, op0, op1))], [o], [d0, d1])
+    def scan(o, d0, d1, op0=A.mult, op1=A.add):
+        do([("V", vt(o, d1 if d0[0] in TWO else d0, None), lambda: g.vector.tensor_tensor_scan(ap(o), ap(d0), ap(d1), 0.0, op0, op1))],
+           [o], [d0, d1])
         return o
 
     def act(o, i, func, ind=None, bias=0.0, scale=1.0):
@@ -245,21 +250,26 @@ def rank_program(g, core, T, topo):
 
     pi = iota(I(1), [[0, 1]], 0, 1)
     one = fill(W("one", 0, 528), 1, "V")
-    io1b = scan(B(256), sub(one, 0, 256), sub(one, 0, 256), A.mult, A.add)
-    io = lin(F(128), sub(io1b, 0, 128), 1.0, -1.0)
-    io1 = lin(F(256), io1b)
-    pay = B(256)
-    lin(sub(pay, 0, 255), sub(io1b, 0, 255))
-    fill(col(pay, 255), 128)
-    lut = B(256)
-    fill(sub(lut, 0, 128), 256)
-    lin(sub(lut, 128, 256), sub(io1b, 0, 128))
+    SG = B(528)
+    io1 = scan(sub(SG, 257, 513), sub(one, 0, 256), sub(one, 0, 256))
+    lin(sub(SG, 0, 256), io1, 1.0, -257.0)
+    fill(col(SG, 256), 0)
+    fill(sub(SG, 513, 528), 0)
+    io = sub(SG, 256, 528)
+    leafy = B(256)
+    fill(sub(leafy, 0, 256, 129), 0)
+    fill(sub(leafy, 1, 129), 1)
+    fill(sub(leafy, 130, 256), 0)
+    PT = B(256)
+    for h in range(2):
+        lin(part(PT, h, 128), sub(io1, 0, 128))
+    UT = lin(B(256), PT, 1.0, 128.0)
+    Z128 = iota(B(256), [[0, 128], [128, 2]], 0)
+    Z1 = iota(B(128), [[0, 64], [1, 2]], 0)
     eb = W("eb", 0, 528)
     do([("G", 170 + 2 * CY * 528, lambda: g.affine_select(ap(eb), ap(one), [[-1, 528]], A.is_equal, 0.0, 3, 4))], [eb], [one])
     crf = F(20)
-    for c in range(4):
-        iota(sub(crf, 5 * c, 4 * c + 4), [[16, 4 - c]], 16 * c)
-        iota(sub(crf, 4 * c + 4, 5 * c + 5), [[16, c + 1]], 64)
+    iota(crf, [[16, 4], [16, 5]], 0)
     quant("z", 0, 128, fill(W("zt", 0, 512), 0))
     for k, z in enumerate((0, 192, 352, 496)):
         dma("Y", "dz%d" % k, T.ql[:, z:z + 128].bitcast(dt.uint8), T.qz[:].bitcast(dt.uint8),
@@ -273,73 +283,80 @@ def rank_program(g, core, T, topo):
     ts(col(ri, 2), pi, 3, A.bitwise_and)
     rf = lin(F(3), ri)
     r, r4, r3 = col(rf, 0), col(rf, 1), col(rf, 2)
-    TB = B(384)
-    fill(sub(TB, 127, 256, 128), 1)
     inv16 = ts(F(1), r, 15.0, A.is_equal, 1.0 / 1024, A.max)
     inv4 = ts(F(1), r4, 3.0, A.is_equal, 1.0 / 1024, A.max)
     inv44 = lin(F(1), inv4, 4.0)
-    invm = lin(F(1), inv16, -128.0)
+    inv2, invm, inv128 = lin(F(1), inv16, 2.0), lin(F(1), inv16, -1.0), lin(F(1), inv16, 128.0)
     r3m = lin(F(1), r3, 1.0, -4.0)
-    r1, r41, r256 = lin(F(1), r, 1.0, 1.0), lin(F(1), r4, 1.0, 1.0), lin(F(1), r, 1.0, 256.0)
+    r1, r41 = lin(F(1), r, 1.0, 1.0), lin(F(1), r4, 1.0, 1.0)
     d0, d1 = F(32), F(32)
     ts(sub(d0, 0, 16), sub(io, 0, 16), r, A.not_equal)
     ts(sub(d1, 0, 16), sub(io, 0, 16), r1, A.is_equal, 1024.0, A.mult)
     ts(sub(d0, 16, 32), sub(io, 0, 16), r4, A.not_equal)
     ts(sub(d1, 16, 32), sub(io, 0, 16), r41, A.is_equal, 1024.0, A.mult)
-    pt = F(32)
-    tt(sub(pt, 0, 16), sub(d0, 0, 16), sub(d1, 0, 16), A.max)
-    tt(sub(pt, 16, 32), sub(d0, 16, 32), sub(d1, 16, 32), A.max)
+    pt = tt(F(32), d0, d1, A.max)
     c16 = lin(U(8), sub(io, 0, 8), 0.0, r)
     c4 = lin(U(8), sub(io, 0, 8), 0.0, r3)
-    P16b = B(320)
-    lin(sub(P16b, 0, 128), sub(pt, 0, 16), ind=c16)
-    lin(sub(P16b, 128, 256), sub(P16b, 0, 128))
-    lin(sub(P16b, 256, 320), sub(P16b, 0, 64))
-    P16 = lin(F(128), sub(P16b, 0, 128))
-    P4 = lin(F(128), sub(pt, 16, 32), ind=c4)
-    self2 = F(16)
-    lin(sub(self2, 0, 8), sub(io, 0, 8), 16.0, r256)
-    lin(sub(self2, 8, 16), sub(io, 0, 8), 16.0, r256)
+    P16 = B(256)
+    lin(sub(P16, 0, 128), sub(pt, 0, 16), ind=c16)
+    lin(sub(P16, 128, 256), sub(P16, 0, 128))
+    P4 = lin(B(128), sub(pt, 16, 32), ind=c4)
+    own = F(16)
+    for h in range(2):
+        lin(part(own, h, 8), sub(io, 0, 8), 16.0, r)
+    self1 = lin(F(16), own, 1.0, 257.0)
     cU = lin(U(8), sub(io, 0, 8), 16.0)
-    nio = iota(F(8), [[-1, 8]], 0)
 
-    def wrapscan(v, per=16, half=False):
+    def wrapscan(v, per=16, o=None):
         n = n_of(v)
-        o = B(n) if half else F(n)
-        scan(o, sub(P16b if half else P16 if per == 16 else P4, 0, n), v, A.mult, A.max)
+        o = o or (B(n) if v[0] == "lb" else F(n))
+        scan(o, sub(P16 if per == 16 else P4, 0, n), v, A.mult, A.max)
         return sub(o, per - 1, n, per)
 
-    def wrap(v, o=None, add=-1.0, half=False):
-        s = wrapscan(v, 16, half)
+    def wrap(v, o=None, add=-1.0):
+        s = wrapscan(v)
         return lin(o or U(n_of(s)), s, inv16, add)
 
     def wrap4(v):
         return lin(U(n_of(v) // 4), wrapscan(v, 4), inv44, r3m)
 
-    k8 = ts(I(16), kin, 255, A.bitwise_and)
-    ksc = lin(U(16), k8)
+    ksc = lin(U(16), kin, 1.0, 1.0)
+    PS = B(272)
+    fill(sub(PS, 256, 272), 128)
+    put(sub(PS, 0, 256), ksc, io1)
+    s = wrapscan(sub(PS, 1, 257))
+    WPS, WP2 = lin(U(16), s, inv16, -1.0), lin(U(16), s, inv2, -1.0)
     X = F(24)
-    lin(sub(X, 0, 16), k8)
-    lin(sub(X, 16, 24), sub(X, 0, 8))
-    PS1 = B(256)
+    lin(sub(X, 0, 16), kin, 1.0, 1.0)
+    lin(sub(X, 16, 24), sub(kin, 0, 8), 1.0, 1.0)
+    pen = ts(F(24), X, 128.0, A.is_le, 512.0, A.mult)
+    X2 = tt(F(24), X, pen, A.add)
+    L, L2 = F(32), F(16)
+    m128 = tt(sub(L, 16, 32), sub(X2, 8, 24), self1, A.min)
+    in2 = tt(F(16), m128, lin(F(16), sub(pen, 0, 16), -1.0, 512.0), A.add)
+    tt(sub(L, 8, 16), sub(X2, 0, 8), sub(in2, 0, 8), A.min)
+    tt(sub(L, 0, 8), sub(X2, 8, 16), sub(in2, 8, 16), A.min)
+    tt(sub(L2, 0, 8), sub(L, 0, 8), sub(L, 8, 16), A.subtract)
+    tt(sub(L2, 8, 16), sub(L, 24, 32), sub(L, 16, 24), A.subtract)
+    WL = lin(U(24), sub(L, 8, 32), 1.0, 128.0)
+    WL2 = lin(U(16), L2, 1.0, 256.0)
+    WL3 = lin(U(16), tt(F(16), sub(pen, 8, 24), sub(pen, 0, 16), A.subtract), 1.0 / 512, 256.0)
+    DR, DU, DW, MS = B(512), B(256), B(512), B(256)
     for h in range(2):
-        put(PS1, part(ksc, h, 8), part(pay, h, 128))
-    WPS, wps = U(16), F(16)
-    for h in (1, 0):
-        s = wrapscan(part(PS1, h, 128), 16, True)
-        lin(part(WPS, h, 8), s, inv16, -1.0)
-        lin(part(wps, h, 8), s, inv16, 255.0)
-    BA = B(256)
-    lin(sub(BA, 0, 128), lut, ind=sub(ksc, 8, 16))
-    lin(sub(BA, 128, 256), lut, ind=sub(ksc, 0, 8))
-    sib = lin(B(128), BA, ind=sub(WPS, 8, 16))
+        lin(part(MS, h, 128), SG, ind=sub(WL, 8 + 8 * h, 16 + 8 * h))
+        lin(odd(part(DR, h, 256)), SG, ind=part(WL, h, 8))
+        lin(even(part(DR, h, 256)), SG, ind=part(WL2, h, 8))
+        lin(odd(part(DW, h, 256)), leafy, ind=part(ksc, h, 8))
+        lin(even(part(DW, h, 256)), SG, ind=part(WL3, h, 8))
+    lin(odd(DU), MS, ind=sub(WPS, 8, 16))
+    tt(even(DU), UT, odd(DU), A.subtract, ind=sub(WPS, 8, 16))
     quant("u", 0, 128, W("uin", 0, 512))
     do([("V", 250.0, lambda: g.vector.tensor_copy(T.qp[:, 0:128].bitcast(dt.uint32),
                                                   T.qu[:, 0:128].bitcast(dt.uint32).indirect(ap(cU))))],
        [W("qp", 0, 128)], [W("qu", 0, 128), cU])
     act(W("sp", 0, 128), W("su", 0, 128), AF.Copy, ind=cU)
     PP = W("ps", 2048, 2176)
-    th = W("th", 0, 1024)
+    xs = W("xs", 0, 1024)
 
     def scores(x):
         quant("x", 128, 256, W(x, 512, 1024))
@@ -348,105 +365,70 @@ def rank_program(g, core, T, topo):
         for b in range(4):
             mm(W("ps", 512 * b, 512 * b + 256), "e", 128 * b, "x", 0)
         for b in range(4):
-            lin(W("th", b, 1024, 4), W("ps", 512 * b, 512 * b + 256), 0.5)
-        lin(W("xs", 0, 1024), th, 2.0)
+            lin(W("xs", b, 1024, 4), W("ps", 512 * b, 512 * b + 256))
 
     scores("xin")
-    th2 = lin(W("th2", 0, 512), W("th", 0, 512))
-    base, delta = F(32), F(32)
-    slot = ts(F(16), wps, 384.0, A.is_ge, -128.0, A.mult)
-    par = F(8)
-    tt(sub(base, 8, 16), sub(wps, 8, 16), sub(slot, 8, 16), A.add)
-    tt(par, sub(wps, 0, 8), sub(slot, 0, 8), A.add)
-    fill(sub(base, 24, 32), 128)
-    sibw = wrap(sib, o=F(8), add=127.0, half=True)
-    u1 = tt(F(8), sibw, sub(base, 8, 16), A.min)
-    tt(sub(delta, 8, 16), u1, sub(base, 8, 16), A.subtract)
-    ts(sub(delta, 24, 32), sibw, 383.0, A.is_equal)
-    pen = ts(F(24), X, 128.0, A.is_lt, 512.0, A.mult)
-    X2 = tt(F(24), X, pen, A.add)
-    inner = tt(F(16), sub(X2, 8, 24), self2, A.min)
-    bump = lin(F(16), sub(pen, 0, 16), -2.0, 1024.0)
-    in2 = tt(F(16), inner, bump, A.add)
-    s01 = tt(F(16), sub(X2, 0, 16), in2, A.min)
-    nY = lin(F(16), sub(pen, 8, 24), 2.0 ** -18, 2.0 ** -9)
-    w01 = tt(F(16), sub(pen, 0, 16), nY, A.mult)
-    lin(sub(base, 0, 8), sub(s01, 0, 8))
-    tt(sub(delta, 0, 8), sub(s01, 8, 16), sub(s01, 0, 8), A.subtract)
-    lin(sub(base, 16, 24), sub(w01, 0, 8), 1.0, 128.0)
-    tt(sub(delta, 16, 24), sub(w01, 8, 16), sub(w01, 0, 8), A.subtract)
-    ts(sub(TB, 128, 255), sub(PP, 0, 127), 0.0, A.is_gt, 1.0, A.add)
-    ts(sub(TB, 0, 127), sub(PP, 0, 127), 0.0, A.is_le, 1.0, A.add)
-    lin(sub(TB, 256, 384), sub(TB, 0, 256), ind=sub(WPS, 8, 16))
-    ilb = lin(B(128), sub(TB, 0, 256), 1.0, 127.0, ind=sub(WPS, 0, 8))
-    s = wrapscan(sub(TB, 128, 384), 16, True)
-    sel, m1, di = lin(F(16), s, inv16, -1.0), F(32), lin(F(32), delta, inv16)
-    tt(sub(m1, 0, 16), s, sub(di, 0, 16), A.mult)
-    tt(sub(m1, 16, 32), s, sub(di, 16, 32), A.mult)
-    m2 = tt(F(32), m1, tt(F(32), base, delta, A.subtract), A.add)
-    WS = lin(U(32), m2, 1.0, -128.0)
-    Wc = sub(WS, 0, 16)
-    R = B(256)
+    T2, IR = fill(B(512), 0), fill(B(256), 0)
+    ts(sub(T2, 1, 254, 2), sub(PP, 0, 127), 0.0, A.is_gt)
+    ts(sub(T2, 257, 510, 2), sub(PP, 0, 127), 0.0, A.is_le)
+    TD = sub(T2, 0, 256)
+    lin(odd(IR), T2, ind=sub(WP2, 8, 16))
+    R, val, EE = B(512), B(512), B(512)
+    scan(sub(R, 0, 256), TD, sub(DR, 0, 256))
+    scan(sub(R, 256, 512), IR, DU)
+    Wc, w0 = U(16), B(256)
     for h in range(2):
-        lin(part(R, h, 128), io1b, ind=part(Wc, h, 8))
-    val = lin(B(256), nio, ind=sub(WS, 16, 32))
+        lin(part(Wc, h, 8), wrapscan(odd(part(R, h, 256))), inv2, -1.0)
+        scan(part(val, h, 256), TD, part(DW, h, 256))
+        lin(part(w0, h, 128), odd(part(val, h, 256)))
     for i in range(8):
-        own, v2 = B(256), B(256)
+        mine, v2 = w0 if i == 0 else B(256), B(256)
         for h in range(2):
-            lin(part(own, h, 128), part(val, h, 128))
+            if i:
+                lin(part(mine, h, 128), part(val, h, 128))
         for h in range(2):
-            tt(part(v2, h, 128), val, part(own, h, 128), A.add, ind=part(Wc, h, 8))
+            tt(part(v2, h, 128), val, part(mine, h, 128), A.add, ind=part(Wc, h, 8))
         val = v2
         if i < 7:
             R2, W2 = B(256), U(16)
             for h in range(2):
                 lin(part(R2, h, 128), R, ind=part(Wc, h, 8), only="S")
-                wrap(part(R2, h, 128), o=part(W2, h, 8), half=True)
+                wrap(part(R2, h, 128), o=part(W2, h, 8))
             R, Wc = R2, W2
-    sil = wrapscan(ilb, 16, True)
-    PID = lin(F(128), io1, ind=lin(U(8), par, 1.0, -128.0))
-    ev1 = tt(F(8), lin(F(8), sil, invm, 16256.0), par, A.add)
-    num1 = tt(B(128), val, ilb, A.add, ind=lin(U(8), ev1))
-    Wn = wrap(num1, half=True)
+    BI = B(272)
+    fill(sub(BI, 0, 16), 1)
+    lin(sub(BI, 16, 144), io, 1.0, 1.0, ind=sub(ksc, 8, 16))
+    lin(sub(BI, 144, 272), io, 1.0, 1.0, ind=sub(ksc, 0, 8))
+    LT = fill(B(512), 0)
+    lin(sub(LT, 0, 512, 4), T2, ind=sub(WP2, 0, 8))
+    lin(sub(LT, 2, 512, 4), PT, ind=sub(WPS, 0, 8))
+    lin(sub(LT, 3, 512, 4), sub(BI, 16, 272), 1.0, -1.0, ind=sub(WPS, 0, 8))
+    scan(sub(EE, 0, 256), Z128, even(LT))
+    scan(sub(EE, 256, 512), TD, sub(DR, 256, 512))
+    WE = wrap(odd(EE))
+    Wn = lin(U(8), wrapscan(lin(B(128), val, ind=sub(WE, 0, 8))), invm, 128.0)
     fill(W("ft", 0, 512), 0)
-    W4 = wrap4(PID)
-    for h in range(4):
-        tt(W("sm", 128 * h, 128 * h + 128), th, part(th2, h, 128), A.add, ind=part(W4, h, 8))
-    WAB = X
-    tw = F(16)
-    lin(sub(tw, 0, 8), sub(sel, 0, 8))
-    lin(sub(tw, 8, 16), sub(sel, 0, 8))
-    S1 = fill(F(320), 1)
-    RZ, PRV, MK = F(392), fill(F(256), 0), B(768)
-    fill(sub(RZ, 0, 8), 0)
-    REP = sub(RZ, 8, 392)
-    for t in range(3):
-        fill(part(MK, t, 256), 0)
-    T01 = fill(B(256), 1)
-    t01 = sub(T01, 128, 256)
-    BI = B(256)
-    lin(sub(BI, 0, 128), io1b, ind=sub(ksc, 8, 16))
-    lin(sub(BI, 128, 256), io1b, ind=sub(ksc, 0, 8))
-    SIB = lin(B(128), BI, ind=sub(WPS, 0, 8))
-    iota(sub(REP, 0, 256), [[1, 256]], 1)
-    fill(sub(REP, 256, 384), 256)
+    W4 = wrap4(sub(LT, 2, 512, 4))
+    for h in range(2):
+        tt(W("sm", 256 * h, 256 * h + 256), sub(xs, 512, 1024), part(xs, h, 256), A.add, ind=part(W4, h, 16))
+    REP = lin(B(272), io)
+    RK, MR = fill(F(128), 0), fill(F(816), 0)
+    t01 = fill(B(128), 1)
     fill(W("xs", 1024, 1280), 0)
     fill(W("hb", 0, 272), 0)
     kc = iota(F(64), [[1, 64]], 257)
     r416 = lin(F(1), r4, 1.0, 272.0)
+    TO = odd(TD)
+    WB = [sub(ksc, 8, 16), sub(ksc, 0, 8)]
 
     for t in range(3):
         K = 64 >> t
         m = 128 if t == 0 else 64
-        OL = F(m)
+        OL = B(m)
         put(OL, Wn, sub(io1, 0, m))
-        ok = sub(OL, 1, 2 * K, 2)
-        Wl = wrap4(ok)
+        Wl = wrap4(sub(OL, 1, 2 * K, 2))
         for h in range(2):
-            lin(W("ft", 2 * K * h, 2 * K * h + 2 * K), W("sm", 0, 4 * m), ind=part(Wl, h, K // 8))
-        Wk = wrap(ok)
-        lk = ok if t == 0 else lin(F(K), LID, ind=Wk)
-        pk = lin(F(K), PID, ind=Wk)
+            lin(W("ft", 2 * K * h, 2 * K * h + 2 * K), W("sm", 0, 4 * m), 0.5, ind=part(Wl, h, K // 8))
         quant("f", 128 * t, 128 * t + 128, W("ft", 0, 512))
         d = T.cores[rank ^ (1 << t)]
         a = LAND[t]
@@ -463,51 +445,31 @@ def rank_program(g, core, T, topo):
            [W("qf", 128 * t, 128 * t + 128), W("sf", 128 * t, 128 * t + 128)],
            sem="arr%d" % t, inc=2 * len(topo.engines(d, core)), tail=FAR)
 
-        if t > 0:
-            lin(sub(t1, 0, 127), sub(t01, 0, 127), 1.0, 1.0)
-            s = wrapscan(t1, 16, True)
-            tw = F(16)
-            lin(sub(tw, 0, 8), s, inv16, -1.0)
-            lin(sub(tw, 8, 16), s, inv16, -1.0)
-        dd = tt(F(16), sub(WAB, 8, 24), sub(WAB, 0, 16), A.subtract)
-        LRw = tt(F(16), tt(F(16), dd, tw, A.mult), sub(WAB, 0, 16), A.add)
-        WLR = lin(U(16), LRw)
-        Wp = wrap(pk)
-        hk = lin(F(1), r3, float(K), r416)
-        hk2 = lin(F(1), r3, float(K), 15.0)
-        HC = lin(U(K // 4), sub(io, 0, K // 4), 4.0, hk)
-        if t == 0:
-            left = lin(F(K), ilb, 1.0, -128.0, ind=Wk)
-            s1 = lin(sub(S1, 0, K), SIB, ind=Wk)
-        else:
-            gl = lin(F(K), sub(ABb, 0, 256), ind=Wp)
-            gs = tt(F(K), sub(ABb, 128, 384), gl, A.add, ind=Wp)
-            left = tt(F(K), T01, tt(F(K), gl, lk, A.is_equal), A.not_equal, ind=Wp)
-            s1 = tt(sub(S1, 0, K), gs, lk, A.subtract)
-        lin(sub(S1, 256, 256 + K), s1)
-        prv = tt(F(K), left, sub(kc, 0, K), A.mult)
-        Ws1 = wrap(s1)
-        right = lin(B(K), left, -1.0, 1.0)
-        mk = part(MK, t, 256)
-        put(PRV, Wp, prv)
-        put(mk, Ws1, right)
-        SP = F(2 * K)
-        ix = tt(sub(SP, K, 2 * K), PRV, sub(io1, 0, K), A.max, ind=Ws1)
-        dup = tt(F(K), mk, prv, A.mult, ind=Wp)
-        so = tt(sub(SP, 0, K), S1, dup, A.max, ind=wrap(ix))
-        s = wrapscan(SP, 4)
-        XO = lin(U(K // 4), (s[0], s[1], s[1] + K - 3, 4), inv44, r3m)
-        HO = lin(U(K // 4), (s[0], s[1] + K, s[2], 4), inv4, hk2)
+        KT = lin(B(4 * K), LT, ind=Wl)
+        pk, s1 = sub(KT, 2, 4 * K, 4), sub(KT, 3, 4 * K, 4)
+        two = B(2 * K)
+        wrapscan(pk, o=part(two, 0, K))
+        wrapscan(s1, o=part(two, 1, K))
+        Wps = lin(U(2 * max(K // 16, 2)), sub(two, 15, 2 * K, 16), inv16) if K > 16 else None
+        Wp = part(Wps, 0, K // 16) if Wps else lin(U(1), col(two, 15), inv16)
+        Ws = part(Wps, 1, K // 16) if Wps else lin(U(1), col(two, 31), inv16)
+        rk, mr, SP = sub(RK, 0, 2 * K), part(MR, t, 272), F(4 * K)
+        tt(odd(rk), sub(KT, 0, 4 * K, 4), sub(kc, 0, K), A.mult)
+        put(mr, Ws, odd(rk))
+        lin(odd(part(SP, 1, 2 * K)), sub(mr, 128, 272), 1.0, 1.0, ind=Wp)
+        put(sub(REP, 128, 272), Wp, s1)
+        tt(sub(KT, 1, 4 * K, 4), REP, s1, A.not_equal, ind=Ws)
+        scan(part(SP, 0, 2 * K), rk, odd(KT), A.mult, A.max)
+        s = wrapscan(odd(SP), 4)
+        XO = lin(U(K // 4), part(s, 0, K // 4), inv44, r3m)
+        HO = lin(U(K // 4), part(s, 1, K // 4), inv4, lin(F(1), r3, float(K), 14.0))
+        HC = lin(U(K // 4), sub(io, 0, K // 4), 4.0, lin(F(1), r3, float(K), r416))
         Ts = lin(W("tsb", 0, 4 * K), W("xs", 0, 1280), ind=XO)
-        put(REP, Wp, so)
-        a1 = lin(B(256), REP, ind=WLR)
-        if t < 2:
-            ABb = B(384)
-            fill(sub(ABb, 0, 128), 1)
-            AB1 = lin(sub(ABb, 128, 384), REP, ind=wrap(a1, half=True))
-        if t == 1:
-            put(sub(ABb, 0, 256), Wp, iota(F(32), [[2, 32]], 258))
-            put(sub(ABb, 128, 384), Wp, iota(F(32), [[2, 32]], 322))
+        put(sub(REP, 128, 272), Wp, lin(B(K), REP, ind=Ws))
+        BI = B(272)
+        fill(sub(BI, 0, 16), 1)
+        for h in range(2):
+            lin(sub(BI, 16 + 128 * h, 144 + 128 * h), REP, 1.0, 1.0, ind=WB[h])
         n = 2 if t == 0 else 4
         for b in range(4):
             j = b % n
@@ -519,102 +481,92 @@ def rank_program(g, core, T, topo):
             relu(W("hb", 400, 528), W("ps", 3072, 3200))
         else:
             relu(W("hb", 272, 272 + 4 * K), W("ps", 2560, 2560 + 4 * K))
-        ab = tt(W("ab", 0, 4 * K), hb, Ts, A.add, ind=HO)
-        ub = tt(W("ub", 0, 4 * K), hb, ab, A.add, ind=HC)
+        ab = tt(W("ab", 0, 4 * K), hb, Ts, A.add, ind=HC)
+        ub = tt(W("ub", 0, 4 * K), hb, ab, A.add, ind=HO)
         put(W("xs", 0, 1280), XO, ub)
         if t == 2:
             break
-        WAB = F(24)
-        wrap(AB1, o=sub(WAB, 0, 16), half=True)
-        lin(sub(WAB, 16, 24), sub(WAB, 0, 8))
+        wb = wrap(sub(BI, 16, 272))
+        WB = [sub(wb, 0, 8), sub(wb, 8, 16)]
+        for k in range(2):
+            put(PS, Ws, lin(B(K), sub(PS, 128, 272), ind=Wp))
         if t == 0:
-            ll = ts(F(8), sub(LRw, 0, 8), 128.0, A.is_lt)
-            i2 = tt(F(8), lin(F(8), ll, -1024.0, 256.0), sub(LRw, 0, 8), A.add)
-            Wm = lin(U(8), tt(F(8), i2, sub(self2, 0, 8), A.max), 1.0, -256.0)
-            mid1 = lin(B(128), val, 1.0, 129.0, ind=Wm)
-            Wmid = lin(U(8), tt(F(8), wrap(mid1, o=F(8), half=True), ll, A.add))
-            INV = F(144)
-            put(INV, Wmid, sub(io1, 0, 128))
-            f1 = tt(F(63), sub(INV, 1, 127, 2), sub(INV, 2, 128, 2), A.add)
+            mid = wrapscan(lin(B(128), val, 1.0, 1.0, ind=sub(WE, 8, 16)))
+            INV = B(144)
+            put(INV, lin(U(8), mid, invm, 129.0), sub(io1, 0, 128))
+            f1 = scan(B(126), sub(Z1, 0, 126), sub(INV, 1, 127))
+            GID = fill(B(64), 128)
+            tt(sub(GID, 1, 64), odd(f1), sub(pk, 0, 63), A.subtract)
+            s, WG = wrapscan(GID), U(20)
+            W1 = lin(sub(WG, 0, 4), s, inv16, -1.0)
+            lin(sub(WG, 4, 8), s, inv16, -1.0)
+            lin(sub(WG, 8, 16), sub(WG, 0, 8))
+            lin(sub(WG, 16, 20), W1)
             WR = lin(U(20), crf, 1.0, r)
-            GID = F(128)
-            fill(col(GID, 0), 256)
-            tt(sub(GID, 1, 64), f1, lin(F(63), sub(pk, 0, 63), 1.0, -256.0), A.subtract)
-            lin(sub(GID, 64, 128), sub(GID, 0, 64))
-            WG = wrap(lin(B(320), GID, ind=WR), add=-129.0, half=True)
-            W1 = wrap(sub(GID, 0, 64), add=-129.0)
             lh = B(128)
-            lin(sub(lh, 0, 64), sub(val, 0, 128), 0.5, 192.25, ind=W1)
-            lin(sub(lh, 64, 128), sub(val, 128, 256), 0.5, 192.25, ind=W1)
-            LH1 = lin(F(128), lh, 1.0, -127.0)
-            lo1, hi1 = sub(LH1, 0, 64), sub(LH1, 64, 128)
+            lin(sub(lh, 0, 64), sub(val, 0, 128), -0.5, 192.25, ind=W1)
+            hv = tt(F(64), sub(val, 128, 256), lin(F(64), sub(w0, 128, 256), ind=W1), A.subtract, ind=W1)
+            lin(sub(lh, 64, 128), hv, -0.5, 192.25)
             icol = lin(F(4), sub(io, 0, 4), 16.0, r)
             nb, ia, ib = lin(F(4), icol, -1.0, -0.5), lin(F(4), icol, 1.0, 2.0), lin(F(4), icol, 1.0, -64.0)
-            KK = F(320)
+            KK = B(320)
             for c in range(4):
                 sg = act(F(64), sub(io, 0, 64), AF.Sign, bias=col(nb, c))
                 act(sub(KK, 80 * c, 64 * c + 64), sub(sg, 16 * c, 64), AF.Relu, scale=col(ia, c))
                 act(sub(KK, 64 * c + 64, 80 * c + 80), sub(sg, 0, 16 * c + 16), AF.Relu, scale=col(ib, c))
-            bd = F(128)
+            bd = B(128)
             lin(sub(bd, 0, 64), sub(lh, 0, 64), 1.0, -127.0)
             lin(sub(bd, 64, 128), sub(lh, 64, 128), -1.0, 192.0)
-            Mk = tt(F(320), bd, KK, A.is_lt, ind=WR)
-            uv = F(128)
-            tt(sub(uv, 0, 64), hi1, sub(io1, 0, 64), A.subtract)
-            tt(sub(uv, 64, 128), lo1, sub(io1, 0, 64), A.subtract)
-        else:
-            CUM = F(80)
-            al = lin(F(64), EV, ind=Wn)
-            fill(sub(CUM, 0, 1), 0)
-            scan(sub(CUM, 1, 65), ones, al, A.mult, A.add)
-            cum = lin(F(64), sub(CUM, 0, 64))
-            tsl = lin(F(64), t01, -2.0, 1.0, ind=W1)
-            n1 = tt(F(64), sub(CUM, 0, 65), cum, A.subtract, ind=sub(WLH, 0, 4))
-            n2 = tt(F(64), sub(CUM, 0, 65), cum, A.subtract, ind=sub(WLH, 4, 8))
-            uv = F(128)
-            tt(sub(uv, 0, 64), n2, tsl, A.mult)
-            tt(sub(uv, 64, 128), n1, tsl, A.mult)
-        C = tt(F(320), uv, Mk, A.mult, ind=WR)
-        if t == 0:
+            Mk = tt(B(320), bd, KK, A.is_lt, ind=WR)
+            uv = B(128)
+            tt(sub(uv, 0, 64), sub(lh, 64, 128), sub(io, 128, 192), A.subtract)
+            tt(sub(uv, 64, 128), sub(lh, 0, 64), sub(io, 128, 192), A.subtract)
+            C = tt(B(320), uv, Mk, A.mult, ind=WR)
             lin(sub(C, 64, 320, 64), icol)
-            t1 = B(128)
-            fill(col(t1, 127), 1)
             RS = fill(B(320), 1)
             fill(sub(RS, 0, 320, 80), 0)
-            LID = lin(F(64), sub(OL, 0, 128, 2))
-            PID = F(64)
-            j1 = tt(F(63), sub(LH1, 1, 64), sub(io1, 0, 63), A.is_equal)
-            j2 = tt(F(63), sub(GID, 1, 64), sub(GID, 0, 63), A.subtract)
-            lin(col(PID, 63), col(GID, 63))
-            tt(sub(PID, 0, 63), tt(F(63), j1, j2, A.mult), sub(GID, 0, 63), A.add)
-            ones = fill(F(64), 1)
-            EV = iota(F(64), [[0, 32], [-1, 2]], 1)
-            UP = fill(F(384), 1)
-            W4L = wrap4(LID)
-            WLID = wrap(LID)
-            WLH = wrap(lh, add=-128.0, half=True)
+            EV = iota(B(64), [[0, 32], [-1, 2]], 1)
+            W4L = wrap4(even(OL))
+            WLID = wrap(even(OL), add=0.0)
+            WLH = wrap(lh, add=-128.0)
         else:
+            CUM = B(80)
+            al = lin(B(64), EV, ind=Wn)
+            fill(col(CUM, 0), 0)
+            scan(sub(CUM, 1, 65), sub(one, 0, 64), al)
+            cum = lin(B(64), sub(CUM, 0, 64))
+            tsl = lin(B(64), t01, -2.0, 1.0, ind=W1)
+            nn, uv = B(128), B(128)
+            tt(sub(nn, 64, 128), sub(CUM, 0, 65), cum, A.subtract, ind=sub(WLH, 0, 4))
+            tt(sub(nn, 0, 64), sub(CUM, 0, 65), cum, A.subtract, ind=sub(WLH, 4, 8))
+            for h in range(2):
+                tt(part(uv, h, 64), part(nn, h, 64), tsl, A.mult)
             hh = lin(B(4), posw, 0.5, 129.75)
             alw = tt(F(4), lin(F(4), hh, 2.0, -259.0), posw, A.subtract)
             bs = tt(F(4), lin(F(4), hh, -63.0, 8190.0), lin(F(4), posw, 32.0), A.add)
-            Cr, C = C, F(320)
+            M2 = B(320)
             for c in range(4):
-                lin(part(C, c, 80), part(Cr, c, 80), col(alw, c))
+                lin(part(M2, c, 80), part(Mk, c, 80), col(alw, c))
+            C = tt(B(320), uv, M2, A.mult, ind=WR)
             lin(sub(C, 64, 320, 64), bs)
-            k3 = F(128)
-            for h in range(2):
-                lin(part(k3, h, 64), part(AB1, h, 128), ind=W1)
-            put(UP, wrap(k3), GID)
-            PID = lin(F(64), UP, ind=WLID)
+        Wsl = wrap(lin(B(64), PS, ind=WLID))
+        LT = fill(B(256), 0)
+        lin(sub(LT, 2, 256, 4), PT, ind=Wsl)
+        lin(sub(LT, 3, 256, 4), sub(BI, 16, 272), 1.0, -1.0, ind=Wsl)
         scores("xs")
-        W4 = wrap4(PID)
+        W4 = wrap4(sub(LT, 2, 256, 4))
         for h in range(2):
-            g1 = lin(W("g1", 128 * h, 128 * h + 128), th, ind=part(W4L, h, 8))
-            tt(W("sm", 128 * h, 128 * h + 128), th, g1, A.add, ind=part(W4, h, 8))
+            g1 = lin(W("g1", 128 * h, 128 * h + 128), xs, ind=part(W4L, h, 8))
+            tt(W("sm", 128 * h, 128 * h + 128), sub(xs, 512, 1024), g1, A.add, ind=part(W4, h, 8))
         ts(sub(t01, 0, 127), sub(PP, 0, 127), 0.0, A.is_gt)
         pr = tt(B(320), t01, C, A.mult, ind=WG)
-        posw = sub(scan(B(320), RS, pr, A.mult, A.add), 79, 320, 80)
+        posw = sub(scan(B(320), RS, pr), 79, 320, 80)
         Wn = lin(U(4), posw)
+        TB = fill(B(256), 0)
+        tt(sub(TB, 0, 127), sub(t01, 0, 127), sub(TO, 0, 127), A.not_equal)
+        TO = sub(TB, 0, 128)
+        lin(sub(TB, 128, 256), TO, -1.0, 1.0)
+        lin(sub(LT, 0, 256, 4), TB, ind=Wsl)
 
     quant("v", 0, 128, W("vin", 0, 512))
     quant("x", 0, 128, W("xs", 0, 512))
@@ -628,12 +580,15 @@ def rank_program(g, core, T, topo):
     lin(W("yb", 128, 256), W("ps", 512, 640), only="S")
     dma("Y", "dy0", T.y[:, 0:128], T.yb[:, 0:128], [], [W("yb", 0, 128)], 2000.0)
     dma("S", "dy1", T.y[:, 128:256], T.yb[:, 128:256], [], [W("yb", 128, 256)], 2000.0)
-    s, rw = wrapscan(sub(REP, 128, 256)), F(16)
-    lin(sub(rw, 0, 8), s, inv16, 127.0)
-    lin(sub(rw, 8, 16), s, inv16, 127.0)
-    off = tt(F(16), wrap(a1, o=F(16), add=7.0, half=True), tt(F(16), rw, self2, A.is_equal), A.mult)
-    ko = lin(F(256), RZ, 1.0, -1.0, ind=lin(U(16), off))
-    fill(col(ko, 255), -1)
+    TE = B(256)
+    lin(sub(TE, 0, 128), TO, -1.0, 2.0)
+    lin(sub(TE, 128, 256), TO, 1.0, 1.0)
+    slot = tt(F(16), lin(F(16), wrapscan(TE), inv128, -112.0), own, A.add)
+    stay = tt(F(8), wrap(sub(REP, 129, 257), o=F(8), add=128.0), sub(self1, 0, 8), A.is_equal)
+    off = F(16)
+    for h in range(2):
+        tt(part(off, h, 8), part(slot, h, 8), stay, A.mult)
+    ko = lin(F(256), BI, 1.0, -2.0, ind=lin(U(16), off))
     dma("YS", "dkid", T.kid[:], T.lf[0:128:16, ko[1]:ko[2]], [], [ko], 1600.0)
 
     got = plan(ops)

@@ -1,28 +1,30 @@
 import math
+from concourse.bass import DstId, RemoteDMATransfer
 from concourse.mybir import dt, AluOpType, ActivationFunctionType
 
 C4 = "float8_e4m3fn_x4"
 TILES = {"lb": 28672, "xin": 1024, "uin": 512, "vin": 512, "xs": 1280, "g1": 256, "ft": 512,
-         "hb": 528, "tsb": 256, "ab": 256, "ub": 256, "one": 528, "eb": 528, "zt": 512}
-PACKS = {"e": 512, "u": 128, "p": 128, "v": 128, "w": 512, "x": 256, "f": 384, "z": 128, "l": 624}
+         "hb": 528, "tsb": 256, "ab": 512, "ub": 512, "one": 528, "eb": 528, "zo": 512, "xy": 1024}
+PACKS = {"e": 512, "u": 128, "p": 128, "v": 128, "w": 512, "x": 256, "y": 256, "o": 256, "f": 384, "l": 320}
 SCRATCH = {
     "lf": ("sbuf", [128, 12288], "float32"), "li": ("sbuf", [128, 128], "int32"), "lu": ("sbuf", [128, 1280], "uint16"),
     "kin": ("sbuf", [128, 16], "int32"), "yb": ("sbuf", [128, 256], "float32"), "ps": ("psum", [128, 4096], "float32"),
-    "sm": ("sbuf", [128, 512], "float32"),
+    "sm": ("sbuf", [128, 512], "float32"), "lp": ("sbuf", [128, 8], "uint16"), "ll": ("sbuf", [128, 16], "uint16"),
 }
 SCRATCH.update({k: ("sbuf", [128, n], "bfloat16") for k, n in TILES.items()})
 SCRATCH.update({"q" + k: ("sbuf", [128, n], C4) for k, n in PACKS.items()})
 SCRATCH.update({"s" + k: ("sbuf", [128, n], "uint8") for k, n in PACKS.items()})
-SEMAPHORES = ["sV", "sS", "sP", "sG", "sent", "arr0", "arr1", "arr2", "dka", "dkb", "dxh", "dxl", "du", "dv", "dwc", "dws",
-              "dkid", "doc", "dos0", "dos1", "dos2", "dos3", "dy0", "dy1",
-              "dz0", "dz1", "dz2", "dz3", "dzs0", "dzs1", "dzs2", "dzs3"]
+SEMAPHORES = ["sV", "sS", "sP", "sG", "sent", "arr0", "arr1", "arr2", "arrx", "arrp", "dka", "dkb", "dxh", "dxl", "du", "dv", "dwc", "dws",
+              "dkid", "doc", "dos0", "dos1", "dos2", "dos3", "dy0", "dy1"]
 A = AluOpType
 AF = ActivationFunctionType
-LAND = [128, 320, 480]
+LAND = [64, 192, 48]
 CY, GA, SC, LAT, FAR = 0.9, 1.56, 3.8, 180.0, 3500.0
+FARX, FARL, EARLY = 5500.0, 2800.0, 38000.0
+NV = [2] * 8
 TWO = tuple(TILES) + ("lu",)
 PLAN = {}
-TRIES = 4500
+TRIES = 7000
 
 
 def place(ops, prio, links, pen, back):
@@ -36,7 +38,7 @@ def place(ops, prio, links, pen, back):
             k -= 1
         i = todo.pop(k)
         o = ops[i]
-        ready = o["tail"] if back else 0.0
+        ready = o["late"] if back else 0.0
         for d, w in links[i]:
             if got[d][2] + w > ready:
                 ready = got[d][2] + w
@@ -55,7 +57,7 @@ def place(ops, prio, links, pen, back):
         key, e, k, s, c, j = best
         busy[e].insert(j, (s, s + c))
         got[i] = (k, s, s + c)
-        last = max(last, s + c + (0.0 if back else o["tail"]))
+        last = max(last, s + c + (0.0 if back else o["late"]))
     return last, got
 
 
@@ -67,7 +69,7 @@ def plan(ops):
     post = [[] for o in ops]
     level = [0.0] * n
     for i in range(n - 1, -1, -1):
-        level[i] += min(x[1] for x in ops[i]["alts"]) + ops[i]["tail"] + LAT
+        level[i] = max(level[i] + ops[i]["tail"], ops[i]["late"]) + min(x[1] for x in ops[i]["alts"]) + LAT
         for d, w in pre[i]:
             post[d].append((i, w))
             level[d] = max(level[d], level[i])
@@ -89,7 +91,7 @@ def plan(ops):
         cur = min(cur, both(cur[2] if k else [-b[1] for b in cur[1]], cur[3]), key=lambda x: x[0])
     best = cur
     for k in range(TRIES):
-        mid, wide, amp = rnd() * cur[0], 500 + 4000 * rnd(), 1500 * rnd() ** 2
+        mid, wide, amp = rnd() ** 1.5 * cur[0], 500 + 4000 * rnd() ** 2, 1500 * rnd() ** 2
         prio, pen = [-b[1] for b in cur[1]], list(cur[3])
         for i in range(n):
             if abs(cur[1][i][1] - mid) < wide:
@@ -97,7 +99,7 @@ def plan(ops):
                 if rnd() < 0.15:
                     pen[i] = 1200 * rnd() ** 2 - 200
         new = both(prio, pen)
-        if new[0] < cur[0] + 60 * (1 - k / TRIES):
+        if new[0] < cur[0] + 120 * (1 - k / TRIES):
             cur = new
             if new[0] < best[0]:
                 best = new
@@ -135,7 +137,7 @@ def rank_program(g, core, T, topo):
     def col(v, j): return sub(v, j, j + 1)
     def src(v, ind): return ap(v).indirect(ap(ind)) if ind else ap(v)
 
-    def do(alts, wr, rd, sem=None, inc=1, tail=0.0, chain=False, after=()):
+    def do(alts, wr, rd, sem=None, inc=1, tail=0.0, chain=False, after=(), late=0.0):
         deps = {d: True for d in after}
         spans = []
         for v, w in [(v, True) for v in wr] + [(v, False) for v in rd]:
@@ -143,12 +145,13 @@ def rank_program(g, core, T, topo):
             ps = v[0] == "ps"
             if ps:
                 lo, hi, step = lo // 512 * 512, (hi + 511) // 512 * 512, 1
-            spans.append((v[0], lo, hi, step, w or ps))
+            spans.append((v[0], lo, hi, step, w))
             for (l2, h2, s2, w2, d) in log.get(v[0], []):
-                if l2 < hi and lo < h2 and (w or ps or w2) and (lo - l2) % math.gcd(step, s2) == 0:
+                apart = ps and not (len(alts) == 1 == len(ops[d]["alts"]) and alts[0][0] == ops[d]["alts"][0][0])
+                if l2 < hi and lo < h2 and (w or w2 or apart) and (lo - l2) % math.gcd(step, s2) == 0:
                     deps[d] = deps.get(d, False) or not (chain and ps)
         me = len(ops)
-        ops.append({"alts": alts, "deps": deps, "sem": sem, "inc": inc, "tail": tail})
+        ops.append({"alts": alts, "deps": deps, "sem": sem, "inc": inc, "tail": tail, "late": max(tail, late)})
         for (name, lo, hi, step, w) in spans:
             old = log.get(name, [])
             if w:
@@ -238,6 +241,24 @@ def rank_program(g, core, T, topo):
     def dma(e, sem, out, in_, wr, rd, tail, after=()):
         return do([(x, 200.0, lambda x=x: Q[x].dma_start(out, in_)) for x in e], wr, rd, sem=sem, inc=16, tail=tail, after=after)
 
+    def send(sem, d, pairs, tail, fused=False, late=0.0):
+        def side(v): return ap(v).bitcast(dt.uint8) if v[0][0] == "q" else ap(v)
+
+        def call():
+            rid, pid = topo.addr(d, core)
+            es = topo.engines(core, d)
+            if fused:
+                g.remote_dma_fused([RemoteDMATransfer(dst_ids=[DstId(rid=rid, pnc=pid)], remote_sem=T.sem[sem], src=side(i), dst=side(o),
+                                                      dma_engine_mask=sum(1 << e for e in es[k::len(pairs)]))
+                                    for k, (o, i) in enumerate(pairs)], local_sem=T.sem.sent)
+                return len(es)
+            for o, i in pairs:
+                g.remote_dma(side(o), side(i), T.sem[sem], T.sem.sent, pid, rid, topo.mask(core, d))
+            return len(pairs) * len(es)
+
+        do([("G", 200.0, call)], [o for o, i in pairs], [i for o, i in pairs], sem=sem,
+           inc=(1 if fused else len(pairs)) * len(topo.engines(d, core)), tail=tail, late=late)
+
     kin = W("kin", 0, 16)
     dma("Y", "dka", T.kin[:, 0:8], T.ka[:], [sub(kin, 0, 8)], [], 1600.0)
     dma("S", "dkb", T.kin[:, 8:16], T.kb[:], [sub(kin, 8, 16)], [], 1600.0)
@@ -249,32 +270,26 @@ def rank_program(g, core, T, topo):
     dma("Y", "dv", T.vin[:], T.v[:], [W("vin", 0, 512)], [], 3000.0, (dx,))
 
     pi = iota(I(1), [[0, 1]], 0, 1)
-    one = fill(W("one", 0, 528), 1, "V")
+    one = fill(W("one", 0, 528), 1)
     SG = B(528)
-    io1 = scan(sub(SG, 257, 513), sub(one, 0, 256), sub(one, 0, 256))
+    io = iota(sub(SG, 256, 528), [[1, 272]], 0)
+    io1 = sub(io, 1, 257)
     lin(sub(SG, 0, 256), io1, 1.0, -257.0)
-    fill(col(SG, 256), 0)
-    fill(sub(SG, 513, 528), 0)
-    io = sub(SG, 256, 528)
     leafy = B(256)
     fill(sub(leafy, 0, 256, 129), 0)
     fill(sub(leafy, 1, 129), 1)
     fill(sub(leafy, 130, 256), 0)
-    PT = B(256)
-    for h in range(2):
-        lin(part(PT, h, 128), sub(io1, 0, 128))
+    PT = iota(B(256), [[0, 2], [1, 128]], 1)
     UT = lin(B(256), PT, 1.0, 128.0)
     Z128 = iota(B(256), [[0, 128], [128, 2]], 0)
-    Z1 = iota(B(128), [[0, 64], [1, 2]], 0)
+    Z1 = W("zo", 0, 512)
+    fill(even(Z1), 0)
+    fill(odd(Z1), 1)
     eb = W("eb", 0, 528)
     do([("G", 170 + 2 * CY * 528, lambda: g.affine_select(ap(eb), ap(one), [[-1, 528]], A.is_equal, 0.0, 3, 4))], [eb], [one])
     crf = F(20)
     iota(crf, [[16, 4], [16, 5]], 0)
-    quant("z", 0, 128, fill(W("zt", 0, 512), 0))
-    for k, z in enumerate((0, 192, 352, 496)):
-        dma("Y", "dz%d" % k, T.ql[:, z:z + 128].bitcast(dt.uint8), T.qz[:].bitcast(dt.uint8),
-            [W("ql", z, z + 128)], [W("qz", 0, 128)], 2200.0, (dx,))
-        dma("Y", "dzs%d" % k, T.sl[:, z:z + 128], T.sz[:], [W("sl", z, z + 128)], [W("sz", 0, 128)], 2200.0, (dx,))
+    fill(W("ft", 256, 512), 0)
     for b in range(4):
         quant("e", 128 * b, 128 * b + 128, W("eb", 3 - b, 515 - b))
     ri = I(3)
@@ -304,7 +319,7 @@ def rank_program(g, core, T, topo):
     own = F(16)
     for h in range(2):
         lin(part(own, h, 8), sub(io, 0, 8), 16.0, r)
-    self1 = lin(F(16), own, 1.0, 257.0)
+    self1 = lin(F(8), sub(own, 0, 8), 1.0, 256.0)
     cU = lin(U(8), sub(io, 0, 8), 16.0)
 
     def wrapscan(v, per=16, o=None):
@@ -326,30 +341,31 @@ def rank_program(g, core, T, topo):
     put(sub(PS, 0, 256), ksc, io1)
     s = wrapscan(sub(PS, 1, 257))
     WPS, WP2 = lin(U(16), s, inv16, -1.0), lin(U(16), s, inv2, -1.0)
-    X = F(24)
-    lin(sub(X, 0, 16), kin, 1.0, 1.0)
-    lin(sub(X, 16, 24), sub(kin, 0, 8), 1.0, 1.0)
-    pen = ts(F(24), X, 128.0, A.is_le, 512.0, A.mult)
-    X2 = tt(F(24), X, pen, A.add)
-    L, L2 = F(32), F(16)
-    m128 = tt(sub(L, 16, 32), sub(X2, 8, 24), self1, A.min)
-    in2 = tt(F(16), m128, lin(F(16), sub(pen, 0, 16), -1.0, 512.0), A.add)
-    tt(sub(L, 8, 16), sub(X2, 0, 8), sub(in2, 0, 8), A.min)
-    tt(sub(L, 0, 8), sub(X2, 8, 16), sub(in2, 8, 16), A.min)
-    tt(sub(L2, 0, 8), sub(L, 0, 8), sub(L, 8, 16), A.subtract)
-    tt(sub(L2, 8, 16), sub(L, 24, 32), sub(L, 16, 24), A.subtract)
-    WL = lin(U(24), sub(L, 8, 32), 1.0, 128.0)
-    WL2 = lin(U(16), L2, 1.0, 256.0)
-    WL3 = lin(U(16), tt(F(16), sub(pen, 8, 24), sub(pen, 0, 16), A.subtract), 1.0 / 512, 256.0)
-    DR, DU, DW, MS = B(512), B(256), B(512), B(256)
+    send("arrp", T.cores[rank ^ 1], [(W("lp", 0, 8), sub(WPS, 0, 8))], FAR)
+    pen = ts(F(16), kin, 127.0, A.is_le, 512.0, A.mult)
+    bump = ts(F(16), kin, 127.0, A.is_gt, 512.0, A.mult)
+    X2 = tt(F(16), kin, pen, A.add)
+    M, V, L2, L3 = F(16), F(16), F(16), F(8)
     for h in range(2):
-        lin(part(MS, h, 128), SG, ind=sub(WL, 8 + 8 * h, 16 + 8 * h))
-        lin(odd(part(DR, h, 256)), SG, ind=part(WL, h, 8))
+        tt(part(M, h, 8), part(X2, 1 - h, 8), sub(self1, 0, 8), A.min)
+    tt(V, X2, tt(F(16), M, bump, A.add), A.min)
+    tt(sub(L2, 0, 8), sub(V, 8, 16), sub(V, 0, 8), A.subtract)
+    tt(sub(L2, 8, 16), sub(M, 8, 16), sub(M, 0, 8), A.subtract)
+    tt(L3, sub(pen, 8, 16), sub(pen, 0, 8), A.subtract)
+    WM, WV, WL2 = lin(U(16), M, 1.0, 129.0), lin(U(8), sub(V, 0, 8), 1.0, 129.0), lin(U(16), L2, 1.0, 256.0)
+    WL3 = lin(U(8), L3, 1.0 / 512, 256.0)
+    DR, DW, MS = B(512), B(512), B(256)
+    UP, DU = fill(B(256), 0), B(256)
+    for h in range(2):
+        lin(part(MS, h, 128), SG, ind=part(WM, h, 8))
         lin(even(part(DR, h, 256)), SG, ind=part(WL2, h, 8))
         lin(odd(part(DW, h, 256)), leafy, ind=part(ksc, h, 8))
-        lin(even(part(DW, h, 256)), SG, ind=part(WL3, h, 8))
+    lin(odd(part(DR, 0, 256)), SG, ind=WV)
+    lin(odd(part(DR, 1, 256)), part(MS, 0, 128))
+    lin(even(part(DW, 0, 256)), SG, ind=WL3)
+    lin(even(part(DW, 1, 256)), even(part(DW, 0, 256)), -1.0)
     lin(odd(DU), MS, ind=sub(WPS, 8, 16))
-    tt(even(DU), UT, odd(DU), A.subtract, ind=sub(WPS, 8, 16))
+    lin(odd(UP), UT, ind=sub(WPS, 8, 16))
     quant("u", 0, 128, W("uin", 0, 512))
     do([("V", 250.0, lambda: g.vector.tensor_copy(T.qp[:, 0:128].bitcast(dt.uint32),
                                                   T.qu[:, 0:128].bitcast(dt.uint32).indirect(ap(cU))))],
@@ -358,24 +374,28 @@ def rank_program(g, core, T, topo):
     PP = W("ps", 2048, 2176)
     xs = W("xs", 0, 1024)
 
-    def scores(x):
-        quant("x", 128, 256, W(x, 512, 1024))
-        mm(PP, "p", 0, "x", 128)
-        quant("x", 0, 128, W(x, 0, 512))
+    def scores(x, q):
+        quant(q, 128, 256, W(x, 512, 1024))
+        mm(PP, "p", 0, q, 128)
+        quant(q, 0, 128, W(x, 0, 512))
         for b in range(4):
-            mm(W("ps", 512 * b, 512 * b + 256), "e", 128 * b, "x", 0)
+            mm(W("ps", 512 * b, 512 * b + 256), "e", 128 * b, q, 0)
         for b in range(4):
             lin(W("xs", b, 1024, 4), W("ps", 512 * b, 512 * b + 256))
 
-    scores("xin")
-    T2, IR = fill(B(512), 0), fill(B(256), 0)
+    scores("xin", "o")
+    send("arrx", T.cores[rank ^ 1], [(W("qy", 0, 256), W("qo", 0, 256)), (W("sy", 0, 256), W("so", 0, 256))], FARX, late=EARLY)
+    for b in range(4):
+        mm(W("ps", 512 * b, 512 * b + 256), "e", 128 * b, "y", 0)
+        lin(W("xy", b, 1024, 4), W("ps", 512 * b, 512 * b + 256))
+    T2 = fill(B(512), 0)
     ts(sub(T2, 1, 254, 2), sub(PP, 0, 127), 0.0, A.is_gt)
     ts(sub(T2, 257, 510, 2), sub(PP, 0, 127), 0.0, A.is_le)
     TD = sub(T2, 0, 256)
-    lin(odd(IR), T2, ind=sub(WP2, 8, 16))
+    lin(even(DU), T2, 256.0, ind=sub(WP2, 8, 16))
     R, val, EE = B(512), B(512), B(512)
     scan(sub(R, 0, 256), TD, sub(DR, 0, 256))
-    scan(sub(R, 256, 512), IR, DU)
+    scan(sub(R, 256, 512), UP, DU, A.min, A.max)
     Wc, w0 = U(16), B(256)
     for h in range(2):
         lin(part(Wc, h, 8), wrapscan(odd(part(R, h, 256))), inv2, -1.0)
@@ -384,22 +404,27 @@ def rank_program(g, core, T, topo):
     for i in range(8):
         mine, v2 = w0 if i == 0 else B(256), B(256)
         for h in range(2):
-            if i:
+            if 0 < i < 7:
                 lin(part(mine, h, 128), part(val, h, 128))
-        for h in range(2):
-            tt(part(v2, h, 128), val, part(mine, h, 128), A.add, ind=part(Wc, h, 8))
+        if i == 7:
+            far = B(256)
+            for h in range(2):
+                lin(part(far, h, 128), val, ind=part(Wc, h, 8))
+            mine, val = val, far
+        for h in range(NV[i]):
+            tt(part(v2, h, 256 // NV[i]), val, part(mine, h, 256 // NV[i]), A.add, ind=part(Wc, h, 16 // NV[i]))
         val = v2
-        if i < 7:
+        if i < 6:
             R2, W2 = B(256), U(16)
             for h in range(2):
                 lin(part(R2, h, 128), R, ind=part(Wc, h, 8), only="S")
                 wrap(part(R2, h, 128), o=part(W2, h, 8))
             R, Wc = R2, W2
     BI = B(272)
-    fill(sub(BI, 0, 16), 1)
     lin(sub(BI, 16, 144), io, 1.0, 1.0, ind=sub(ksc, 8, 16))
     lin(sub(BI, 144, 272), io, 1.0, 1.0, ind=sub(ksc, 0, 8))
-    LT = fill(B(512), 0)
+    LT = B(512)
+    fill(sub(LT, 1, 512, 4), 0)
     lin(sub(LT, 0, 512, 4), T2, ind=sub(WP2, 0, 8))
     lin(sub(LT, 2, 512, 4), PT, ind=sub(WPS, 0, 8))
     lin(sub(LT, 3, 512, 4), sub(BI, 16, 272), 1.0, -1.0, ind=sub(WPS, 0, 8))
@@ -407,17 +432,20 @@ def rank_program(g, core, T, topo):
     scan(sub(EE, 256, 512), TD, sub(DR, 256, 512))
     WE = wrap(odd(EE))
     Wn = lin(U(8), wrapscan(lin(B(128), val, ind=sub(WE, 0, 8))), invm, 128.0)
-    fill(W("ft", 0, 512), 0)
-    W4 = wrap4(sub(LT, 2, 512, 4))
-    for h in range(2):
-        tt(W("sm", 256 * h, 256 * h + 256), sub(xs, 512, 1024), part(xs, h, 256), A.add, ind=part(W4, h, 16))
-    REP = lin(B(272), io)
+    W4 = wrap4(lin(B(128), PT, ind=W("lp", 0, 8)))
+    for h in range(4):
+        tt(W("sm", 128 * h, 128 * h + 128), W("xy", 512, 1024), W("xy", 128 * h, 128 * h + 128), A.add, ind=part(W4, h, 8))
+    REP = iota(B(272), [[1, 272]], 0)
     RK, MR = fill(F(128), 0), fill(F(816), 0)
-    t01 = fill(B(128), 1)
+    t01, TB = B(128), B(256)
+    fill(col(t01, 127), 1)
+    fill(col(TB, 127), 0)
     fill(W("xs", 1024, 1280), 0)
     fill(W("hb", 0, 272), 0)
     kc = iota(F(64), [[1, 64]], 257)
-    r416 = lin(F(1), r4, 1.0, 272.0)
+    h14 = lin(F(1), r3, 64.0, 14.0)
+    HC = lin(U(16), sub(io, 0, 16), 4.0, lin(F(1), r3, 64.0, lin(F(1), r4, 1.0, 272.0)))
+    hb = W("hb", 0, 528)
     TO = odd(TD)
     WB = [sub(ksc, 8, 16), sub(ksc, 0, 8)]
 
@@ -427,23 +455,19 @@ def rank_program(g, core, T, topo):
         OL = B(m)
         put(OL, Wn, sub(io1, 0, m))
         Wl = wrap4(sub(OL, 1, 2 * K, 2))
-        for h in range(2):
-            lin(W("ft", 2 * K * h, 2 * K * h + 2 * K), W("sm", 0, 4 * m), 0.5, ind=part(Wl, h, K // 8))
-        quant("f", 128 * t, 128 * t + 128, W("ft", 0, 512))
         d = T.cores[rank ^ (1 << t)]
         a = LAND[t]
-
-        def send(d=d, a=a, t=t, K=K):
-            rid, pid = topo.addr(d, core)
-            arr, mask = T.sem["arr%d" % t], topo.mask(core, d)
-            g.remote_dma(T.ql[:, a:a + K].bitcast(dt.uint8), T.qf[:, 128 * t:128 * t + K].bitcast(dt.uint8), arr, T.sem.sent,
-                         pid, rid, mask)
-            g.remote_dma(T.sl[:, a:a + K], T.sf[:, 128 * t:128 * t + K], arr, T.sem.sent, pid, rid, mask)
-            return 2 * len(topo.engines(core, d))
-
-        do([("G", 200.0, send)], [W("ql", a, a + K), W("sl", a, a + K)],
-           [W("qf", 128 * t, 128 * t + 128), W("sf", 128 * t, 128 * t + 128)],
-           sem="arr%d" % t, inc=2 * len(topo.engines(d, core)), tail=FAR)
+        if t == 0:
+            send("arr0", d, [(W("ll", 0, 16), Wl)], FARL)
+        for h in range(2):
+            lin(W("ft", 2 * K * h, 2 * K * h + 2 * K), W("sm", 0, 4 * m), 0.5, ind=part(Wl if t else W("ll", 0, 16), h, K // 8))
+        if t == 0:
+            quant("l", a, a + 128, W("ft", 0, 512))
+        else:
+            quant("f", 128 * t, 128 * t + 128, W("ft", 0, 512))
+            z = 3 * K * (t - 1)
+            send("arr%d" % t, d, [(W("ql", a, a + K), W("qf", 128 * t, 128 * t + K)),
+                                  (W("sl", a - z, a - z + 4 * K), W("sf", 128 * t - z, 128 * t - z + 4 * K))], FAR, True)
 
         KT = lin(B(4 * K), LT, ind=Wl)
         pk, s1 = sub(KT, 2, 4 * K, 4), sub(KT, 3, 4 * K, 4)
@@ -462,28 +486,22 @@ def rank_program(g, core, T, topo):
         scan(part(SP, 0, 2 * K), rk, odd(KT), A.mult, A.max)
         s = wrapscan(odd(SP), 4)
         XO = lin(U(K // 4), part(s, 0, K // 4), inv44, r3m)
-        HO = lin(U(K // 4), part(s, 1, K // 4), inv4, lin(F(1), r3, float(K), 14.0))
-        HC = lin(U(K // 4), sub(io, 0, K // 4), 4.0, lin(F(1), r3, float(K), r416))
+        HO = lin(U(K // 4), part(s, 1, K // 4), inv4, h14)
         Ts = lin(W("tsb", 0, 4 * K), W("xs", 0, 1280), ind=XO)
         put(sub(REP, 128, 272), Wp, lin(B(K), REP, ind=Ws))
         BI = B(272)
-        fill(sub(BI, 0, 16), 1)
+        if t == 2:
+            fill(sub(BI, 0, 16), 1)
         for h in range(2):
             lin(sub(BI, 16 + 128 * h, 144 + 128 * h), REP, 1.0, 1.0, ind=WB[h])
-        n = 2 if t == 0 else 4
+        z = 128 - K if t == 1 else 0
         for b in range(4):
-            j = b % n
-            bank = 2560 + 512 * (b // n)
-            mm(W("ps", bank, bank + 128), "w", 128 * b, "l", a - K * j, j == 0, j == n - 1)
-        hb = W("hb", 0, 272 + 4 * K)
-        if t == 0:
-            relu(W("hb", 272, 400), W("ps", 2560, 2688))
-            relu(W("hb", 400, 528), W("ps", 3072, 3200))
-        else:
-            relu(W("hb", 272, 272 + 4 * K), W("ps", 2560, 2560 + 4 * K))
-        ab = tt(W("ab", 0, 4 * K), hb, Ts, A.add, ind=HC)
-        ub = tt(W("ub", 0, 4 * K), hb, ab, A.add, ind=HO)
-        put(W("xs", 0, 1280), XO, ub)
+            mm(W("ps", 2048 + 512 * b, 2176 + 512 * b), "w", 128 * b, "l", a - z)
+            relu(sub(hb, 272 + 64 * b, 272 + 64 * b + K), W("ps", 2048 + 512 * b + z, 2048 + 512 * b + z + K))
+        ab = W("ab", 0, 8 * K)
+        tt(odd(ab), hb, Ts, A.add, ind=sub(HC, 0, K // 4))
+        lin(even(ab), hb, ind=HO)
+        put(W("xs", 0, 1280), XO, odd(scan(W("ub", 0, 8 * K), W("zo", 0, 8 * K), ab)))
         if t == 2:
             break
         wb = wrap(sub(BI, 16, 272))
@@ -495,7 +513,8 @@ def rank_program(g, core, T, topo):
             INV = B(144)
             put(INV, lin(U(8), mid, invm, 129.0), sub(io1, 0, 128))
             f1 = scan(B(126), sub(Z1, 0, 126), sub(INV, 1, 127))
-            GID = fill(B(64), 128)
+            GID = B(64)
+            fill(col(GID, 0), 128)
             tt(sub(GID, 1, 64), odd(f1), sub(pk, 0, 63), A.subtract)
             s, WG = wrapscan(GID), U(20)
             W1 = lin(sub(WG, 0, 4), s, inv16, -1.0)
@@ -517,12 +536,13 @@ def rank_program(g, core, T, topo):
             bd = B(128)
             lin(sub(bd, 0, 64), sub(lh, 0, 64), 1.0, -127.0)
             lin(sub(bd, 64, 128), sub(lh, 64, 128), -1.0, 192.0)
-            Mk = tt(B(320), bd, KK, A.is_lt, ind=WR)
-            uv = B(128)
+            MZ, UZ = B(640), B(640)
+            fill(even(MZ), 0)
+            fill(odd(UZ), 0)
+            Mk = tt(odd(MZ), bd, KK, A.is_lt, ind=WR)
+            uv, bs = B(128), icol
             tt(sub(uv, 0, 64), sub(lh, 64, 128), sub(io, 128, 192), A.subtract)
             tt(sub(uv, 64, 128), sub(lh, 0, 64), sub(io, 128, 192), A.subtract)
-            C = tt(B(320), uv, Mk, A.mult, ind=WR)
-            lin(sub(C, 64, 320, 64), icol)
             RS = fill(B(320), 1)
             fill(sub(RS, 0, 320, 80), 0)
             EV = iota(B(64), [[0, 32], [-1, 2]], 1)
@@ -534,26 +554,27 @@ def rank_program(g, core, T, topo):
             al = lin(B(64), EV, ind=Wn)
             fill(col(CUM, 0), 0)
             scan(sub(CUM, 1, 65), sub(one, 0, 64), al)
-            cum = lin(B(64), sub(CUM, 0, 64))
-            tsl = lin(B(64), t01, -2.0, 1.0, ind=W1)
-            nn, uv = B(128), B(128)
-            tt(sub(nn, 64, 128), sub(CUM, 0, 65), cum, A.subtract, ind=sub(WLH, 0, 4))
-            tt(sub(nn, 0, 64), sub(CUM, 0, 65), cum, A.subtract, ind=sub(WLH, 4, 8))
+            n0, n1, n2 = B(384), B(384), B(384)
+            iota(n0, [[0, 128], [1, 3]], 0)
+            fill(sub(n1, 2, 384, 3), 0)
             for h in range(2):
-                tt(part(uv, h, 64), part(nn, h, 64), tsl, A.mult)
+                lin(sub(part(n0, h, 192), 2, 192, 3), t01, -2.0, 1.0, ind=W1)
+                lin(sub(part(n1, h, 192), 0, 192, 3), sub(CUM, 0, 65), ind=part(WLH, 1 - h, 4))
+                lin(sub(part(n1, h, 192), 1, 192, 3), sub(CUM, 0, 64), -1.0)
+            uv = lin(B(128), sub(scan(n2, n0, n1), 2, 384, 3))
             hh = lin(B(4), posw, 0.5, 129.75)
             alw = tt(F(4), lin(F(4), hh, 2.0, -259.0), posw, A.subtract)
             bs = tt(F(4), lin(F(4), hh, -63.0, 8190.0), lin(F(4), posw, 32.0), A.add)
-            M2 = B(320)
             for c in range(4):
-                lin(part(M2, c, 80), part(Mk, c, 80), col(alw, c))
-            C = tt(B(320), uv, M2, A.mult, ind=WR)
-            lin(sub(C, 64, 320, 64), bs)
+                lin(part(Mk, c, 80), part(Mk, c, 80), col(alw, c))
+        lin(even(UZ), uv, ind=WR)
+        C = odd(scan(B(640), MZ, UZ))
+        lin(sub(C, 64, 320, 64), bs)
         Wsl = wrap(lin(B(64), PS, ind=WLID))
-        LT = fill(B(256), 0)
+        LT = sub(LT, 0, 256)
         lin(sub(LT, 2, 256, 4), PT, ind=Wsl)
         lin(sub(LT, 3, 256, 4), sub(BI, 16, 272), 1.0, -1.0, ind=Wsl)
-        scores("xs")
+        scores("xs", "x")
         W4 = wrap4(sub(LT, 2, 256, 4))
         for h in range(2):
             g1 = lin(W("g1", 128 * h, 128 * h + 128), xs, ind=part(W4L, h, 8))
@@ -562,7 +583,6 @@ def rank_program(g, core, T, topo):
         pr = tt(B(320), t01, C, A.mult, ind=WG)
         posw = sub(scan(B(320), RS, pr), 79, 320, 80)
         Wn = lin(U(4), posw)
-        TB = fill(B(256), 0)
         tt(sub(TB, 0, 127), sub(t01, 0, 127), sub(TO, 0, 127), A.not_equal)
         TO = sub(TB, 0, 128)
         lin(sub(TB, 128, 256), TO, -1.0, 1.0)
@@ -584,7 +604,7 @@ def rank_program(g, core, T, topo):
     lin(sub(TE, 0, 128), TO, -1.0, 2.0)
     lin(sub(TE, 128, 256), TO, 1.0, 1.0)
     slot = tt(F(16), lin(F(16), wrapscan(TE), inv128, -112.0), own, A.add)
-    stay = tt(F(8), wrap(sub(REP, 129, 257), o=F(8), add=128.0), sub(self1, 0, 8), A.is_equal)
+    stay = tt(F(8), wrap(sub(REP, 129, 257), o=F(8), add=127.0), self1, A.is_equal)
     off = F(16)
     for h in range(2):
         tt(part(off, h, 8), part(slot, h, 8), stay, A.mult)

@@ -19,12 +19,13 @@ SEMAPHORES = ["sV", "sS", "sP", "sG", "sent", "arr0", "arr1", "arr2", "arrx", "a
 A = AluOpType
 AF = ActivationFunctionType
 LAND = [64, 192, 48]
-CY, GA, SC, LAT, FAR = 0.9, 1.56, 3.8, 180.0, 3500.0
-FARX, FARL, EARLY = 5500.0, 2800.0, 38000.0
+CY, GA, SC, LAT, FAR = 0.9, 1.56, 3.8, 225.0, 2700.0
+FARX, FARL, EARLY = 5000.0, 2200.0, 39000.0
 NV = [2] * 8
+DS = 400.0
 TWO = tuple(TILES) + ("lu",)
 PLAN = {}
-TRIES = 7000
+TRIES = 4500
 
 
 def place(ops, prio, links, pen, back):
@@ -239,7 +240,7 @@ def rank_program(g, core, T, topo):
            [o], [lc, ls, rc, rs], chain=not start)
 
     def dma(e, sem, out, in_, wr, rd, tail, after=()):
-        return do([(x, 200.0, lambda x=x: Q[x].dma_start(out, in_)) for x in e], wr, rd, sem=sem, inc=16, tail=tail, after=after)
+        return do([(x, 200.0, lambda x=x: Q[x].dma_start(out, in_)) for x in e], wr, rd, sem=sem, inc=16, tail=tail - DS, after=after)
 
     def send(sem, d, pairs, tail, fused=False, late=0.0):
         def side(v): return ap(v).bitcast(dt.uint8) if v[0][0] == "q" else ap(v)

@@ -3,8 +3,8 @@ from concourse.bass import DstId, RemoteDMATransfer
 from concourse.mybir import dt, AluOpType, ActivationFunctionType
 
 C4 = "float8_e4m3fn_x4"
-TILES = {"lb": 28672, "xin": 1024, "uin": 512, "vin": 512, "xs": 1280, "g1": 256, "ft": 512,
-         "hb": 528, "tsb": 256, "ab": 512, "ub": 512, "one": 528, "eb": 528, "zo": 512, "xy": 1024}
+TILES = {"lb": 32768, "xin": 1024, "uin": 512, "vin": 512, "xs": 1280, "g1": 256, "ft": 512,
+         "hb": 528, "tsb": 256, "ab": 512, "ub": 512, "one": 528, "eb": 528, "zo": 512, "xy": 512, "xz": 1024, "sz": 1024}
 PACKS = {"e": 512, "u": 128, "p": 128, "v": 128, "w": 512, "x": 256, "y": 256, "o": 256, "f": 384, "l": 320}
 SCRATCH = {
     "lf": ("sbuf", [128, 12288], "float32"), "li": ("sbuf", [128, 128], "int32"), "lu": ("sbuf", [128, 1280], "uint16"),
@@ -19,25 +19,29 @@ SEMAPHORES = ["sV", "sS", "sP", "sG", "sent", "arr0", "arr1", "arr2", "arrx", "a
 A = AluOpType
 AF = ActivationFunctionType
 LAND = [64, 192, 48]
-CY, GA, SC, LAT, FAR = 0.9, 1.56, 3.8, 225.0, 2700.0
-FARX, FARL, EARLY = 5000.0, 2200.0, 39000.0
-NV = [2] * 8
-DS = 400.0
+FIGS = [(0.5, 215.0, 0.87, 1.56, 3.8, 1800.0, 1400.0, 6500.0, 1000.0, 36500.0, 200.0),
+        (0.25, 270.0, 1.1, 1.8, 4.8, 2600.0, 2100.0, 9500.0, 1300.0, 0.0, 600.0),
+        (0.25, 170.0, 0.9, 1.25, 2.4, 2300.0, 1800.0, 8000.0, 900.0, 0.0, 400.0)]
 TWO = tuple(TILES) + ("lu",)
-PLAN = {}
-TRIES = 4500
+PLAN = []
+TRIES, MOVES, SEED = 2500, (20000, 25000), 777
 
 
-def place(ops, prio, links, pen, back):
+def place(ops, prio, links, mirror, pen, back):
     busy = {e: [] for e in "VSPGY"}
     got = [None] * len(ops)
     last = 0.0
-    todo = sorted(range(len(ops)), key=lambda j: prio[j])
+    lack = [len(x) for x in links]
+    todo = sorted((prio[j], j) for j in range(len(ops)) if not lack[j])
     while todo:
-        k = len(todo) - 1
-        while any(got[d] is None for d, w in links[todo[k]]):
-            k -= 1
-        i = todo.pop(k)
+        i = todo.pop()[1]
+        for j, w in mirror[i]:
+            lack[j] -= 1
+            if not lack[j]:
+                x, k = (prio[j], j), len(todo)
+                while k and todo[k - 1] > x:
+                    k -= 1
+                todo.insert(k, x)
         o = ops[i]
         ready = o["late"] if back else 0.0
         for d, w in links[i]:
@@ -46,12 +50,18 @@ def place(ops, prio, links, pen, back):
         best = None
         for k, (e, c, f) in enumerate(o["alts"]):
             s, b = ready, busy[e]
-            j = len(b)
-            while j > 0 and b[j - 1][1] > s:
-                j -= 1
-            while j < len(b) and s + c > b[j][0]:
-                s = max(s, b[j][1])
-                j += 1
+            j = n = len(b)
+            if n and b[-1][1] > s:
+                lo = 0
+                while lo < j:
+                    h = (lo + j) >> 1
+                    if b[h][1] > s:
+                        j = h
+                    else:
+                        lo = h + 1
+                while j < n and s + c > b[j][0]:
+                    s = b[j][1]
+                    j += 1
             key = s + c + (pen[i] if e == "V" else 0.0)
             if best is None or key < best[0]:
                 best = (key, e, k, s, c, j)
@@ -62,11 +72,11 @@ def place(ops, prio, links, pen, back):
     return last, got
 
 
-def plan(ops):
+def plan(sets):
+    ops, LAT = sets[0], FIGS[0][1]
     n = len(ops)
-    if n in PLAN:
-        return PLAN[n]
-    pre = [[(d, ops[d]["tail"] + LAT if hard else 0.5) for d, hard in o["deps"].items()] for o in ops]
+    pres = [[[(d, x[d]["tail"] + f[1] if hard else 0.5) for d, hard in o["deps"].items()] for o in x] for x, f in zip(sets, FIGS)]
+    pre = pres[0]
     post = [[] for o in ops]
     level = [0.0] * n
     for i in range(n - 1, -1, -1):
@@ -74,17 +84,19 @@ def plan(ops):
         for d, w in pre[i]:
             post[d].append((i, w))
             level[d] = max(level[d], level[i])
-    seed = [12345]
+    seed = [SEED]
+    sends = [i for i, o in enumerate(ops) if o["sem"] in ("arr0", "arr1", "arr2")]
 
     def rnd():
         seed[0] = (seed[0] * 1103515245 + 12345) % 2147483648
         return (seed[0] >> 8) / 8388608.0
 
     def both(prio, pen):
-        end, got = place(ops, prio, pre, pen, False)
-        e2, g2 = place(ops, [got[i][2] + ops[i]["tail"] for i in range(n)], post, pen, True)
+        end, got = place(ops, prio, pre, post, pen, False)
+        e2, g2 = place(ops, [got[i][2] + ops[i]["tail"] for i in range(n)], post, pre, pen, True)
         p2 = [b[2] for b in g2]
-        e2, g2 = place(ops, p2, pre, pen, False)
+        e2, g2 = place(ops, p2, pre, post, pen, False)
+        end, e2 = end + 0.1 * sum(got[i][1] for i in sends), e2 + 0.1 * sum(g2[i][1] for i in sends)
         return (end, got, prio, pen) if end <= e2 else (e2, g2, p2, pen)
 
     cur = both(level, [150.0] * n)
@@ -92,7 +104,7 @@ def plan(ops):
         cur = min(cur, both(cur[2] if k else [-b[1] for b in cur[1]], cur[3]), key=lambda x: x[0])
     best = cur
     for k in range(TRIES):
-        mid, wide, amp = rnd() ** 1.5 * cur[0], 500 + 4000 * rnd() ** 2, 1500 * rnd() ** 2
+        mid, wide, amp = rnd() ** 1.5 * cur[0] * 0.84, 300 + 4000 * rnd() ** 2, 1200 * rnd() ** 2
         prio, pen = [-b[1] for b in cur[1]], list(cur[3])
         for i in range(n):
             if abs(cur[1][i][1] - mid) < wide:
@@ -104,15 +116,82 @@ def plan(ops):
             cur = new
             if new[0] < best[0]:
                 best = new
-    PLAN[n] = best[1]
-    return best[1]
+    data = [(p, [[(e, c) for e, c, h in o["alts"]] for o in x], [o["late"] for o in x], f[0]) for p, x, f in zip(pres, sets, FIGS)]
+    got = polish([data[0][:3] + (1.0,)], best[1], post, sends, rnd, MOVES[0], 25.0)
+    return polish(data, got, post, sends, rnd, MOVES[1], 25.0)
 
 
-def rank_program(g, core, T, topo):
-    rank = T.rank_of(core)
-    if rank is None:
-        return
-    Q = {"V": g.vector, "S": g.scalar, "P": g.tensor, "G": g, "Y": g.sync}
+def polish(data, got, post, sends, rnd, moves, heat):
+    pre, alts, n = data[0][0], data[0][1], len(got)
+    order, pick = sorted(range(n), key=lambda i: (got[i][1], i)), [x[0] for x in got]
+
+    def run(order, pick):
+        each = [one(order, pick, p, a, l) for p, a, l, w in data]
+        return sum(x[0] * d[3] for x, d in zip(each, data)), each
+
+    def one(order, pick, pre, alts, late):
+        free, prev = {e: 0.0 for e in "VSPGY"}, {e: -1 for e in "VSPGY"}
+        end, by, last, top = [0.0] * n, [-1] * n, 0.0, 0
+        for i in order:
+            e, c = alts[i][pick[i]]
+            s, b = free[e], -2 - prev[e]
+            for d, w in pre[i]:
+                if end[d] + w > s:
+                    s, b = end[d] + w, d
+            by[i], prev[e] = b, i
+            end[i] = free[e] = s = s + c
+            if s + late[i] > last:
+                last, top = s + late[i], i
+        return last + 0.2 * sum(end[i] for i in sends), end, by, top
+
+    def move(a, b, u, ahead):
+        mid, tied = order[a:b + 1], {u}
+        for j in (mid[::-1] if ahead else mid):
+            if j in tied:
+                tied.update(d for d, w in (pre if ahead else post)[j])
+        return order[:a] + [j for j in mid if (j in tied) == ahead] + [j for j in mid if (j in tied) != ahead] + order[b + 1:]
+
+    cur = run(order, pick)
+    best = (cur[0], order, pick)
+    for k in range(moves):
+        c = cur[1][int(rnd() * len(data))]
+        arcs, i = [], c[3] if rnd() < 0.6 else sends[int(rnd() * len(sends))]
+        while i >= 0:
+            b = c[2][i]
+            if b <= -2:
+                b = -2 - b
+                arcs.append((b, i))
+            i = b
+        o2, p2 = order, pick
+        if arcs and rnd() < 0.75:
+            u, v = arcs[int(rnd() * len(arcs))]
+            a, b = order.index(u), order.index(v)
+        else:
+            a = int(rnd() * n)
+            b = min(n - 1, a + int(rnd() ** 2 * 60) + 1)
+            u, v = order[a], order[b]
+        y = rnd()
+        j = u if len(alts[u]) > 1 and (len(alts[v]) == 1 or rnd() < 0.7) else v
+        if y < 0.25 and len(alts[j]) > 1:
+            p2 = list(pick)
+            p2[j] = (p2[j] + 1 + int(rnd() * (len(alts[j]) - 1))) % len(alts[j])
+        elif y < 0.6:
+            o2 = move(a, b, v, True)
+        else:
+            o2 = move(a, min(n - 1, b + int(rnd() ** 2 * 25)), u, False)
+        new = run(o2, p2)
+        if new[0] <= cur[0] - heat * (1.02 - k / moves) * math.log(rnd() + 1e-9):
+            cur, order, pick = new, o2, p2
+            if k % 7 == 0:
+                order = sorted(order, key=lambda i: new[1][0][1][i] - alts[i][pick[i]][1])
+            if new[0] < best[0]:
+                best = (new[0], order, pick)
+    end = run(best[1], best[2])[1][0][1]
+    return [(best[2][i], end[i] - alts[i][best[2][i]][1], end[i]) for i in range(n)]
+
+
+def record(g, Q, core, rank, T, topo, fig):
+    CY, GA, SC, FAR, FARL, FARX, DS, EARLY, CALL = fig[2:]
     ops = []
     log = {}
     top = {"lf": 0, "lb": 0, "li": 0, "lu": 0}
@@ -188,6 +267,8 @@ def rank_program(g, core, T, topo):
         alts = [("V", vt(o, i, ind), v)]
         if o[0] not in ("li", "lu") and i[0] not in ("li", "lu", "kin"):
             alts.append(("S", st(o, ind), s))
+            if m == 1.0 and a == 0.0 and not ind and i[0] == "lb":
+                alts.append(("G", 170 + 2 * CY * n_of(o), lambda: g.affine_select(ap(o), ap(i), [[0, n_of(o)]], A.is_equal, 0.0, 0, 0)))
         do([x for x in alts if only in (None, x[0])], [o], views(i, m, a, ind))
         return o
 
@@ -240,7 +321,7 @@ def rank_program(g, core, T, topo):
            [o], [lc, ls, rc, rs], chain=not start)
 
     def dma(e, sem, out, in_, wr, rd, tail, after=()):
-        return do([(x, 200.0, lambda x=x: Q[x].dma_start(out, in_)) for x in e], wr, rd, sem=sem, inc=16, tail=tail - DS, after=after)
+        return do([(x, 200.0, lambda x=x: Q[x].dma_start(out, in_)) for x in e], wr, rd, sem=sem, inc=16, tail=tail - 1600.0 + DS, after=after)
 
     def send(sem, d, pairs, tail, fused=False, late=0.0):
         def side(v): return ap(v).bitcast(dt.uint8) if v[0][0] == "q" else ap(v)
@@ -257,7 +338,7 @@ def rank_program(g, core, T, topo):
                 g.remote_dma(side(o), side(i), T.sem[sem], T.sem.sent, pid, rid, topo.mask(core, d))
             return len(pairs) * len(es)
 
-        do([("G", 200.0, call)], [o for o, i in pairs], [i for o, i in pairs], sem=sem,
+        do([("G", CALL * (1 if fused else len(pairs)), call)], [o for o, i in pairs], [i for o, i in pairs], sem=sem,
            inc=(1 if fused else len(pairs)) * len(topo.engines(d, core)), tail=tail, late=late)
 
     kin = W("kin", 0, 16)
@@ -336,6 +417,8 @@ def rank_program(g, core, T, topo):
     def wrap4(v):
         return lin(U(n_of(v) // 4), wrapscan(v, 4), inv44, r3m)
 
+    inv48, r37 = lin(F(1), inv4, 8.0), lin(F(1), r3, 2.0, -7.0)
+
     ksc = lin(U(16), kin, 1.0, 1.0)
     PS = B(272)
     fill(sub(PS, 256, 272), 128)
@@ -388,7 +471,8 @@ def rank_program(g, core, T, topo):
     send("arrx", T.cores[rank ^ 1], [(W("qy", 0, 256), W("qo", 0, 256)), (W("sy", 0, 256), W("so", 0, 256))], FARX, late=EARLY)
     for b in range(4):
         mm(W("ps", 512 * b, 512 * b + 256), "e", 128 * b, "y", 0)
-        lin(W("xy", b, 1024, 4), W("ps", 512 * b, 512 * b + 256))
+        lin(W("xz", 2 * b + 1, 1024, 8), W("ps", 512 * b, 512 * b + 128), 0.5)
+        lin(W("xy", b, 512, 4), W("ps", 512 * b + 128, 512 * b + 256), 0.5)
     T2 = fill(B(512), 0)
     ts(sub(T2, 1, 254, 2), sub(PP, 0, 127), 0.0, A.is_gt)
     ts(sub(T2, 257, 510, 2), sub(PP, 0, 127), 0.0, A.is_le)
@@ -411,9 +495,9 @@ def rank_program(g, core, T, topo):
             far = B(256)
             for h in range(2):
                 lin(part(far, h, 128), val, ind=part(Wc, h, 8))
-            mine, val = val, far
-        for h in range(NV[i]):
-            tt(part(v2, h, 256 // NV[i]), val, part(mine, h, 256 // NV[i]), A.add, ind=part(Wc, h, 16 // NV[i]))
+            mine, val, near = val, far, val
+        for h in range(2):
+            tt(part(v2, h, 128), val, part(mine, h, 128), A.add, ind=part(Wc, h, 8))
         val = v2
         if i < 6:
             R2, W2 = B(256), U(16)
@@ -432,16 +516,17 @@ def rank_program(g, core, T, topo):
     scan(sub(EE, 0, 256), Z128, even(LT))
     scan(sub(EE, 256, 512), TD, sub(DR, 256, 512))
     WE = wrap(odd(EE))
-    Wn = lin(U(8), wrapscan(lin(B(128), val, ind=sub(WE, 0, 8))), invm, 128.0)
+    WY = wrap(lin(B(128), R, ind=sub(WE, 0, 8)))
+    Wn = lin(U(8), wrapscan(tt(B(128), far, lin(B(128), near, ind=sub(WE, 0, 8)), A.add, ind=WY)), invm, 128.0)
     W4 = wrap4(lin(B(128), PT, ind=W("lp", 0, 8)))
     for h in range(4):
-        tt(W("sm", 128 * h, 128 * h + 128), W("xy", 512, 1024), W("xy", 128 * h, 128 * h + 128), A.add, ind=part(W4, h, 8))
+        lin(W("xz", 256 * h, 256 * h + 256, 2), W("xy", 0, 512), ind=part(W4, h, 8))
+        scan(W("sz", 256 * h, 256 * h + 256), sub(Z1, 0, 256), W("xz", 256 * h, 256 * h + 256))
     REP = iota(B(272), [[1, 272]], 0)
     RK, MR = fill(F(128), 0), fill(F(816), 0)
     t01, TB = B(128), B(256)
     fill(col(t01, 127), 1)
-    fill(col(TB, 127), 0)
-    fill(W("xs", 1024, 1280), 0)
+    fill(sub(TB, 127, 256, 128), 0)
     fill(W("hb", 0, 272), 0)
     kc = iota(F(64), [[1, 64]], 257)
     h14 = lin(F(1), r3, 64.0, 14.0)
@@ -452,16 +537,20 @@ def rank_program(g, core, T, topo):
 
     for t in range(3):
         K = 64 >> t
-        m = 128 if t == 0 else 64
+        m = 2 * K
         OL = B(m)
         put(OL, Wn, sub(io1, 0, m))
-        Wl = wrap4(sub(OL, 1, 2 * K, 2))
+        s = wrapscan(sub(OL, 1, 2 * K, 2), 4)
+        Wl = lin(U(K // 4), s, inv44, r3m)
         d = T.cores[rank ^ (1 << t)]
         a = LAND[t]
         if t == 0:
-            send("arr0", d, [(W("ll", 0, 16), Wl)], FARL)
+            send("arr0", d, [(W("ll", 0, 16), lin(U(16), s, inv48, r37))], FARL)
         for h in range(2):
-            lin(W("ft", 2 * K * h, 2 * K * h + 2 * K), W("sm", 0, 4 * m), 0.5, ind=part(Wl if t else W("ll", 0, 16), h, K // 8))
+            if t:
+                lin(W("ft", 2 * K * h, 2 * K * h + 2 * K), W("sm", 0, 4 * m), 0.5, ind=part(Wl, h, K // 8))
+            else:
+                lin(W("ft", 128 * h, 128 * h + 128), W("sz", 0, 1024), ind=W("ll", 8 * h, 8 * h + 8))
         if t == 0:
             quant("l", a, a + 128, W("ft", 0, 512))
         else:
@@ -485,10 +574,9 @@ def rank_program(g, core, T, topo):
         put(sub(REP, 128, 272), Wp, s1)
         tt(sub(KT, 1, 4 * K, 4), REP, s1, A.not_equal, ind=Ws)
         scan(part(SP, 0, 2 * K), rk, odd(KT), A.mult, A.max)
-        s = wrapscan(odd(SP), 4)
-        XO = lin(U(K // 4), part(s, 0, K // 4), inv44, r3m)
-        HO = lin(U(K // 4), part(s, 1, K // 4), inv4, h14)
-        Ts = lin(W("tsb", 0, 4 * K), W("xs", 0, 1280), ind=XO)
+        HO = lin(U(K // 4), wrapscan(odd(part(SP, 1, 2 * K)), 4), inv4, h14)
+        XO = wrap4(odd(part(SP, 0, 2 * K)))
+        Ts = lin(W("tsb", 0, 4 * K), xs, ind=wrap4(s1))
         put(sub(REP, 128, 272), Wp, lin(B(K), REP, ind=Ws))
         BI = B(272)
         if t == 2:
@@ -517,38 +605,37 @@ def rank_program(g, core, T, topo):
             GID = B(64)
             fill(col(GID, 0), 128)
             tt(sub(GID, 1, 64), odd(f1), sub(pk, 0, 63), A.subtract)
-            s, WG = wrapscan(GID), U(20)
-            W1 = lin(sub(WG, 0, 4), s, inv16, -1.0)
-            lin(sub(WG, 4, 8), s, inv16, -1.0)
-            lin(sub(WG, 8, 16), sub(WG, 0, 8))
-            lin(sub(WG, 16, 20), W1)
-            WR = lin(U(20), crf, 1.0, r)
+            s = B(64)
+            wrapscan(GID, o=s)
+            WG = lin(U(32), s, inv16, -1.0, ind=lin(U(2), sub(io, 0, 2), 0.0, lin(F(1), r3, 16.0, 15.0)))
+            W1, WG = sub(WG, 0, 4), sub(WG, 0, 20)
+            WR = lin(U(20), crf, 2.0, lin(F(1), r, 2.0, 1.0))
             lh = B(128)
             lin(sub(lh, 0, 64), sub(val, 0, 128), -0.5, 192.25, ind=W1)
             hv = tt(F(64), sub(val, 128, 256), lin(F(64), sub(w0, 128, 256), ind=W1), A.subtract, ind=W1)
             lin(sub(lh, 64, 128), hv, -0.5, 192.25)
             icol = lin(F(4), sub(io, 0, 4), 16.0, r)
-            nb, ia, ib = lin(F(4), icol, -1.0, -0.5), lin(F(4), icol, 1.0, 2.0), lin(F(4), icol, 1.0, -64.0)
-            KK = B(320)
+            ia, ib = lin(F(4), icol, 1.0, 128.5), lin(F(4), icol, -1.0, -128.5)
+            MZ, UZ = B(960), B(960)
+            fill(sub(MZ, 0, 960, 3), 0)
+            fill(sub(UZ, 2, 960, 3), 0)
+            sg, Mk = sub(MZ, 1, 960, 3), sub(MZ, 2, 960, 3)
+            ts(part(Mk, 0, 80), act(B(80), sub(io, 0, 80), AF.Abs, bias=lin(F(1), r, -1.0, -32.5)), 32.0, A.is_lt)
             for c in range(4):
-                sg = act(F(64), sub(io, 0, 64), AF.Sign, bias=col(nb, c))
-                act(sub(KK, 80 * c, 64 * c + 64), sub(sg, 16 * c, 64), AF.Relu, scale=col(ia, c))
-                act(sub(KK, 64 * c + 64, 80 * c + 80), sub(sg, 0, 16 * c + 16), AF.Relu, scale=col(ib, c))
-            bd = B(128)
-            lin(sub(bd, 0, 64), sub(lh, 0, 64), 1.0, -127.0)
-            lin(sub(bd, 64, 128), sub(lh, 64, 128), -1.0, 192.0)
-            MZ, UZ = B(640), B(640)
-            fill(even(MZ), 0)
-            fill(odd(UZ), 0)
-            Mk = tt(odd(MZ), bd, KK, A.is_lt, ind=WR)
-            uv, bs = B(128), icol
-            tt(sub(uv, 0, 64), sub(lh, 64, 128), sub(io, 128, 192), A.subtract)
-            tt(sub(uv, 64, 128), sub(lh, 0, 64), sub(io, 128, 192), A.subtract)
+                if c:
+                    lin(part(Mk, c, 80), part(Mk, 0, 80))
+                act(sub(sg, 80 * c, 64 * c + 64), sub(lh, 16 * c, 64), AF.Sign, bias=col(ia, c), scale=-1.0)
+                act(sub(sg, 64 * c + 64, 80 * c + 80), sub(lh, 64, 16 * c + 80), AF.Sign, bias=col(ib, c))
+            uv, lj = B(256), B(256)
+            iota(odd(lj), [[0, 2], [-1, 64]], -128)
+            for h in range(2):
+                lin(even(part(lj, h, 128)), part(lh, 1 - h, 64))
+            scan(uv, sub(Z1, 0, 256), lj)
+            lin(sub(UZ, 1, 960, 3), lin(sub(UZ, 0, 960, 3), uv, 0.5, ind=WR))
             RS = fill(B(320), 1)
             fill(sub(RS, 0, 320, 80), 0)
             EV = iota(B(64), [[0, 32], [-1, 2]], 1)
-            W4L = wrap4(even(OL))
-            WLID = wrap(even(OL), add=0.0)
+            OL0, LID = OL, even(OL)
             WLH = wrap(lh, add=-128.0)
         else:
             CUM = B(80)
@@ -562,32 +649,38 @@ def rank_program(g, core, T, topo):
                 lin(sub(part(n0, h, 192), 2, 192, 3), t01, -2.0, 1.0, ind=W1)
                 lin(sub(part(n1, h, 192), 0, 192, 3), sub(CUM, 0, 65), ind=part(WLH, 1 - h, 4))
                 lin(sub(part(n1, h, 192), 1, 192, 3), sub(CUM, 0, 64), -1.0)
-            uv = lin(B(128), sub(scan(n2, n0, n1), 2, 384, 3))
-            hh = lin(B(4), posw, 0.5, 129.75)
-            alw = tt(F(4), lin(F(4), hh, 2.0, -259.0), posw, A.subtract)
-            bs = tt(F(4), lin(F(4), hh, -63.0, 8190.0), lin(F(4), posw, 32.0), A.add)
-            for c in range(4):
-                lin(part(Mk, c, 80), part(Mk, c, 80), col(alw, c))
-        lin(even(UZ), uv, ind=WR)
-        C = odd(scan(B(640), MZ, UZ))
-        lin(sub(C, 64, 320, 64), bs)
-        Wsl = wrap(lin(B(64), PS, ind=WLID))
-        LT = sub(LT, 0, 256)
-        lin(sub(LT, 2, 256, 4), PT, ind=Wsl)
-        lin(sub(LT, 3, 256, 4), sub(BI, 16, 272), 1.0, -1.0, ind=Wsl)
+            uv = sub(scan(n2, n0, n1), 2, 384, 3)
+            s = wrapscan(even(OL))
+            row, ia, ib = lin(F(2), s, inv16, -1.0), lin(F(2), s, inv16, 127.5), lin(F(2), s, invm, -127.5)
+            LID = lin(B(32), OL0, ind=lin(U(2), s, inv2, -2.0))
+            for c in range(2):
+                ts(part(Mk, 2 * c, 64), sub(io, 0, 64), col(row, c), A.is_gt)
+                ts(part(Mk, 2 * c + 1, 64), sub(io, 0, 64), col(row, c), A.is_le)
+                act(part(sg, 2 * c, 64), sub(lh, 0, 64), AF.Sign, bias=col(ia, c), scale=-1.0)
+                act(part(sg, 2 * c + 1, 64), sub(lh, 64, 128), AF.Sign, bias=col(ib, c))
+                for k in range(2):
+                    lin(sub(UZ, 384 * c + k, 384 * c + 384, 3), uv, 0.5)
+            RS = fill(B(256), 1)
+            fill(sub(RS, 0, 256, 128), 0)
+        n, per = (320, 80) if t == 0 else (256, 128)
+        C = sub(scan(B(3 * n), sub(MZ, 0, 3 * n), sub(UZ, 0, 3 * n)), 2, 3 * n, 3)
+        lin(sub(C, 64, n, 64 << t), sub(icol, 0, 4 >> t))
+        W4L, Wsl = wrap4(LID), wrap(lin(B(K), PS, ind=wrap(LID, add=0.0)))
+        LT = sub(LT, 0, 4 * K)
+        lin(sub(LT, 2, 4 * K, 4), PT, ind=Wsl)
+        lin(sub(LT, 3, 4 * K, 4), sub(BI, 16, 272), 1.0, -1.0, ind=Wsl)
         scores("xs", "x")
-        W4 = wrap4(sub(LT, 2, 256, 4))
-        for h in range(2):
+        W4 = wrap4(sub(LT, 2, 4 * K, 4))
+        for h in range(K // 32):
             g1 = lin(W("g1", 128 * h, 128 * h + 128), xs, ind=part(W4L, h, 8))
             tt(W("sm", 128 * h, 128 * h + 128), sub(xs, 512, 1024), g1, A.add, ind=part(W4, h, 8))
         ts(sub(t01, 0, 127), sub(PP, 0, 127), 0.0, A.is_gt)
-        pr = tt(B(320), t01, C, A.mult, ind=WG)
-        posw = sub(scan(B(320), RS, pr), 79, 320, 80)
-        Wn = lin(U(4), posw)
+        pr = tt(B(n), t01, C, A.mult, ind=sub(WG, 0, n // 16))
+        Wn = lin(U(4 >> t), sub(scan(B(n), RS, pr), per - 1, n, per))
         tt(sub(TB, 0, 127), sub(t01, 0, 127), sub(TO, 0, 127), A.not_equal)
         TO = sub(TB, 0, 128)
         lin(sub(TB, 128, 256), TO, -1.0, 1.0)
-        lin(sub(LT, 0, 256, 4), TB, ind=Wsl)
+        lin(sub(LT, 0, 4 * K, 4), TB, ind=Wsl)
 
     quant("v", 0, 128, W("vin", 0, 512))
     quant("x", 0, 128, W("xs", 0, 512))
@@ -611,8 +704,18 @@ def rank_program(g, core, T, topo):
         tt(part(off, h, 8), part(slot, h, 8), stay, A.mult)
     ko = lin(F(256), BI, 1.0, -2.0, ind=lin(U(16), off))
     dma("YS", "dkid", T.kid[:], T.lf[0:128:16, ko[1]:ko[2]], [], [ko], 1600.0)
+    return ops
 
-    got = plan(ops)
+
+def rank_program(g, core, T, topo):
+    rank = T.rank_of(core)
+    if rank is None:
+        return
+    Q = {"V": g.vector, "S": g.scalar, "P": g.tensor, "G": g, "Y": g.sync}
+    ops = record(g, Q, core, rank, T, topo, FIGS[0])
+    if not PLAN:
+        PLAN.append(plan([ops] + [record(g, Q, core, rank, T, topo, f) for f in FIGS[1:]]))
+    got = PLAN[0]
     total, known, clocks = {}, {e: {} for e in Q}, {}
 
     def wait(e, sem, v):

import math
from concourse.bass import DstId, RemoteDMATransfer
from concourse.mybir import dt, AluOpType, ActivationFunctionType

C4 = "float8_e4m3fn_x4"
TILES = {"lb": 32768, "xin": 1024, "uin": 512, "vin": 512, "xs": 1280, "g1": 256, "ft": 512,
         "hb": 528, "tsb": 256, "ab": 512, "ub": 512, "one": 528, "eb": 528, "zo": 512, "xy": 512, "xz": 1024, "sz": 1024}
PACKS = {"e": 512, "u": 128, "p": 128, "v": 128, "w": 512, "x": 256, "y": 256, "o": 256, "f": 384, "l": 320}
SCRATCH = {
    "lf": ("sbuf", [128, 12288], "float32"), "li": ("sbuf", [128, 128], "int32"), "lu": ("sbuf", [128, 1280], "uint16"),
    "kin": ("sbuf", [128, 16], "int32"), "yb": ("sbuf", [128, 256], "float32"), "ps": ("psum", [128, 4096], "float32"),
    "sm": ("sbuf", [128, 512], "float32"), "lp": ("sbuf", [128, 8], "uint16"), "ll": ("sbuf", [128, 16], "uint16"),
}
SCRATCH.update({k: ("sbuf", [128, n], "bfloat16") for k, n in TILES.items()})
SCRATCH.update({"q" + k: ("sbuf", [128, n], C4) for k, n in PACKS.items()})
SCRATCH.update({"s" + k: ("sbuf", [128, n], "uint8") for k, n in PACKS.items()})
SEMAPHORES = ["sV", "sS", "sP", "sG", "sent", "arr0", "arr1", "arr2", "arrx", "arrp", "dka", "dkb", "dxh", "dxl", "du", "dv", "dwc", "dws",
              "dkid", "doc", "dos0", "dos1", "dos2", "dos3", "dy0", "dy1"]
A = AluOpType
AF = ActivationFunctionType
LAND = [64, 192, 48]
FIGS = [(0.5, 215.0, 0.87, 1.56, 3.8, 1800.0, 1400.0, 6500.0, 1000.0, 36500.0, 200.0),
        (0.25, 270.0, 1.1, 1.8, 4.8, 2600.0, 2100.0, 9500.0, 1300.0, 0.0, 600.0),
        (0.25, 170.0, 0.9, 1.25, 2.4, 2300.0, 1800.0, 8000.0, 900.0, 0.0, 400.0)]
TWO = tuple(TILES) + ("lu",)
PLAN = []
TRIES, MOVES, SEED = 2500, (20000, 25000), 777


def place(ops, prio, links, mirror, pen, back):
    busy = {e: [] for e in "VSPGY"}
    got = [None] * len(ops)
    last = 0.0
    lack = [len(x) for x in links]
    todo = sorted((prio[j], j) for j in range(len(ops)) if not lack[j])
    while todo:
        i = todo.pop()[1]
        for j, w in mirror[i]:
            lack[j] -= 1
            if not lack[j]:
                x, k = (prio[j], j), len(todo)
                while k and todo[k - 1] > x:
                    k -= 1
                todo.insert(k, x)
        o = ops[i]
        ready = o["late"] if back else 0.0
        for d, w in links[i]:
            if got[d][2] + w > ready:
                ready = got[d][2] + w
        best = None
        for k, (e, c, f) in enumerate(o["alts"]):
            s, b = ready, busy[e]
            j = n = len(b)
            if n and b[-1][1] > s:
                lo = 0
                while lo < j:
                    h = (lo + j) >> 1
                    if b[h][1] > s:
                        j = h
                    else:
                        lo = h + 1
                while j < n and s + c > b[j][0]:
                    s = b[j][1]
                    j += 1
            key = s + c + (pen[i] if e == "V" else 0.0)
            if best is None or key < best[0]:
                best = (key, e, k, s, c, j)
        key, e, k, s, c, j = best
        busy[e].insert(j, (s, s + c))
        got[i] = (k, s, s + c)
        last = max(last, s + c + (0.0 if back else o["late"]))
    return last, got


def plan(sets):
    ops, LAT = sets[0], FIGS[0][1]
    n = len(ops)
    pres = [[[(d, x[d]["tail"] + f[1] if hard else 0.5) for d, hard in o["deps"].items()] for o in x] for x, f in zip(sets, FIGS)]
    pre = pres[0]
    post = [[] for o in ops]
    level = [0.0] * n
    for i in range(n - 1, -1, -1):
        level[i] = max(level[i] + ops[i]["tail"], ops[i]["late"]) + min(x[1] for x in ops[i]["alts"]) + LAT
        for d, w in pre[i]:
            post[d].append((i, w))
            level[d] = max(level[d], level[i])
    seed = [SEED]
    sends = [i for i, o in enumerate(ops) if o["sem"] in ("arr0", "arr1", "arr2")]

    def rnd():
        seed[0] = (seed[0] * 1103515245 + 12345) % 2147483648
        return (seed[0] >> 8) / 8388608.0

    def both(prio, pen):
        end, got = place(ops, prio, pre, post, pen, False)
        e2, g2 = place(ops, [got[i][2] + ops[i]["tail"] for i in range(n)], post, pre, pen, True)
        p2 = [b[2] for b in g2]
        e2, g2 = place(ops, p2, pre, post, pen, False)
        end, e2 = end + 0.1 * sum(got[i][1] for i in sends), e2 + 0.1 * sum(g2[i][1] for i in sends)
        return (end, got, prio, pen) if end <= e2 else (e2, g2, p2, pen)

    cur = both(level, [150.0] * n)
    for k in range(6):
        cur = min(cur, both(cur[2] if k else [-b[1] for b in cur[1]], cur[3]), key=lambda x: x[0])
    best = cur
    for k in range(TRIES):
        mid, wide, amp = rnd() ** 1.5 * cur[0] * 0.84, 300 + 4000 * rnd() ** 2, 1200 * rnd() ** 2
        prio, pen = [-b[1] for b in cur[1]], list(cur[3])
        for i in range(n):
            if abs(cur[1][i][1] - mid) < wide:
                prio[i] += amp * rnd()
                if rnd() < 0.15:
                    pen[i] = 1200 * rnd() ** 2 - 200
        new = both(prio, pen)
        if new[0] < cur[0] + 120 * (1 - k / TRIES):
            cur = new
            if new[0] < best[0]:
                best = new
    data = [(p, [[(e, c) for e, c, h in o["alts"]] for o in x], [o["late"] for o in x], f[0]) for p, x, f in zip(pres, sets, FIGS)]
    got = polish([data[0][:3] + (1.0,)], best[1], post, sends, rnd, MOVES[0], 25.0)
    return polish(data, got, post, sends, rnd, MOVES[1], 25.0)


def polish(data, got, post, sends, rnd, moves, heat):
    pre, alts, n = data[0][0], data[0][1], len(got)
    order, pick = sorted(range(n), key=lambda i: (got[i][1], i)), [x[0] for x in got]

    def run(order, pick):
        each = [one(order, pick, p, a, l) for p, a, l, w in data]
        return sum(x[0] * d[3] for x, d in zip(each, data)), each

    def one(order, pick, pre, alts, late):
        free, prev = {e: 0.0 for e in "VSPGY"}, {e: -1 for e in "VSPGY"}
        end, by, last, top = [0.0] * n, [-1] * n, 0.0, 0
        for i in order:
            e, c = alts[i][pick[i]]
            s, b = free[e], -2 - prev[e]
            for d, w in pre[i]:
                if end[d] + w > s:
                    s, b = end[d] + w, d
            by[i], prev[e] = b, i
            end[i] = free[e] = s = s + c
            if s + late[i] > last:
                last, top = s + late[i], i
        return last + 0.2 * sum(end[i] for i in sends), end, by, top

    def move(a, b, u, ahead):
        mid, tied = order[a:b + 1], {u}
        for j in (mid[::-1] if ahead else mid):
            if j in tied:
                tied.update(d for d, w in (pre if ahead else post)[j])
        return order[:a] + [j for j in mid if (j in tied) == ahead] + [j for j in mid if (j in tied) != ahead] + order[b + 1:]

    cur = run(order, pick)
    best = (cur[0], order, pick)
    for k in range(moves):
        c = cur[1][int(rnd() * len(data))]
        arcs, i = [], c[3] if rnd() < 0.6 else sends[int(rnd() * len(sends))]
        while i >= 0:
            b = c[2][i]
            if b <= -2:
                b = -2 - b
                arcs.append((b, i))
            i = b
        o2, p2 = order, pick
        if arcs and rnd() < 0.75:
            u, v = arcs[int(rnd() * len(arcs))]
            a, b = order.index(u), order.index(v)
        else:
            a = int(rnd() * n)
            b = min(n - 1, a + int(rnd() ** 2 * 60) + 1)
            u, v = order[a], order[b]
        y = rnd()
        j = u if len(alts[u]) > 1 and (len(alts[v]) == 1 or rnd() < 0.7) else v
        if y < 0.25 and len(alts[j]) > 1:
            p2 = list(pick)
            p2[j] = (p2[j] + 1 + int(rnd() * (len(alts[j]) - 1))) % len(alts[j])
        elif y < 0.6:
            o2 = move(a, b, v, True)
        else:
            o2 = move(a, min(n - 1, b + int(rnd() ** 2 * 25)), u, False)
        new = run(o2, p2)
        if new[0] <= cur[0] - heat * (1.02 - k / moves) * math.log(rnd() + 1e-9):
            cur, order, pick = new, o2, p2
            if k % 7 == 0:
                order = sorted(order, key=lambda i: new[1][0][1][i] - alts[i][pick[i]][1])
            if new[0] < best[0]:
                best = (new[0], order, pick)
    end = run(best[1], best[2])[1][0][1]
    return [(best[2][i], end[i] - alts[i][best[2][i]][1], end[i]) for i in range(n)]


def record(g, Q, core, rank, T, topo, fig):
    CY, GA, SC, FAR, FARL, FARX, DS, EARLY, CALL = fig[2:]
    ops = []
    log = {}
    top = {"lf": 0, "lb": 0, "li": 0, "lu": 0}

    def new(pool, n):
        a = top[pool]
        top[pool] = a + (n + 15) // 16 * 16
        return (pool, a, a + n, 1)

    def F(n): return new("lf", n)
    def B(n): return new("lb", n)
    def I(n): return new("li", n)
    def U(n): return new("lu", n)
    def W(name, a, b, s=1): return (name, a, b, s)
    def sub(v, a, b, s=1): return (v[0], v[1] + a * v[3], min(v[2], v[1] + b * v[3]), s * v[3])
    def part(v, h, n): return sub(v, n * h, n * h + n)
    def n_of(v): return (v[2] - v[1] + v[3] - 1) // v[3]
    def even(v): return sub(v, 0, n_of(v), 2)
    def odd(v): return sub(v, 1, n_of(v), 2)
    def ap(v): return T[v[0]][:, v[1]:v[2]:v[3]] if v[3] != 1 else T[v[0]][:, v[1]:v[2]]
    def num(s): return ap(s) if isinstance(s, tuple) else s
    def views(*xs): return [x for x in xs if isinstance(x, tuple)]
    def col(v, j): return sub(v, j, j + 1)
    def src(v, ind): return ap(v).indirect(ap(ind)) if ind else ap(v)

    def do(alts, wr, rd, sem=None, inc=1, tail=0.0, chain=False, after=(), late=0.0):
        deps = {d: True for d in after}
        spans = []
        for v, w in [(v, True) for v in wr] + [(v, False) for v in rd]:
            lo, hi, step = v[1], v[1] + (n_of(v) - 1) * v[3] + 1, v[3]
            ps = v[0] == "ps"
            if ps:
                lo, hi, step = lo // 512 * 512, (hi + 511) // 512 * 512, 1
            spans.append((v[0], lo, hi, step, w))
            for (l2, h2, s2, w2, d) in log.get(v[0], []):
                apart = ps and not (len(alts) == 1 == len(ops[d]["alts"]) and alts[0][0] == ops[d]["alts"][0][0])
                if l2 < hi and lo < h2 and (w or w2 or apart) and (lo - l2) % math.gcd(step, s2) == 0:
                    deps[d] = deps.get(d, False) or not (chain and ps)
        me = len(ops)
        ops.append({"alts": alts, "deps": deps, "sem": sem, "inc": inc, "tail": tail, "late": max(tail, late)})
        for (name, lo, hi, step, w) in spans:
            old = log.get(name, [])
            if w:
                old = [x for x in old if not (lo <= x[0] and x[1] <= hi and x[2] % step == 0 and (x[0] - lo) % step == 0)]
            log[name] = old + [(lo, hi, step, w, me)]
        return me

    def vt(o, i, ind, k=1.0):
        if ind:
            return 50 + 16 * n_of(ind) * GA * CY
        if k == 1.0 and o[0] in TWO and i[0] in TWO:
            k = 0.5
        return max(64, n_of(o) * k) * CY

    def st(o, ind): return 65 + 16 * n_of(ind) * GA * CY if ind else 60 + max(64, n_of(o)) * CY

    def ts_call(o, i, s1, op0, s2, op1, ind):
        if op1 is None:
            return lambda: g.vector.tensor_scalar(ap(o), src(i, ind), num(s1), None, op0)
        return lambda: g.vector.tensor_scalar(ap(o), src(i, ind), num(s1), num(s2), op0, op1)

    def ts(o, i, s1, op0, s2=None, op1=None, ind=None):
        do([("V", vt(o, i, ind), ts_call(o, i, s1, op0, s2, op1, ind))], [o], views(i, s1, s2, ind))
        return o

    def lin(o, i, m=1.0, a=0.0, ind=None, only=None):
        if m == 1.0 and a == 0.0:
            v = lambda: g.vector.tensor_copy(ap(o), src(i, ind))
            s = lambda: g.scalar.activation(ap(o), src(i, ind), AF.Copy)
        else:
            v = ts_call(o, i, m, A.mult, a, A.add, ind)
            s = lambda: g.scalar.activation(ap(o), src(i, ind), AF.Identity, bias=num(a), scale=num(m))
        alts = [("V", vt(o, i, ind), v)]
        if o[0] not in ("li", "lu") and i[0] not in ("li", "lu", "kin"):
            alts.append(("S", st(o, ind), s))
            if m == 1.0 and a == 0.0 and not ind and i[0] == "lb":
                alts.append(("G", 170 + 2 * CY * n_of(o), lambda: g.affine_select(ap(o), ap(i), [[0, n_of(o)]], A.is_equal, 0.0, 0, 0)))
        do([x for x in alts if only in (None, x[0])], [o], views(i, m, a, ind))
        return o

    def tt(o, a, b, op, ind=None):
        do([("V", vt(o, a, ind, 2.0), lambda: g.vector.tensor_tensor(ap(o), src(a, ind), ap(b), op))], [o], views(a, b, ind))
        return o

    def put(win, off, i):
        do([("V", 50 + n_of(i) * SC * CY, lambda: g.vector.tensor_copy(ap(win).indirect(ap(off)), ap(i)))], [win], [off, i])

    def iota(o, pat, base, cm=0):
        if o[0] == "li":
            f = lambda: g.iota(ap(o), pat, base, cm)
        else:
            f = lambda: g.iota(ap(o), pat, base, cm, allow_small_or_imprecise_dtypes=True)
        do([("G", 130 + 2 * CY * n_of(o), f)], [o], [])
        return o

    def fill(o, c, only=None):
        alts = [("V", vt(o, o, None), lambda: g.vector.memset(ap(o), float(c))),
                ("G", 130 + 2 * CY * n_of(o), lambda: g.iota(ap(o), [[0, n_of(o)]], c, 0, allow_small_or_imprecise_dtypes=True))]
        do([x for x in alts if only in (None, x[0])], [o], [])
        return o

    def scan(o, d0, d1, op0=A.mult, op1=A.add):
        do([("V", vt(o, d1 if d0[0] in TWO else d0, None), lambda: g.vector.tensor_tensor_scan(ap(o), ap(d0), ap(d1), 0.0, op0, op1))],
           [o], [d0, d1])
        return o

    def act(o, i, func, ind=None, bias=0.0, scale=1.0):
        if func == AF.Copy:
            f = lambda: g.scalar.activation(ap(o), src(i, ind), func)
        else:
            f = lambda: g.scalar.activation(ap(o), src(i, ind), func, bias=num(bias), scale=num(scale))
        do([("S", st(o, ind), f)], [o], views(i, ind, bias, scale))
        return o

    def relu(o, i):
        do([("V", vt(o, i, None), ts_call(o, i, 0.0, A.max, 0.03125, A.mult, None)),
            ("S", st(o, None), lambda: g.scalar.activation(ap(o), ap(i), AF.Relu, scale=0.03125))], [o], [i])

    def quant(n, a, b, i):
        c, s = W("q" + n, a, b), W("s" + n, a, b)
        do([("V", 12 + 0.22 * n_of(i), lambda: g.vector.quantize_mx(ap(c), ap(s), ap(i)))], [c, s], [i])

    def mm(o, l, la, r, ra, start=True, stop=True):
        n = n_of(o)
        lc, ls, rc, rs = W("q" + l, la, la + 128), W("s" + l, la, la + 128), W("q" + r, ra, ra + n), W("s" + r, ra, ra + n)
        do([("P", (n + 16) * 0.7, lambda: g.tensor.matmul_mx(ap(o), ap(lc), ap(ls), ap(rc), ap(rs), start, stop))],
           [o], [lc, ls, rc, rs], chain=not start)

    def dma(e, sem, out, in_, wr, rd, tail, after=()):
        return do([(x, 200.0, lambda x=x: Q[x].dma_start(out, in_)) for x in e], wr, rd, sem=sem, inc=16, tail=tail - 1600.0 + DS, after=after)

    def send(sem, d, pairs, tail, fused=False, late=0.0):
        def side(v): return ap(v).bitcast(dt.uint8) if v[0][0] == "q" else ap(v)

        def call():
            rid, pid = topo.addr(d, core)
            es = topo.engines(core, d)
            if fused:
                g.remote_dma_fused([RemoteDMATransfer(dst_ids=[DstId(rid=rid, pnc=pid)], remote_sem=T.sem[sem], src=side(i), dst=side(o),
                                                      dma_engine_mask=sum(1 << e for e in es[k::len(pairs)]))
                                    for k, (o, i) in enumerate(pairs)], local_sem=T.sem.sent)
                return len(es)
            for o, i in pairs:
                g.remote_dma(side(o), side(i), T.sem[sem], T.sem.sent, pid, rid, topo.mask(core, d))
            return len(pairs) * len(es)

        do([("G", CALL * (1 if fused else len(pairs)), call)], [o for o, i in pairs], [i for o, i in pairs], sem=sem,
           inc=(1 if fused else len(pairs)) * len(topo.engines(d, core)), tail=tail, late=late)

    kin = W("kin", 0, 16)
    dma("Y", "dka", T.kin[:, 0:8], T.ka[:], [sub(kin, 0, 8)], [], 1600.0)
    dma("S", "dkb", T.kin[:, 8:16], T.kb[:], [sub(kin, 8, 16)], [], 1600.0)
    dma("S", "du", T.uin[:], T.u[:], [W("uin", 0, 512)], [], 2300.0)
    dma("Y", "dxh", T.xin[:, 512:1024], T.x[:, 512:1024], [W("xin", 512, 1024)], [], 2500.0)
    dx = dma("Y", "dxl", T.xin[:, 0:512], T.x[:, 0:512], [W("xin", 0, 512)], [], 2800.0)
    dma("Y", "dwc", T.qw[:].bitcast(dt.uint8), T.wc[:], [W("qw", 0, 512)], [], 3000.0, (dx,))
    dma("Y", "dws", T.sw[:], T.ws[:], [W("sw", 0, 512)], [], 3000.0, (dx,))
    dma("Y", "dv", T.vin[:], T.v[:], [W("vin", 0, 512)], [], 3000.0, (dx,))

    pi = iota(I(1), [[0, 1]], 0, 1)
    one = fill(W("one", 0, 528), 1)
    SG = B(528)
    io = iota(sub(SG, 256, 528), [[1, 272]], 0)
    io1 = sub(io, 1, 257)
    lin(sub(SG, 0, 256), io1, 1.0, -257.0)
    leafy = B(256)
    fill(sub(leafy, 0, 256, 129), 0)
    fill(sub(leafy, 1, 129), 1)
    fill(sub(leafy, 130, 256), 0)
    PT = iota(B(256), [[0, 2], [1, 128]], 1)
    UT = lin(B(256), PT, 1.0, 128.0)
    Z128 = iota(B(256), [[0, 128], [128, 2]], 0)
    Z1 = W("zo", 0, 512)
    fill(even(Z1), 0)
    fill(odd(Z1), 1)
    eb = W("eb", 0, 528)
    do([("G", 170 + 2 * CY * 528, lambda: g.affine_select(ap(eb), ap(one), [[-1, 528]], A.is_equal, 0.0, 3, 4))], [eb], [one])
    crf = F(20)
    iota(crf, [[16, 4], [16, 5]], 0)
    fill(W("ft", 256, 512), 0)
    for b in range(4):
        quant("e", 128 * b, 128 * b + 128, W("eb", 3 - b, 515 - b))
    ri = I(3)
    ts(col(ri, 0), pi, 15, A.bitwise_and)
    ts(col(ri, 1), pi, 2, A.arith_shift_right, 3, A.bitwise_and)
    ts(col(ri, 2), pi, 3, A.bitwise_and)
    rf = lin(F(3), ri)
    r, r4, r3 = col(rf, 0), col(rf, 1), col(rf, 2)
    inv16 = ts(F(1), r, 15.0, A.is_equal, 1.0 / 1024, A.max)
    inv4 = ts(F(1), r4, 3.0, A.is_equal, 1.0 / 1024, A.max)
    inv44 = lin(F(1), inv4, 4.0)
    inv2, invm, inv128 = lin(F(1), inv16, 2.0), lin(F(1), inv16, -1.0), lin(F(1), inv16, 128.0)
    r3m = lin(F(1), r3, 1.0, -4.0)
    r1, r41 = lin(F(1), r, 1.0, 1.0), lin(F(1), r4, 1.0, 1.0)
    d0, d1 = F(32), F(32)
    ts(sub(d0, 0, 16), sub(io, 0, 16), r, A.not_equal)
    ts(sub(d1, 0, 16), sub(io, 0, 16), r1, A.is_equal, 1024.0, A.mult)
    ts(sub(d0, 16, 32), sub(io, 0, 16), r4, A.not_equal)
    ts(sub(d1, 16, 32), sub(io, 0, 16), r41, A.is_equal, 1024.0, A.mult)
    pt = tt(F(32), d0, d1, A.max)
    c16 = lin(U(8), sub(io, 0, 8), 0.0, r)
    c4 = lin(U(8), sub(io, 0, 8), 0.0, r3)
    P16 = B(256)
    lin(sub(P16, 0, 128), sub(pt, 0, 16), ind=c16)
    lin(sub(P16, 128, 256), sub(P16, 0, 128))
    P4 = lin(B(128), sub(pt, 16, 32), ind=c4)
    own = F(16)
    for h in range(2):
        lin(part(own, h, 8), sub(io, 0, 8), 16.0, r)
    self1 = lin(F(8), sub(own, 0, 8), 1.0, 256.0)
    cU = lin(U(8), sub(io, 0, 8), 16.0)

    def wrapscan(v, per=16, o=None):
        n = n_of(v)
        o = o or (B(n) if v[0] == "lb" else F(n))
        scan(o, sub(P16 if per == 16 else P4, 0, n), v, A.mult, A.max)
        return sub(o, per - 1, n, per)

    def wrap(v, o=None, add=-1.0):
        s = wrapscan(v)
        return lin(o or U(n_of(s)), s, inv16, add)

    def wrap4(v):
        return lin(U(n_of(v) // 4), wrapscan(v, 4), inv44, r3m)

    inv48, r37 = lin(F(1), inv4, 8.0), lin(F(1), r3, 2.0, -7.0)

    ksc = lin(U(16), kin, 1.0, 1.0)
    PS = B(272)
    fill(sub(PS, 256, 272), 128)
    put(sub(PS, 0, 256), ksc, io1)
    s = wrapscan(sub(PS, 1, 257))
    WPS, WP2 = lin(U(16), s, inv16, -1.0), lin(U(16), s, inv2, -1.0)
    send("arrp", T.cores[rank ^ 1], [(W("lp", 0, 8), sub(WPS, 0, 8))], FAR)
    pen = ts(F(16), kin, 127.0, A.is_le, 512.0, A.mult)
    bump = ts(F(16), kin, 127.0, A.is_gt, 512.0, A.mult)
    X2 = tt(F(16), kin, pen, A.add)
    M, V, L2, L3 = F(16), F(16), F(16), F(8)
    for h in range(2):
        tt(part(M, h, 8), part(X2, 1 - h, 8), sub(self1, 0, 8), A.min)
    tt(V, X2, tt(F(16), M, bump, A.add), A.min)
    tt(sub(L2, 0, 8), sub(V, 8, 16), sub(V, 0, 8), A.subtract)
    tt(sub(L2, 8, 16), sub(M, 8, 16), sub(M, 0, 8), A.subtract)
    tt(L3, sub(pen, 8, 16), sub(pen, 0, 8), A.subtract)
    WM, WV, WL2 = lin(U(16), M, 1.0, 129.0), lin(U(8), sub(V, 0, 8), 1.0, 129.0), lin(U(16), L2, 1.0, 256.0)
    WL3 = lin(U(8), L3, 1.0 / 512, 256.0)
    DR, DW, MS = B(512), B(512), B(256)
    UP, DU = fill(B(256), 0), B(256)
    for h in range(2):
        lin(part(MS, h, 128), SG, ind=part(WM, h, 8))
        lin(even(part(DR, h, 256)), SG, ind=part(WL2, h, 8))
        lin(odd(part(DW, h, 256)), leafy, ind=part(ksc, h, 8))
    lin(odd(part(DR, 0, 256)), SG, ind=WV)
    lin(odd(part(DR, 1, 256)), part(MS, 0, 128))
    lin(even(part(DW, 0, 256)), SG, ind=WL3)
    lin(even(part(DW, 1, 256)), even(part(DW, 0, 256)), -1.0)
    lin(odd(DU), MS, ind=sub(WPS, 8, 16))
    lin(odd(UP), UT, ind=sub(WPS, 8, 16))
    quant("u", 0, 128, W("uin", 0, 512))
    do([("V", 250.0, lambda: g.vector.tensor_copy(T.qp[:, 0:128].bitcast(dt.uint32),
                                                  T.qu[:, 0:128].bitcast(dt.uint32).indirect(ap(cU))))],
       [W("qp", 0, 128)], [W("qu", 0, 128), cU])
    act(W("sp", 0, 128), W("su", 0, 128), AF.Copy, ind=cU)
    PP = W("ps", 2048, 2176)
    xs = W("xs", 0, 1024)

    def scores(x, q):
        quant(q, 128, 256, W(x, 512, 1024))
        mm(PP, "p", 0, q, 128)
        quant(q, 0, 128, W(x, 0, 512))
        for b in range(4):
            mm(W("ps", 512 * b, 512 * b + 256), "e", 128 * b, q, 0)
        for b in range(4):
            lin(W("xs", b, 1024, 4), W("ps", 512 * b, 512 * b + 256))

    scores("xin", "o")
    send("arrx", T.cores[rank ^ 1], [(W("qy", 0, 256), W("qo", 0, 256)), (W("sy", 0, 256), W("so", 0, 256))], FARX, late=EARLY)
    for b in range(4):
        mm(W("ps", 512 * b, 512 * b + 256), "e", 128 * b, "y", 0)
        lin(W("xz", 2 * b + 1, 1024, 8), W("ps", 512 * b, 512 * b + 128), 0.5)
        lin(W("xy", b, 512, 4), W("ps", 512 * b + 128, 512 * b + 256), 0.5)
    T2 = fill(B(512), 0)
    ts(sub(T2, 1, 254, 2), sub(PP, 0, 127), 0.0, A.is_gt)
    ts(sub(T2, 257, 510, 2), sub(PP, 0, 127), 0.0, A.is_le)
    TD = sub(T2, 0, 256)
    lin(even(DU), T2, 256.0, ind=sub(WP2, 8, 16))
    R, val, EE = B(512), B(512), B(512)
    scan(sub(R, 0, 256), TD, sub(DR, 0, 256))
    scan(sub(R, 256, 512), UP, DU, A.min, A.max)
    Wc, w0 = U(16), B(256)
    for h in range(2):
        lin(part(Wc, h, 8), wrapscan(odd(part(R, h, 256))), inv2, -1.0)
        scan(part(val, h, 256), TD, part(DW, h, 256))
        lin(part(w0, h, 128), odd(part(val, h, 256)))
    for i in range(8):
        mine, v2 = w0 if i == 0 else B(256), B(256)
        for h in range(2):
            if 0 < i < 7:
                lin(part(mine, h, 128), part(val, h, 128))
        if i == 7:
            far = B(256)
            for h in range(2):
                lin(part(far, h, 128), val, ind=part(Wc, h, 8))
            mine, val, near = val, far, val
        for h in range(2):
            tt(part(v2, h, 128), val, part(mine, h, 128), A.add, ind=part(Wc, h, 8))
        val = v2
        if i < 6:
            R2, W2 = B(256), U(16)
            for h in range(2):
                lin(part(R2, h, 128), R, ind=part(Wc, h, 8), only="S")
                wrap(part(R2, h, 128), o=part(W2, h, 8))
            R, Wc = R2, W2
    BI = B(272)
    lin(sub(BI, 16, 144), io, 1.0, 1.0, ind=sub(ksc, 8, 16))
    lin(sub(BI, 144, 272), io, 1.0, 1.0, ind=sub(ksc, 0, 8))
    LT = B(512)
    fill(sub(LT, 1, 512, 4), 0)
    lin(sub(LT, 0, 512, 4), T2, ind=sub(WP2, 0, 8))
    lin(sub(LT, 2, 512, 4), PT, ind=sub(WPS, 0, 8))
    lin(sub(LT, 3, 512, 4), sub(BI, 16, 272), 1.0, -1.0, ind=sub(WPS, 0, 8))
    scan(sub(EE, 0, 256), Z128, even(LT))
    scan(sub(EE, 256, 512), TD, sub(DR, 256, 512))
    WE = wrap(odd(EE))
    WY = wrap(lin(B(128), R, ind=sub(WE, 0, 8)))
    Wn = lin(U(8), wrapscan(tt(B(128), far, lin(B(128), near, ind=sub(WE, 0, 8)), A.add, ind=WY)), invm, 128.0)
    W4 = wrap4(lin(B(128), PT, ind=W("lp", 0, 8)))
    for h in range(4):
        lin(W("xz", 256 * h, 256 * h + 256, 2), W("xy", 0, 512), ind=part(W4, h, 8))
        scan(W("sz", 256 * h, 256 * h + 256), sub(Z1, 0, 256), W("xz", 256 * h, 256 * h + 256))
    REP = iota(B(272), [[1, 272]], 0)
    RK, MR = fill(F(128), 0), fill(F(816), 0)
    t01, TB = B(128), B(256)
    fill(col(t01, 127), 1)
    fill(sub(TB, 127, 256, 128), 0)
    fill(W("hb", 0, 272), 0)
    kc = iota(F(64), [[1, 64]], 257)
    h14 = lin(F(1), r3, 64.0, 14.0)
    HC = lin(U(16), sub(io, 0, 16), 4.0, lin(F(1), r3, 64.0, lin(F(1), r4, 1.0, 272.0)))
    hb = W("hb", 0, 528)
    TO = odd(TD)
    WB = [sub(ksc, 8, 16), sub(ksc, 0, 8)]

    for t in range(3):
        K = 64 >> t
        m = 2 * K
        OL = B(m)
        put(OL, Wn, sub(io1, 0, m))
        s = wrapscan(sub(OL, 1, 2 * K, 2), 4)
        Wl = lin(U(K // 4), s, inv44, r3m)
        d = T.cores[rank ^ (1 << t)]
        a = LAND[t]
        if t == 0:
            send("arr0", d, [(W("ll", 0, 16), lin(U(16), s, inv48, r37))], FARL)
        for h in range(2):
            if t:
                lin(W("ft", 2 * K * h, 2 * K * h + 2 * K), W("sm", 0, 4 * m), 0.5, ind=part(Wl, h, K // 8))
            else:
                lin(W("ft", 128 * h, 128 * h + 128), W("sz", 0, 1024), ind=W("ll", 8 * h, 8 * h + 8))
        if t == 0:
            quant("l", a, a + 128, W("ft", 0, 512))
        else:
            quant("f", 128 * t, 128 * t + 128, W("ft", 0, 512))
            z = 3 * K * (t - 1)
            send("arr%d" % t, d, [(W("ql", a, a + K), W("qf", 128 * t, 128 * t + K)),
                                  (W("sl", a - z, a - z + 4 * K), W("sf", 128 * t - z, 128 * t - z + 4 * K))], FAR, True)

        KT = lin(B(4 * K), LT, ind=Wl)
        pk, s1 = sub(KT, 2, 4 * K, 4), sub(KT, 3, 4 * K, 4)
        two = B(2 * K)
        wrapscan(pk, o=part(two, 0, K))
        wrapscan(s1, o=part(two, 1, K))
        Wps = lin(U(2 * max(K // 16, 2)), sub(two, 15, 2 * K, 16), inv16) if K > 16 else None
        Wp = part(Wps, 0, K // 16) if Wps else lin(U(1), col(two, 15), inv16)
        Ws = part(Wps, 1, K // 16) if Wps else lin(U(1), col(two, 31), inv16)
        rk, mr, SP = sub(RK, 0, 2 * K), part(MR, t, 272), F(4 * K)
        tt(odd(rk), sub(KT, 0, 4 * K, 4), sub(kc, 0, K), A.mult)
        put(mr, Ws, odd(rk))
        lin(odd(part(SP, 1, 2 * K)), sub(mr, 128, 272), 1.0, 1.0, ind=Wp)
        put(sub(REP, 128, 272), Wp, s1)
        tt(sub(KT, 1, 4 * K, 4), REP, s1, A.not_equal, ind=Ws)
        scan(part(SP, 0, 2 * K), rk, odd(KT), A.mult, A.max)
        HO = lin(U(K // 4), wrapscan(odd(part(SP, 1, 2 * K)), 4), inv4, h14)
        XO = wrap4(odd(part(SP, 0, 2 * K)))
        Ts = lin(W("tsb", 0, 4 * K), xs, ind=wrap4(s1))
        put(sub(REP, 128, 272), Wp, lin(B(K), REP, ind=Ws))
        BI = B(272)
        if t == 2:
            fill(sub(BI, 0, 16), 1)
        for h in range(2):
            lin(sub(BI, 16 + 128 * h, 144 + 128 * h), REP, 1.0, 1.0, ind=WB[h])
        z = 128 - K if t == 1 else 0
        for b in range(4):
            mm(W("ps", 2048 + 512 * b, 2176 + 512 * b), "w", 128 * b, "l", a - z)
            relu(sub(hb, 272 + 64 * b, 272 + 64 * b + K), W("ps", 2048 + 512 * b + z, 2048 + 512 * b + z + K))
        ab = W("ab", 0, 8 * K)
        tt(odd(ab), hb, Ts, A.add, ind=sub(HC, 0, K // 4))
        lin(even(ab), hb, ind=HO)
        put(W("xs", 0, 1280), XO, odd(scan(W("ub", 0, 8 * K), W("zo", 0, 8 * K), ab)))
        if t == 2:
            break
        wb = wrap(sub(BI, 16, 272))
        WB = [sub(wb, 0, 8), sub(wb, 8, 16)]
        for k in range(2):
            put(PS, Ws, lin(B(K), sub(PS, 128, 272), ind=Wp))
        if t == 0:
            mid = wrapscan(lin(B(128), val, 1.0, 1.0, ind=sub(WE, 8, 16)))
            INV = B(144)
            put(INV, lin(U(8), mid, invm, 129.0), sub(io1, 0, 128))
            f1 = scan(B(126), sub(Z1, 0, 126), sub(INV, 1, 127))
            GID = B(64)
            fill(col(GID, 0), 128)
            tt(sub(GID, 1, 64), odd(f1), sub(pk, 0, 63), A.subtract)
            s = B(64)
            wrapscan(GID, o=s)
            WG = lin(U(32), s, inv16, -1.0, ind=lin(U(2), sub(io, 0, 2), 0.0, lin(F(1), r3, 16.0, 15.0)))
            W1, WG = sub(WG, 0, 4), sub(WG, 0, 20)
            WR = lin(U(20), crf, 2.0, lin(F(1), r, 2.0, 1.0))
            lh = B(128)
            lin(sub(lh, 0, 64), sub(val, 0, 128), -0.5, 192.25, ind=W1)
            hv = tt(F(64), sub(val, 128, 256), lin(F(64), sub(w0, 128, 256), ind=W1), A.subtract, ind=W1)
            lin(sub(lh, 64, 128), hv, -0.5, 192.25)
            icol = lin(F(4), sub(io, 0, 4), 16.0, r)
            ia, ib = lin(F(4), icol, 1.0, 128.5), lin(F(4), icol, -1.0, -128.5)
            MZ, UZ = B(960), B(960)
            fill(sub(MZ, 0, 960, 3), 0)
            fill(sub(UZ, 2, 960, 3), 0)
            sg, Mk = sub(MZ, 1, 960, 3), sub(MZ, 2, 960, 3)
            ts(part(Mk, 0, 80), act(B(80), sub(io, 0, 80), AF.Abs, bias=lin(F(1), r, -1.0, -32.5)), 32.0, A.is_lt)
            for c in range(4):
                if c:
                    lin(part(Mk, c, 80), part(Mk, 0, 80))
                act(sub(sg, 80 * c, 64 * c + 64), sub(lh, 16 * c, 64), AF.Sign, bias=col(ia, c), scale=-1.0)
                act(sub(sg, 64 * c + 64, 80 * c + 80), sub(lh, 64, 16 * c + 80), AF.Sign, bias=col(ib, c))
            uv, lj = B(256), B(256)
            iota(odd(lj), [[0, 2], [-1, 64]], -128)
            for h in range(2):
                lin(even(part(lj, h, 128)), part(lh, 1 - h, 64))
            scan(uv, sub(Z1, 0, 256), lj)
            lin(sub(UZ, 1, 960, 3), lin(sub(UZ, 0, 960, 3), uv, 0.5, ind=WR))
            RS = fill(B(320), 1)
            fill(sub(RS, 0, 320, 80), 0)
            EV = iota(B(64), [[0, 32], [-1, 2]], 1)
            OL0, LID = OL, even(OL)
            WLH = wrap(lh, add=-128.0)
        else:
            CUM = B(80)
            al = lin(B(64), EV, ind=Wn)
            fill(col(CUM, 0), 0)
            scan(sub(CUM, 1, 65), sub(one, 0, 64), al)
            n0, n1, n2 = B(384), B(384), B(384)
            iota(n0, [[0, 128], [1, 3]], 0)
            fill(sub(n1, 2, 384, 3), 0)
            for h in range(2):
                lin(sub(part(n0, h, 192), 2, 192, 3), t01, -2.0, 1.0, ind=W1)
                lin(sub(part(n1, h, 192), 0, 192, 3), sub(CUM, 0, 65), ind=part(WLH, 1 - h, 4))
                lin(sub(part(n1, h, 192), 1, 192, 3), sub(CUM, 0, 64), -1.0)
            uv = sub(scan(n2, n0, n1), 2, 384, 3)
            s = wrapscan(even(OL))
            row, ia, ib = lin(F(2), s, inv16, -1.0), lin(F(2), s, inv16, 127.5), lin(F(2), s, invm, -127.5)
            LID = lin(B(32), OL0, ind=lin(U(2), s, inv2, -2.0))
            for c in range(2):
                ts(part(Mk, 2 * c, 64), sub(io, 0, 64), col(row, c), A.is_gt)
                ts(part(Mk, 2 * c + 1, 64), sub(io, 0, 64), col(row, c), A.is_le)
                act(part(sg, 2 * c, 64), sub(lh, 0, 64), AF.Sign, bias=col(ia, c), scale=-1.0)
                act(part(sg, 2 * c + 1, 64), sub(lh, 64, 128), AF.Sign, bias=col(ib, c))
                for k in range(2):
                    lin(sub(UZ, 384 * c + k, 384 * c + 384, 3), uv, 0.5)
            RS = fill(B(256), 1)
            fill(sub(RS, 0, 256, 128), 0)
        n, per = (320, 80) if t == 0 else (256, 128)
        C = sub(scan(B(3 * n), sub(MZ, 0, 3 * n), sub(UZ, 0, 3 * n)), 2, 3 * n, 3)
        lin(sub(C, 64, n, 64 << t), sub(icol, 0, 4 >> t))
        W4L, Wsl = wrap4(LID), wrap(lin(B(K), PS, ind=wrap(LID, add=0.0)))
        LT = sub(LT, 0, 4 * K)
        lin(sub(LT, 2, 4 * K, 4), PT, ind=Wsl)
        lin(sub(LT, 3, 4 * K, 4), sub(BI, 16, 272), 1.0, -1.0, ind=Wsl)
        scores("xs", "x")
        W4 = wrap4(sub(LT, 2, 4 * K, 4))
        for h in range(K // 32):
            g1 = lin(W("g1", 128 * h, 128 * h + 128), xs, ind=part(W4L, h, 8))
            tt(W("sm", 128 * h, 128 * h + 128), sub(xs, 512, 1024), g1, A.add, ind=part(W4, h, 8))
        ts(sub(t01, 0, 127), sub(PP, 0, 127), 0.0, A.is_gt)
        pr = tt(B(n), t01, C, A.mult, ind=sub(WG, 0, n // 16))
        Wn = lin(U(4 >> t), sub(scan(B(n), RS, pr), per - 1, n, per))
        tt(sub(TB, 0, 127), sub(t01, 0, 127), sub(TO, 0, 127), A.not_equal)
        TO = sub(TB, 0, 128)
        lin(sub(TB, 128, 256), TO, -1.0, 1.0)
        lin(sub(LT, 0, 4 * K, 4), TB, ind=Wsl)

    quant("v", 0, 128, W("vin", 0, 512))
    quant("x", 0, 128, W("xs", 0, 512))
    quant("x", 128, 256, W("xs", 512, 1024))
    dma("Y", "doc", T.oc[:], T.qx[:].bitcast(dt.uint8), [], [W("qx", 0, 256)], 2300.0)
    for k in range(4):
        dma("YS", "dos%d" % k, T.osc[4 * k:4 * k + 4, :], T.sx[32 * k:32 * k + 4, :], [], [W("sx", 0, 256)], 1600.0)
    for h in range(2):
        mm(W("ps", 512 * h, 512 * h + 128), "v", 0, "x", 128 * h)
    lin(W("yb", 0, 128), W("ps", 0, 128), only="V")
    lin(W("yb", 128, 256), W("ps", 512, 640), only="S")
    dma("Y", "dy0", T.y[:, 0:128], T.yb[:, 0:128], [], [W("yb", 0, 128)], 2000.0)
    dma("S", "dy1", T.y[:, 128:256], T.yb[:, 128:256], [], [W("yb", 128, 256)], 2000.0)
    TE = B(256)
    lin(sub(TE, 0, 128), TO, -1.0, 2.0)
    lin(sub(TE, 128, 256), TO, 1.0, 1.0)
    slot = tt(F(16), lin(F(16), wrapscan(TE), inv128, -112.0), own, A.add)
    stay = tt(F(8), wrap(sub(REP, 129, 257), o=F(8), add=127.0), self1, A.is_equal)
    off = F(16)
    for h in range(2):
        tt(part(off, h, 8), part(slot, h, 8), stay, A.mult)
    ko = lin(F(256), BI, 1.0, -2.0, ind=lin(U(16), off))
    dma("YS", "dkid", T.kid[:], T.lf[0:128:16, ko[1]:ko[2]], [], [ko], 1600.0)
    return ops


def rank_program(g, core, T, topo):
    rank = T.rank_of(core)
    if rank is None:
        return
    Q = {"V": g.vector, "S": g.scalar, "P": g.tensor, "G": g, "Y": g.sync}
    ops = record(g, Q, core, rank, T, topo, FIGS[0])
    if not PLAN:
        PLAN.append(plan([ops] + [record(g, Q, core, rank, T, topo, f) for f in FIGS[1:]]))
    got = PLAN[0]
    total, known, clocks = {}, {e: {} for e in Q}, {}

    def wait(e, sem, v):
        if known[e].get(sem, 0) >= v:
            return
        Q[e].wait_ge(T.sem[sem], v)
        for k, x in clocks.get((sem, v), {}).items():
            if known[e].get(k, 0) < x:
                known[e][k] = x
        known[e][sem] = v

    for i in sorted(range(len(ops)), key=lambda i: (got[i][1], i)):
        o = ops[i]
        e, c, f = o["alts"][got[i][0]]
        need = {}
        for d, hard in o["deps"].items():
            if hard:
                s, v = ops[d]["mark"]
                need[s] = max(need.get(s, 0), v)
        for s, v in sorted(need.items(), key=lambda x: -len(clocks.get(x, {}))):
            wait(e, s, v)
        sem = o["sem"] or "s" + e
        total[sem] = total.get(sem, 0) + o["inc"]
        o["mark"] = (sem, total[sem])
        if sem.startswith("arr"):
            total["sent"] = total.get("sent", 0) + f()
        else:
            f().then_inc(T.sem[sem], o["inc"])
            clocks[o["mark"]] = dict(known[e])
    for s, v in sorted(total.items()):
        wait("Y", s, v)
